import numpy as np
import ml_dtypes


def mxq(x, axis, fmt="e4m3"):
    dtype, down = {"e4m3": (ml_dtypes.float8_e4m3fn, 7), "e5m2": (ml_dtypes.float8_e5m2, 14)}[fmt]
    v = np.moveaxis(np.asarray(x, np.float32).astype(ml_dtypes.bfloat16).astype(np.float64), axis, -1)
    blocks = v.reshape(v.shape[:-1] + (-1, 32))
    amax = np.abs(blocks).max(-1, keepdims=True)
    byte = np.maximum(np.where(amax > 0, np.frexp(amax)[1] - 1 + 127, 0) - down, 1)
    scale = np.exp2(byte - 127.0)
    codes = (blocks / scale).astype(np.float32).astype(dtype).astype(np.float64)
    return np.moveaxis((codes * scale).reshape(v.shape), -1, axis)


WIDE = False


def mx_kscale(k):
    if not WIDE:
        return np.ones(k)
    levels = np.array([10, -10, 5, -5, 0])
    if k % 512:
        return np.exp2(np.random.permutation(np.resize(levels, k // 32))).repeat(32)
    a = np.empty((k // 512, 16))
    for p in range(k // 512):
        a[p, :8] = np.random.permutation(np.resize(levels, 8))
        for g in range(8):
            far = levels[np.abs(levels - a[p, g]) >= 10]
            a[p, g + 8] = far[np.random.randint(len(far))]
    return np.exp2(a.ravel()).repeat(32)


BF16 = ml_dtypes.bfloat16


def bf(x):
    return np.asarray(x, np.float32).astype(BF16)


def f64(x):
    return np.asarray(x).astype(np.float64)


E2M1 = np.array([0.0, 0.5, 1.0, 1.5, 2.0, 3.0, 4.0, 6.0, -0.0, -0.5, -1.0, -1.5, -2.0, -3.0, -4.0, -6.0])


def pack_weight(w, fmt):
    k, n = w.shape
    w = f64(bf(w)).reshape(k // 32, 32, n)
    amax = np.abs(w).max(1)
    if fmt == "e4m3":
        byte = np.frexp(amax)[1] - 1 + 127 - 7
    else:
        mant, ex = np.frexp(amax / 6.0)
        byte = np.where(mant > 0.5, ex, ex - 1) + 127
    byte = np.clip(np.where(amax > 0, byte, 1), 1, 254)
    scaled = (w * np.exp2(127.0 - byte)[:, None, :]).reshape(k, n).astype(np.float32)
    by_word = np.ascontiguousarray(scaled.reshape(k // 512, 128, 4, n).transpose(0, 1, 3, 2))
    if fmt == "e4m3":
        words = by_word.astype(ml_dtypes.float8_e4m3fn).view(np.uint8)
    else:
        c = by_word.astype(ml_dtypes.float4_e2m1fn).view(np.uint8) & 0xF
        words = c[..., 0::2] | (c[..., 1::2] << 4)
    return np.ascontiguousarray(words), np.ascontiguousarray(byte.astype(np.uint8).reshape(k // 512, 16, n))


def unpack_weight(words, scales, fmt):
    g, p, n, _ = words.shape
    if fmt == "e4m3":
        vals = np.ascontiguousarray(words).view(ml_dtypes.float8_e4m3fn).astype(np.float64)
    else:
        nib = np.empty((g, p, n, 4), np.uint8)
        nib[..., 0::2] = words & 0xF
        nib[..., 1::2] = words >> 4
        vals = E2M1[nib]
    vals = vals * np.repeat(np.exp2(scales.astype(np.float64) - 127.0), 8, axis=1)[..., None]
    return vals.transpose(0, 1, 3, 2).reshape(g * 512, n)
def pack4(w):
    words, scales = pack_weight(w, "e2m1")
    return words.reshape(words.shape[0], 128, -1), scales


def unpack4(words, scales):
    return unpack_weight(words.reshape(words.shape[0], 128, -1, 2), scales, "e2m1")


def planes(Y):
    n, m = Y.shape
    b = f64(bf(Y)).reshape(n // 32, 32, m)
    amax = np.abs(b).max(1)
    byte = np.clip(np.where(amax > 0, np.frexp(amax)[1] - 1 + 127 - 7, 1), 1, 254)
    codes = (b * np.exp2(127.0 - byte)[:, None, :]).reshape(n, m).astype(np.float32).astype(ml_dtypes.float8_e4m3fn).view(np.uint8)
    words = codes.reshape(n // 512, 128, 4, m).transpose(0, 1, 3, 2)
    return np.ascontiguousarray(words), np.ascontiguousarray(byte.astype(np.uint8).reshape(n // 512, 16, m))


M, K, F, N = 1024, 1536, 1024, 2048


def setup_inputs():
    s = mx_kscale(K)
    t = mx_kscale(F)
    spread = np.exp(0.8 * np.random.randn(N))
    amp = bf(0.7 * np.random.randn(M, K) * s)
    coup_words, coup_scales = pack4(np.random.randn(K, F) / np.sqrt(K) / s[:, None])
    cubic = bf(0.7 * (1.0 + 0.1 * np.random.randn(F)) * t)
    forc_words, forc_scales = pack4(np.random.randn(F, N) / np.sqrt(F) * spread / t[:, None])
    slow = bf(np.random.randn(M, N) * spread)
    drag = bf(0.5 * np.exp(0.5 * np.random.randn(N)))
    return {"amp": amp, "coup_words": coup_words, "coup_scales": coup_scales, "cubic": cubic,
            "forc_words": forc_words, "forc_scales": forc_scales, "slow": slow, "drag": drag}

def reference(amp, coup_words, coup_scales, cubic, forc_words, forc_scales, slow, drag):
    u = mxq(f64(amp), 1, "e4m3") @ unpack4(coup_words, coup_scales)
    h = u * u * u * f64(cubic)
    force = mxq(h, 1, "e4m3") @ unpack4(forc_words, forc_scales)
    y = (f64(slow) + force) / (1.0 + f64(drag))
    words, scales = planes(y.T)
    return y, words, scales

@@ -1,0 +1,342 @@
+from contextlib import ExitStack
+
+import concourse.mybir as mybir
+from concourse.masks import make_identity
+
+M, K, F, N = 1024, 1536, 1024, 2048
+FLOPS = 2 * M * K * F + 2 * M * F * N
+
+F32 = mybir.dt.float32
+BF16 = mybir.dt.bfloat16
+U32 = mybir.dt.uint32
+I32 = mybir.dt.int32
+U8 = mybir.dt.uint8
+FP8X4 = mybir.dt.float8_e4m3fn_x4
+FP4X4 = mybir.dt.float4_e2m1fn_x4
+ALU = mybir.AluOpType
+ACT = mybir.ActivationFunctionType
+
+P = 128
+BANK = 512
+TILES = M // P
+GK = K // BANK
+GF = F // BANK
+GN = N // BANK
+POOL_GROUPS = 3
+
+
+def tile_cubic_ocean_mode_step_h1_kernel(
+    tc, amp, coup_words, coup_scales, cubic, forc_words, forc_scales, slow, drag, out_0, out_1, out_2
+):
+    nc = tc.nc
+    with ExitStack() as ctx:
+        keep = ctx.enter_context(tc.tile_pool(name="keep", bufs=1))
+        work = ctx.enter_context(tc.tile_pool(name="work", bufs=3))
+        psum = ctx.enter_context(tc.psum_pool(name="psum", bufs=1))
+        ctx.enter_context(tc.manual_schedule())
+
+        def bank(b):
+            return psum.tile([P, BANK], F32, name="bank%d" % b)
+
+        c_words = keep.tile([P, GK, 2 * F], U8, align_bytes=64)
+        c_scales = keep.tile([P, GK, F], U8, align_bytes=64)
+        b_words = keep.tile([P, GF, 2 * N], U8, align_bytes=64)
+        b_scales = keep.tile([P, GF, N], U8, align_bytes=64)
+        y_codes = keep.tile([P, GN, M], U32, align_bytes=64)
+        y_scales = keep.tile([P, GN, M], U8, align_bytes=64)
+        amp_sb = keep.tile([P, TILES, K], BF16, align_bytes=64)
+        slow_sb = keep.tile([P, TILES, N], BF16, align_bytes=64)
+        cubic_sb = keep.tile([P, GF, 4], BF16)
+        drag_sb = keep.tile([P, N // P], BF16)
+        denom = keep.tile([P, N // P], F32)
+        recip = keep.tile([P, N // P], F32)
+        recip_rows = keep.tile([P, N], F32, align_bytes=64)
+        ident = keep.tile([P, P], F32, align_bytes=64)
+
+        def rows(i):
+            return slice(i * P, (i + 1) * P)
+
+        def cols(g):
+            return slice(g * BANK, (g + 1) * BANK)
+
+        def load_scales(plane, scales):
+            for q in range(4):
+                nc.sync.dma_start(
+                    out=plane[32 * q : 32 * q + 4, :, :].bitcast(I32),
+                    in_=scales[:, 4 * q : 4 * q + 4, :].rearrange("g r n -> r g n").bitcast(I32),
+                )
+
+        def load_words(words_sb, words):
+            for g in range(words.shape[0]):
+                nc.sync.dma_start(out=words_sb[:, g, :].bitcast(I32), in_=words[g].bitcast(I32))
+
+        def load_amp(i):
+            nc.sync.dma_start(out=amp_sb[:, i, :], in_=amp[rows(i), :])
+
+        def load_slow(i):
+            nc.sync.dma_start(out=slow_sb[:, i, :], in_=slow[rows(i), :])
+
+        nc.vector.memset(c_scales[:].bitcast(I32), 0)
+        nc.vector.memset(b_scales[:].bitcast(I32), 0)
+        make_identity(nc, ident[:])
+
+        load_amp(0)
+        nc.sync.dma_start(out=drag_sb[:], in_=drag.rearrange("(p j) -> p j", p=P))
+        load_amp(1)
+        load_scales(c_scales, coup_scales)
+        load_words(c_words, coup_words)
+        nc.sync.dma_start(out=cubic_sb[:], in_=cubic.rearrange("(g p t) -> p g t", p=P, t=4))
+        load_amp(2)
+        load_scales(b_scales, forc_scales)
+        load_words(b_words, forc_words)
+        for i in range(TILES):
+            load_slow(i)
+            if i + 3 < TILES:
+                load_amp(i + 3)
+
+        nc.scalar.activation(out=denom[:], in_=drag_sb[:], func=ACT.Identity, bias=1.0)
+        nc.vector.reciprocal(out=recip[:], in_=denom[:])
+
+        def spread_recip(b):
+            spread = bank(b)
+            for jj in range(4):
+                j = 4 * b + jj
+                nc.tensor.transpose(
+                    spread[:, jj * P : (jj + 1) * P], recip[:, j : j + 1].to_broadcast([P, P]), ident[:]
+                )
+            nc.scalar.copy(
+                out=recip_rows[:].rearrange("c (p j) -> c p j", p=P)[:, :, 4 * b : 4 * b + 4],
+                in_=spread[:].rearrange("c (j p) -> c p j", j=4),
+            )
+
+        a_grouped, a_codes, a_scales = {}, {}, {}
+        u_banks, squares, cubes, cube_banks = {}, {}, {}, {}
+        h_grouped, h_codes, h_scales = {}, {}, {}
+        e_banks, sums, ys, y_pairs, y_banks, y_grouped = {}, {}, {}, {}, {}, {}
+
+        def transpose_amp(i):
+            words = amp_sb[:, i, :].bitcast(F32)
+            a_grouped[i] = work.tile([P, GK, BANK], BF16, align_bytes=64, name="a_grouped")
+            for b, groups in ((6, (0, 1)), (7, (2,))):
+                turned = bank(b)
+                for slot, g in enumerate(groups):
+                    for u in range(2):
+                        at = (2 * slot + u) * P
+                        nc.tensor.transpose(
+                            turned[:, at : at + P], words[:, 256 * g + u : 256 * (g + 1) : 2], ident[:]
+                        )
+                width = len(groups)
+                nc.scalar.copy(
+                    out=a_grouped[i][:, groups[0] : groups[0] + width, :]
+                    .bitcast(F32)
+                    .rearrange("p g (m u) -> p g m u", u=2),
+                    in_=turned[:, : 256 * width].rearrange("p (g u m) -> p g m u", u=2, m=P),
+                )
+
+        def quantize_amp(i):
+            a_codes[i] = work.tile([P, GK, P], U32, align_bytes=64, name="a_codes")
+            a_scales[i] = work.tile([P, GK, P], U8, align_bytes=64, name="a_scales")
+            for lo, hi in ((0, 2), (2, 3)):
+                nc.vector.quantize_mx(
+                    out=a_codes[i][:, lo:hi, :].rearrange("p g m -> p (g m)").bitcast(FP8X4),
+                    scales=a_scales[i][:, lo:hi, :].rearrange("p g m -> p (g m)"),
+                    in_=a_grouped[i][:, lo:hi, :].rearrange("p g c -> p (g c)"),
+                )
+
+        def couple(i):
+            squares[i] = work.tile([P, GF, BANK], F32, align_bytes=64, name="squares")
+            for j in range(GF):
+                u_banks[i, j] = bank(4 + j)
+                for g in range(GK):
+                    nc.tensor.matmul_mx(
+                        out=u_banks[i, j][:],
+                        lhsT=a_codes[i][:, g, :].bitcast(FP8X4),
+                        lhsT_scale=a_scales[i][:, g, :],
+                        rhs=c_words[:, g, 2 * BANK * j : 2 * BANK * (j + 1)].bitcast(FP4X4),
+                        rhs_scale=c_scales[:, g, cols(j)],
+                        start=(g == 0),
+                        stop=(g == GK - 1),
+                    )
+                nc.scalar.activation(
+                    out=squares[i][:, j, :].rearrange("m (t p) -> m t p", t=4),
+                    in_=u_banks[i, j][:].rearrange("m (p t) -> m t p", t=4),
+                    func=ACT.Square,
+                )
+
+        def cube(i):
+            cubes[i] = work.tile([P, GF, BANK], F32, align_bytes=64, name="cubes")
+            for j in range(GF):
+                nc.vector.tensor_tensor(
+                    out=cubes[i][:, j, :].rearrange("m (t p) -> m t p", t=4),
+                    in0=u_banks[i, j][:].rearrange("m (p t) -> m t p", t=4),
+                    in1=squares[i][:, j, :].rearrange("m (t p) -> m t p", t=4),
+                    op=ALU.mult,
+                )
+
+        def transpose_cubes(i):
+            for j in range(GF):
+                cube_banks[i, j] = bank(6 + j)
+                for t in range(4):
+                    nc.tensor.transpose(
+                        cube_banks[i, j][:, t * P : (t + 1) * P], cubes[i][:, j, t * P : (t + 1) * P], ident[:]
+                    )
+
+        def weigh_cubes(i):
+            h_grouped[i] = work.tile([P, GF, BANK], BF16, align_bytes=64, name="h_grouped")
+            for j in range(GF):
+                nc.vector.tensor_tensor(
+                    out=h_grouped[i][:, j, :].rearrange("p (m t) -> p m t", t=4),
+                    in0=cube_banks[i, j][:].rearrange("p (t m) -> p m t", t=4),
+                    in1=cubic_sb[:, j, :].unsqueeze(1).to_broadcast([P, P, 4]),
+                    op=ALU.mult,
+                )
+
+        def quantize_h(i):
+            h_codes[i] = work.tile([P, GF, P], U32, align_bytes=64, name="h_codes")
+            h_scales[i] = work.tile([P, GF, P], U8, align_bytes=64, name="h_scales")
+            nc.vector.quantize_mx(
+                out=h_codes[i][:].rearrange("p g m -> p (g m)").bitcast(FP8X4),
+                scales=h_scales[i][:].rearrange("p g m -> p (g m)"),
+                in_=h_grouped[i][:].rearrange("p g c -> p (g c)"),
+            )
+
+        def force(i):
+            sums[i] = work.tile([P, N], F32, align_bytes=64, name="sums")
+            ys[i] = work.tile([P, N], F32, align_bytes=64, name="ys")
+            for j in range(GN):
+                e_banks[i, j] = bank(j)
+                for g in range(GF):
+                    nc.tensor.matmul_mx(
+                        out=e_banks[i, j][:],
+                        lhsT=h_codes[i][:, g, :].bitcast(FP8X4),
+                        lhsT_scale=h_scales[i][:, g, :],
+                        rhs=b_words[:, g, 2 * BANK * j : 2 * BANK * (j + 1)].bitcast(FP4X4),
+                        rhs_scale=b_scales[:, g, cols(j)],
+                        start=(g == 0),
+                        stop=(g == GF - 1),
+                    )
+
+        def add_slow(i, j):
+            nc.vector.tensor_tensor(
+                out=sums[i][:, cols(j)], in0=e_banks[i, j][:], in1=slow_sb[:, i, cols(j)], op=ALU.add
+            )
+
+        def damp(engine, i, j):
+            engine.tensor_tensor(
+                out=ys[i][:, cols(j)], in0=sums[i][:, cols(j)], in1=recip_rows[:, cols(j)], op=ALU.mult
+            )
+
+        def store_y(i, lo, hi):
+            nc.sync.dma_start(out=out_0[rows(i), lo * BANK : hi * BANK], in_=ys[i][:, lo * BANK : hi * BANK])
+
+        def round_y(i, j):
+            if j == 0:
+                y_pairs[i] = work.tile([P, GN, BANK], BF16, align_bytes=64, name="y_pairs")
+            nc.scalar.copy(
+                out=y_pairs[i][:, j, :].rearrange("m (u p e) -> m u p e", u=2, e=2),
+                in_=ys[i][:, cols(j)].rearrange("m (p u e) -> m u p e", u=2, e=2),
+            )
+
+        def transpose_y(i, half):
+            y_banks[i, half] = bank(half)
+            words = y_pairs[i][:, 2 * half : 2 * half + 2, :].rearrange("m g c -> m (g c)").bitcast(F32)
+            for s in range(4):
+                nc.tensor.transpose(y_banks[i, half][:, s * P : (s + 1) * P], words[:, s * P : (s + 1) * P], ident[:])
+
+        def group_y(i, half):
+            if half == 0:
+                y_grouped[i] = work.tile([P, GN, BANK], BF16, align_bytes=64, name="y_grouped")
+            nc.scalar.copy(
+                out=y_grouped[i][:, 2 * half : 2 * half + 2, :].bitcast(F32).rearrange("p g (m u) -> p g m u", u=2),
+                in_=y_banks[i, half][:].rearrange("p (g u m) -> p g m u", u=2, m=P),
+            )
+
+        def quantize_y(i, half):
+            for g in (2 * half, 2 * half + 1):
+                nc.vector.quantize_mx(
+                    out=y_codes[:, g, rows(i)].bitcast(FP8X4),
+                    scales=y_scales[:, g, rows(i)],
+                    in_=y_grouped[i][:, g, :],
+                )
+
+        def store_codes(lo, hi):
+            nc.sync.dma_start(
+                out=out_1.rearrange("g p m t -> p g (m t)").bitcast(I32)[:, :, lo * P : hi * P],
+                in_=y_codes[:].bitcast(I32)[:, :, lo * P : hi * P],
+            )
+
+        def store_scales(lo, hi):
+            for q in range(4):
+                nc.sync.dma_start(
+                    out=out_2[:, 4 * q : 4 * q + 4, lo * P : hi * P].rearrange("g r m -> r g m").bitcast(I32),
+                    in_=y_scales[32 * q : 32 * q + 4, :, lo * P : hi * P].bitcast(I32),
+                )
+
+        def live(i):
+            return 0 <= i < TILES
+
+        last = TILES - 1
+        for c in range(-2, TILES + 1):
+            if live(c - 3):
+                quantize_y(c - 3, 0)
+            if live(c - 1):
+                quantize_h(c - 1)
+            if live(c + 1):
+                quantize_amp(c + 1)
+            if live(c - 3):
+                quantize_y(c - 3, 1)
+            if live(c - 2):
+                for j in range(POOL_GROUPS, GN):
+                    damp(nc.vector, c - 2, j)
+                store_y(c - 2, 2, 4)
+            if live(c - 3) and (c - 3) % 2 == 1:
+                store_codes(c - 4, c - 2)
+            if live(c - 1):
+                force(c - 1)
+            if live(c - 2):
+                for j in range(GN):
+                    round_y(c - 2, j)
+            for j in range(GN):
+                if live(c - 1):
+                    add_slow(c - 1, j)
+                    if j < (POOL_GROUPS if c - 1 < last else 1):
+                        damp(nc.gpsimd, c - 1, j)
+                if j == 1 and live(c):
+                    cube(c)
+            if live(c + 2):
+                transpose_amp(c + 2)
+            if c in (-1, 0):
+                spread_recip(2 * c + 2)
+                spread_recip(2 * c + 3)
+            if live(c - 2):
+                transpose_y(c - 2, 0)
+                transpose_y(c - 2, 1)
+            if live(c):
+                transpose_cubes(c)
+            if live(c - 2):
+                group_y(c - 2, 0)
+                group_y(c - 2, 1)
+            if live(c):
+                weigh_cubes(c)
+            if live(c - 1) and c - 1 < last:
+                store_y(c - 1, 0, 2)
+            if live(c + 1):
+                couple(c + 1)
+
+        round_y(last, 0)
+        store_y(last, 0, 1)
+        for j in range(1, GN):
+            damp(nc.vector, last, j)
+            round_y(last, j)
+            store_y(last, j, j + 1)
+            if j % 2 == 1:
+                transpose_y(last, j // 2)
+                group_y(last, j // 2)
+        quantize_y(last - 1, 0)
+        quantize_y(last - 1, 1)
+        store_codes(last - 1, last)
+        store_scales(0, last)
+        quantize_y(last, 0)
+        quantize_y(last, 1)
+        store_codes(last, TILES)
+        store_scales(last, TILES)

@@ -22,7 +22,7 @@ TILES = M // P
 GK = K // BANK
 GF = F // BANK
 GN = N // BANK
-POOL_GROUPS = 3
+POOL_COLS = 1472
 
 
 def tile_cubic_ocean_mode_step_h1_kernel(
@@ -47,9 +47,9 @@ def tile_cubic_ocean_mode_step_h1_kernel(
         amp_sb = keep.tile([P, TILES, K], BF16, align_bytes=64)
         slow_sb = keep.tile([P, TILES, N], BF16, align_bytes=64)
         cubic_sb = keep.tile([P, GF, 4], BF16)
-        drag_sb = keep.tile([P, N // P], BF16)
-        denom = keep.tile([P, N // P], F32)
-        recip = keep.tile([P, N // P], F32)
+        drag_sb = keep.tile([P, GN, 4], BF16)
+        denom = keep.tile([P, GN, 4], F32)
+        recip = keep.tile([P, GN, 4], F32)
         recip_rows = keep.tile([P, N], F32, align_bytes=64)
         ident = keep.tile([P, P], F32, align_bytes=64)
 
@@ -66,9 +66,12 @@ def tile_cubic_ocean_mode_step_h1_kernel(
                     in_=scales[:, 4 * q : 4 * q + 4, :].rearrange("g r n -> r g n").bitcast(I32),
                 )
 
-        def load_words(words_sb, words):
-            for g in range(words.shape[0]):
-                nc.sync.dma_start(out=words_sb[:, g, :].bitcast(I32), in_=words[g].bitcast(I32))
+        def load_words(words_sb, words, half):
+            width = words.shape[2] // 2
+            part = slice(half * width, (half + 1) * width)
+            nc.sync.dma_start(
+                out=words_sb[:, :, part].bitcast(I32), in_=words[:, :, part].rearrange("g p b -> p g b").bitcast(I32)
+            )
 
         def load_amp(i):
             nc.sync.dma_start(out=amp_sb[:, i, :], in_=amp[rows(i), :])
@@ -81,43 +84,52 @@ def tile_cubic_ocean_mode_step_h1_kernel(
         make_identity(nc, ident[:])
 
         load_amp(0)
-        nc.sync.dma_start(out=drag_sb[:], in_=drag.rearrange("(p j) -> p j", p=P))
-        load_amp(1)
+        nc.sync.dma_start(out=drag_sb[:], in_=drag.rearrange("(g p t) -> p g t", p=P, t=4))
         load_scales(c_scales, coup_scales)
-        load_words(c_words, coup_words)
+        load_words(c_words, coup_words, 0)
+        load_words(c_words, coup_words, 1)
+        load_amp(1)
         nc.sync.dma_start(out=cubic_sb[:], in_=cubic.rearrange("(g p t) -> p g t", p=P, t=4))
         load_amp(2)
         load_scales(b_scales, forc_scales)
-        load_words(b_words, forc_words)
-        for i in range(TILES):
+        load_words(b_words, forc_words, 0)
+        load_slow(0)
+        load_words(b_words, forc_words, 1)
+        for i in range(1, TILES):
+            if i + 2 < TILES:
+                load_amp(i + 2)
             load_slow(i)
-            if i + 3 < TILES:
-                load_amp(i + 3)
 
         nc.scalar.activation(out=denom[:], in_=drag_sb[:], func=ACT.Identity, bias=1.0)
         nc.vector.reciprocal(out=recip[:], in_=denom[:])
 
-        def spread_recip(b):
+        def spread_recip(g, b):
             spread = bank(b)
-            for jj in range(4):
-                j = 4 * b + jj
-                nc.tensor.transpose(
-                    spread[:, jj * P : (jj + 1) * P], recip[:, j : j + 1].to_broadcast([P, P]), ident[:]
-                )
+            for t in range(4):
+                nc.tensor.transpose(spread[:, t * P : (t + 1) * P], recip[:, g, t : t + 1].to_broadcast([P, P]), ident[:])
             nc.scalar.copy(
-                out=recip_rows[:].rearrange("c (p j) -> c p j", p=P)[:, :, 4 * b : 4 * b + 4],
-                in_=spread[:].rearrange("c (j p) -> c p j", j=4),
+                out=recip_rows[:, cols(g)].rearrange("m (p t) -> m p t", t=4),
+                in_=spread[:].rearrange("m (t p) -> m p t", t=4),
             )
+
+        def pair(i):
+            return (4, 5) if i % 2 == 0 else (6, 7)
+
+        def in_blocks(natural):
+            return natural.rearrange("m (c i t) -> m c t i", i=4, t=4)
+
+        def out_blocks(by_slot):
+            return by_slot.rearrange("m (t c i) -> m c t i", i=4, t=4)
 
         a_grouped, a_codes, a_scales = {}, {}, {}
         u_banks, squares, cubes, cube_banks = {}, {}, {}, {}
         h_grouped, h_codes, h_scales = {}, {}, {}
         e_banks, sums, ys, y_pairs, y_banks, y_grouped = {}, {}, {}, {}, {}, {}
 
-        def transpose_amp(i):
+        def transpose_amp(i, banks):
             words = amp_sb[:, i, :].bitcast(F32)
             a_grouped[i] = work.tile([P, GK, BANK], BF16, align_bytes=64, name="a_grouped")
-            for b, groups in ((6, (0, 1)), (7, (2,))):
+            for b, groups in zip(banks, ((0, 1), (2,))):
                 turned = bank(b)
                 for slot, g in enumerate(groups):
                     for u in range(2):
@@ -133,20 +145,21 @@ def tile_cubic_ocean_mode_step_h1_kernel(
                     in_=turned[:, : 256 * width].rearrange("p (g u m) -> p g m u", u=2, m=P),
                 )
 
-        def quantize_amp(i):
-            a_codes[i] = work.tile([P, GK, P], U32, align_bytes=64, name="a_codes")
-            a_scales[i] = work.tile([P, GK, P], U8, align_bytes=64, name="a_scales")
-            for lo, hi in ((0, 2), (2, 3)):
-                nc.vector.quantize_mx(
-                    out=a_codes[i][:, lo:hi, :].rearrange("p g m -> p (g m)").bitcast(FP8X4),
-                    scales=a_scales[i][:, lo:hi, :].rearrange("p g m -> p (g m)"),
-                    in_=a_grouped[i][:, lo:hi, :].rearrange("p g c -> p (g c)"),
-                )
+        def quantize_amp(i, part):
+            if part == 0:
+                a_codes[i] = work.tile([P, GK, P], U32, align_bytes=64, name="a_codes")
+                a_scales[i] = work.tile([P, GK, P], U8, align_bytes=64, name="a_scales")
+            lo, hi = ((0, 2), (2, 3))[part]
+            nc.vector.quantize_mx(
+                out=a_codes[i][:, lo:hi, :].rearrange("p g m -> p (g m)").bitcast(FP8X4),
+                scales=a_scales[i][:, lo:hi, :].rearrange("p g m -> p (g m)"),
+                in_=a_grouped[i][:, lo:hi, :].rearrange("p g c -> p (g c)"),
+            )
 
         def couple(i):
             squares[i] = work.tile([P, GF, BANK], F32, align_bytes=64, name="squares")
             for j in range(GF):
-                u_banks[i, j] = bank(4 + j)
+                u_banks[i, j] = bank(pair(i)[j])
                 for g in range(GK):
                     nc.tensor.matmul_mx(
                         out=u_banks[i, j][:],
@@ -158,8 +171,8 @@ def tile_cubic_ocean_mode_step_h1_kernel(
                         stop=(g == GK - 1),
                     )
                 nc.scalar.activation(
-                    out=squares[i][:, j, :].rearrange("m (t p) -> m t p", t=4),
-                    in_=u_banks[i, j][:].rearrange("m (p t) -> m t p", t=4),
+                    out=out_blocks(squares[i][:, j, :]),
+                    in_=in_blocks(u_banks[i, j][:]),
                     func=ACT.Square,
                 )
 
@@ -167,15 +180,15 @@ def tile_cubic_ocean_mode_step_h1_kernel(
             cubes[i] = work.tile([P, GF, BANK], F32, align_bytes=64, name="cubes")
             for j in range(GF):
                 nc.vector.tensor_tensor(
-                    out=cubes[i][:, j, :].rearrange("m (t p) -> m t p", t=4),
-                    in0=u_banks[i, j][:].rearrange("m (p t) -> m t p", t=4),
-                    in1=squares[i][:, j, :].rearrange("m (t p) -> m t p", t=4),
+                    out=out_blocks(cubes[i][:, j, :]),
+                    in0=in_blocks(u_banks[i, j][:]),
+                    in1=out_blocks(squares[i][:, j, :]),
                     op=ALU.mult,
                 )
 
         def transpose_cubes(i):
             for j in range(GF):
-                cube_banks[i, j] = bank(6 + j)
+                cube_banks[i, j] = bank(pair(i)[j])
                 for t in range(4):
                     nc.tensor.transpose(
                         cube_banks[i, j][:, t * P : (t + 1) * P], cubes[i][:, j, t * P : (t + 1) * P], ident[:]
@@ -221,9 +234,15 @@ def tile_cubic_ocean_mode_step_h1_kernel(
                 out=sums[i][:, cols(j)], in0=e_banks[i, j][:], in1=slow_sb[:, i, cols(j)], op=ALU.add
             )
 
-        def damp(engine, i, j):
-            engine.tensor_tensor(
-                out=ys[i][:, cols(j)], in0=sums[i][:, cols(j)], in1=recip_rows[:, cols(j)], op=ALU.mult
+        def damp(engine, i, lo, hi):
+            engine.tensor_tensor(out=ys[i][:, lo:hi], in0=sums[i][:, lo:hi], in1=recip_rows[:, lo:hi], op=ALU.mult)
+
+        def damp_rounded(i, j):
+            nc.vector.tensor_tensor(
+                out=y_pairs[i][:, j, :].rearrange("m (u p e) -> m u p e", u=2, e=2),
+                in0=sums[i][:, cols(j)].rearrange("m (p u e) -> m u p e", u=2, e=2),
+                in1=recip_rows[:, cols(j)].rearrange("m (p u e) -> m u p e", u=2, e=2),
+                op=ALU.mult,
             )
 
         def store_y(i, lo, hi):
@@ -237,22 +256,22 @@ def tile_cubic_ocean_mode_step_h1_kernel(
                 in_=ys[i][:, cols(j)].rearrange("m (p u e) -> m u p e", u=2, e=2),
             )
 
-        def transpose_y(i, half):
-            y_banks[i, half] = bank(half)
+        def transpose_y(i, half, b):
+            y_banks[i, half] = bank(b)
             words = y_pairs[i][:, 2 * half : 2 * half + 2, :].rearrange("m g c -> m (g c)").bitcast(F32)
             for s in range(4):
                 nc.tensor.transpose(y_banks[i, half][:, s * P : (s + 1) * P], words[:, s * P : (s + 1) * P], ident[:])
 
         def group_y(i, half):
-            if half == 0:
+            if i not in y_grouped:
                 y_grouped[i] = work.tile([P, GN, BANK], BF16, align_bytes=64, name="y_grouped")
             nc.scalar.copy(
                 out=y_grouped[i][:, 2 * half : 2 * half + 2, :].bitcast(F32).rearrange("p g (m u) -> p g m u", u=2),
                 in_=y_banks[i, half][:].rearrange("p (g u m) -> p g m u", u=2, m=P),
             )
 
-        def quantize_y(i, half):
-            for g in (2 * half, 2 * half + 1):
+        def quantize_y(i, groups):
+            for g in groups:
                 nc.vector.quantize_mx(
                     out=y_codes[:, g, rows(i)].bitcast(FP8X4),
                     scales=y_scales[:, g, rows(i)],
@@ -276,67 +295,82 @@ def tile_cubic_ocean_mode_step_h1_kernel(
             return 0 <= i < TILES
 
         last = TILES - 1
-        for c in range(-2, TILES + 1):
-            if live(c - 3):
-                quantize_y(c - 3, 0)
-            if live(c - 1):
-                quantize_h(c - 1)
+        transpose_amp(0, pair(1))
+        quantize_amp(0, 0)
+        quantize_amp(0, 1)
+        spread_recip(0, 0)
+        spread_recip(1, 1)
+        couple(0)
+        transpose_amp(1, (2, 3))
+        cube(0)
+        quantize_amp(1, 0)
+        quantize_amp(1, 1)
+        transpose_amp(2, (0, 1))
+        transpose_cubes(0)
+        weigh_cubes(0)
+        couple(1)
+
+        for c in range(1, TILES + 1):
+            y_groups = list(range(GN)) if live(c - 3) else []
             if live(c + 1):
-                quantize_amp(c + 1)
-            if live(c - 3):
-                quantize_y(c - 3, 1)
+                quantize_amp(c + 1, 0)
+            else:
+                quantize_y(c - 3, y_groups[:1])
+                y_groups = y_groups[1:]
+            quantize_h(c - 1)
+            if live(c + 1):
+                quantize_amp(c + 1, 1)
             if live(c - 2):
-                for j in range(POOL_GROUPS, GN):
-                    damp(nc.vector, c - 2, j)
+                damp(nc.vector, c - 2, POOL_COLS, N)
                 store_y(c - 2, 2, 4)
-            if live(c - 3) and (c - 3) % 2 == 1:
-                store_codes(c - 4, c - 2)
-            if live(c - 1):
-                force(c - 1)
+            if live(c - 3):
+                quantize_y(c - 3, y_groups)
+                store_codes(c - 3, c - 2)
+            if c == TILES:
+                store_scales(0, last - 1)
+            force(c - 1)
             if live(c - 2):
                 for j in range(GN):
                     round_y(c - 2, j)
-            for j in range(GN):
-                if live(c - 1):
-                    add_slow(c - 1, j)
-                    if j < (POOL_GROUPS if c - 1 < last else 1):
-                        damp(nc.gpsimd, c - 1, j)
-                if j == 1 and live(c):
-                    cube(c)
+            add_slow(c - 1, 0)
+            damp(nc.gpsimd, c - 1, 0, BANK)
+            add_slow(c - 1, 1)
+            if c == 1:
+                spread_recip(2, 0)
+                spread_recip(3, 1)
+            add_slow(c - 1, 2)
+            if live(c):
+                damp(nc.gpsimd, c - 1, BANK, POOL_COLS)
+                cube(c)
+            add_slow(c - 1, 3)
             if live(c + 2):
-                transpose_amp(c + 2)
-            if c in (-1, 0):
-                spread_recip(2 * c + 2)
-                spread_recip(2 * c + 3)
+                transpose_amp(c + 2, pair(c + 1))
             if live(c - 2):
-                transpose_y(c - 2, 0)
-                transpose_y(c - 2, 1)
+                for half in range(2):
+                    transpose_y(c - 2, half, half if live(c) else 4 + half)
+                    group_y(c - 2, half)
             if live(c):
                 transpose_cubes(c)
-            if live(c - 2):
-                group_y(c - 2, 0)
-                group_y(c - 2, 1)
-            if live(c):
                 weigh_cubes(c)
-            if live(c - 1) and c - 1 < last:
                 store_y(c - 1, 0, 2)
             if live(c + 1):
                 couple(c + 1)
 
         round_y(last, 0)
         store_y(last, 0, 1)
-        for j in range(1, GN):
-            damp(nc.vector, last, j)
-            round_y(last, j)
+        damp(nc.vector, last, BANK, 2 * BANK)
+        round_y(last, 1)
+        store_y(last, 1, 2)
+        damp_rounded(last, 2)
+        damp_rounded(last, 3)
+        for half in (1, 0):
+            transpose_y(last, half, half)
+            group_y(last, half)
+        for j in (2, 3):
+            damp(nc.vector, last, j * BANK, (j + 1) * BANK)
             store_y(last, j, j + 1)
-            if j % 2 == 1:
-                transpose_y(last, j // 2)
-                group_y(last, j // 2)
-        quantize_y(last - 1, 0)
-        quantize_y(last - 1, 1)
+        quantize_y(last - 1, range(GN))
         store_codes(last - 1, last)
-        store_scales(0, last)
-        quantize_y(last, 0)
-        quantize_y(last, 1)
+        quantize_y(last, (2, 3, 0, 1))
         store_codes(last, TILES)
-        store_scales(last, TILES)
+        store_scales(last - 1, TILES)

@@ -42,8 +42,8 @@ def tile_cubic_ocean_mode_step_h1_kernel(
         c_scales = keep.tile([P, GK, F], U8, align_bytes=64)
         b_words = keep.tile([P, GF, 2 * N], U8, align_bytes=64)
         b_scales = keep.tile([P, GF, N], U8, align_bytes=64)
-        y_codes = keep.tile([P, GN, M], U32, align_bytes=64)
-        y_scales = keep.tile([P, GN, M], U8, align_bytes=64)
+        y_codes = keep.tile([P, TILES, GN, P], U32, align_bytes=64)
+        y_scales = keep.tile([P, TILES, GN, P], U8, align_bytes=64)
         amp_sb = keep.tile([P, TILES, K], BF16, align_bytes=64)
         slow_sb = keep.tile([P, TILES, N], BF16, align_bytes=64)
         cubic_sb = keep.tile([P, GF, 4], BF16)
@@ -251,9 +251,10 @@ def tile_cubic_ocean_mode_step_h1_kernel(
         def round_y(i, j):
             if j == 0:
                 y_pairs[i] = work.tile([P, GN, BANK], BF16, align_bytes=64, name="y_pairs")
-            nc.scalar.copy(
-                out=y_pairs[i][:, j, :].rearrange("m (u p e) -> m u p e", u=2, e=2),
-                in_=ys[i][:, cols(j)].rearrange("m (p u e) -> m u p e", u=2, e=2),
+            nc.scalar.activation(
+                out=y_pairs[i][:, j, :].rearrange("m (u p e) -> m p u e", u=2, e=2),
+                in_=ys[i][:, cols(j)].rearrange("m (p u e) -> m p u e", u=2, e=2),
+                func=ACT.Copy,
             )
 
         def transpose_y(i, half, b):
@@ -270,25 +271,23 @@ def tile_cubic_ocean_mode_step_h1_kernel(
                 in_=y_banks[i, half][:].rearrange("p (g u m) -> p g m u", u=2, m=P),
             )
 
-        def quantize_y(i, groups):
-            for g in groups:
-                nc.vector.quantize_mx(
-                    out=y_codes[:, g, rows(i)].bitcast(FP8X4),
-                    scales=y_scales[:, g, rows(i)],
-                    in_=y_grouped[i][:, g, :],
-                )
-
-        def store_codes(lo, hi):
-            nc.sync.dma_start(
-                out=out_1.rearrange("g p m t -> p g (m t)").bitcast(I32)[:, :, lo * P : hi * P],
-                in_=y_codes[:].bitcast(I32)[:, :, lo * P : hi * P],
+        def quantize_y(i, half):
+            part = slice(2 * half, 2 * half + 2)
+            nc.vector.quantize_mx(
+                out=y_codes[:, i, part, :].rearrange("p g m -> p (g m)").bitcast(FP8X4),
+                scales=y_scales[:, i, part, :].rearrange("p g m -> p (g m)"),
+                in_=y_grouped[i][:, part, :].rearrange("p g c -> p (g c)"),
             )
 
-        def store_scales(lo, hi):
+        def store_planes(i):
+            nc.sync.dma_start(
+                out=out_1.rearrange("g p m t -> p g (m t)").bitcast(I32)[:, :, rows(i)],
+                in_=y_codes[:, i, :, :].bitcast(I32),
+            )
             for q in range(4):
                 nc.sync.dma_start(
-                    out=out_2[:, 4 * q : 4 * q + 4, lo * P : hi * P].rearrange("g r m -> r g m").bitcast(I32),
-                    in_=y_scales[32 * q : 32 * q + 4, :, lo * P : hi * P].bitcast(I32),
+                    out=out_2[:, 4 * q : 4 * q + 4, rows(i)].rearrange("g r m -> r g m").bitcast(I32),
+                    in_=y_scales[32 * q : 32 * q + 4, i, :, :].bitcast(I32),
                 )
 
         def live(i):
@@ -311,12 +310,10 @@ def tile_cubic_ocean_mode_step_h1_kernel(
         couple(1)
 
         for c in range(1, TILES + 1):
-            y_groups = list(range(GN)) if live(c - 3) else []
             if live(c + 1):
                 quantize_amp(c + 1, 0)
             else:
-                quantize_y(c - 3, y_groups[:1])
-                y_groups = y_groups[1:]
+                quantize_y(c - 3, 0)
             quantize_h(c - 1)
             if live(c + 1):
                 quantize_amp(c + 1, 1)
@@ -324,10 +321,10 @@ def tile_cubic_ocean_mode_step_h1_kernel(
                 damp(nc.vector, c - 2, POOL_COLS, N)
                 store_y(c - 2, 2, 4)
             if live(c - 3):
-                quantize_y(c - 3, y_groups)
-                store_codes(c - 3, c - 2)
-            if c == TILES:
-                store_scales(0, last - 1)
+                if live(c + 1):
+                    quantize_y(c - 3, 0)
+                quantize_y(c - 3, 1)
+                store_planes(c - 3)
             force(c - 1)
             if live(c - 2):
                 for j in range(GN):
@@ -369,8 +366,9 @@ def tile_cubic_ocean_mode_step_h1_kernel(
         for j in (2, 3):
             damp(nc.vector, last, j * BANK, (j + 1) * BANK)
             store_y(last, j, j + 1)
-        quantize_y(last - 1, range(GN))
-        store_codes(last - 1, last)
-        quantize_y(last, (2, 3, 0, 1))
-        store_codes(last, TILES)
-        store_scales(last - 1, TILES)
+        quantize_y(last - 1, 0)
+        quantize_y(last - 1, 1)
+        store_planes(last - 1)
+        quantize_y(last, 1)
+        quantize_y(last, 0)
+        store_planes(last)

@@ -22,7 +22,8 @@ TILES = M // P
 GK = K // BANK
 GF = F // BANK
 GN = N // BANK
-POOL_COLS = 1472
+POOL_COLS = 3 * BANK
+MERGED = TILES - 2
 
 
 def tile_cubic_ocean_mode_step_h1_kernel(
@@ -42,15 +43,17 @@ def tile_cubic_ocean_mode_step_h1_kernel(
         c_scales = keep.tile([P, GK, F], U8, align_bytes=64)
         b_words = keep.tile([P, GF, 2 * N], U8, align_bytes=64)
         b_scales = keep.tile([P, GF, N], U8, align_bytes=64)
-        y_codes = keep.tile([P, TILES, GN, P], U32, align_bytes=64)
-        y_scales = keep.tile([P, TILES, GN, P], U8, align_bytes=64)
+        y_codes = keep.tile([P, MERGED, GN, P], U32, align_bytes=64)
+        y_scales = keep.tile([P, MERGED, GN, P], U8, align_bytes=64)
+        end_codes = keep.tile([P, GN, 2 * P], U32, align_bytes=64)
+        end_scales = keep.tile([P, GN, 2 * P], U8, align_bytes=64)
         amp_sb = keep.tile([P, TILES, K], BF16, align_bytes=64)
         slow_sb = keep.tile([P, TILES, N], BF16, align_bytes=64)
         cubic_sb = keep.tile([P, GF, 4], BF16)
         drag_sb = keep.tile([P, GN, 4], BF16)
         denom = keep.tile([P, GN, 4], F32)
         recip = keep.tile([P, GN, 4], F32)
-        recip_rows = keep.tile([P, N], F32, align_bytes=64)
+        recip_rows = keep.tile([P, POOL_COLS], F32, align_bytes=64)
         ident = keep.tile([P, P], F32, align_bytes=64)
 
         def rows(i):
@@ -83,7 +86,8 @@ def tile_cubic_ocean_mode_step_h1_kernel(
         nc.vector.memset(b_scales[:].bitcast(I32), 0)
         make_identity(nc, ident[:])
 
-        load_amp(0)
+        nc.sync.dma_start(out=amp_sb[:, 0, : 2 * BANK], in_=amp[rows(0), : 2 * BANK])
+        nc.sync.dma_start(out=amp_sb[:, 0, 2 * BANK :], in_=amp[rows(0), 2 * BANK :])
         nc.sync.dma_start(out=drag_sb[:], in_=drag.rearrange("(g p t) -> p g t", p=P, t=4))
         load_scales(c_scales, coup_scales)
         load_words(c_words, coup_words, 0)
@@ -107,6 +111,10 @@ def tile_cubic_ocean_mode_step_h1_kernel(
             spread = bank(b)
             for t in range(4):
                 nc.tensor.transpose(spread[:, t * P : (t + 1) * P], recip[:, g, t : t + 1].to_broadcast([P, P]), ident[:])
+            return spread
+
+        def keep_recip(g, b):
+            spread = spread_recip(g, b)
             nc.scalar.copy(
                 out=recip_rows[:, cols(g)].rearrange("m (p t) -> m p t", t=4),
                 in_=spread[:].rearrange("m (t p) -> m p t", t=4),
@@ -186,13 +194,12 @@ def tile_cubic_ocean_mode_step_h1_kernel(
                     op=ALU.mult,
                 )
 
-        def transpose_cubes(i):
-            for j in range(GF):
-                cube_banks[i, j] = bank(pair(i)[j])
-                for t in range(4):
-                    nc.tensor.transpose(
-                        cube_banks[i, j][:, t * P : (t + 1) * P], cubes[i][:, j, t * P : (t + 1) * P], ident[:]
-                    )
+        def transpose_cubes(i, j):
+            cube_banks[i, j] = bank(pair(i)[j])
+            for t in range(4):
+                nc.tensor.transpose(
+                    cube_banks[i, j][:, t * P : (t + 1) * P], cubes[i][:, j, t * P : (t + 1) * P], ident[:]
+                )
 
         def weigh_cubes(i):
             h_grouped[i] = work.tile([P, GF, BANK], BF16, align_bytes=64, name="h_grouped")
@@ -217,7 +224,7 @@ def tile_cubic_ocean_mode_step_h1_kernel(
             sums[i] = work.tile([P, N], F32, align_bytes=64, name="sums")
             ys[i] = work.tile([P, N], F32, align_bytes=64, name="ys")
             for j in range(GN):
-                e_banks[i, j] = bank(j)
+                e_banks[i, j] = bank((pair(i) + (0, 1))[j])
                 for g in range(GF):
                     nc.tensor.matmul_mx(
                         out=e_banks[i, j][:],
@@ -237,11 +244,19 @@ def tile_cubic_ocean_mode_step_h1_kernel(
         def damp(engine, i, lo, hi):
             engine.tensor_tensor(out=ys[i][:, lo:hi], in0=sums[i][:, lo:hi], in1=recip_rows[:, lo:hi], op=ALU.mult)
 
-        def damp_rounded(i, j):
+        def damp_last_group(i):
+            nc.vector.tensor_tensor(
+                out=ys[i][:, POOL_COLS:].rearrange("m (p t) -> m p t", t=4),
+                in0=sums[i][:, POOL_COLS:].rearrange("m (p t) -> m p t", t=4),
+                in1=recip_bank[0][:].rearrange("m (t p) -> m p t", t=4),
+                op=ALU.mult,
+            )
+
+        def damp_rounded(i, j, factors):
             nc.vector.tensor_tensor(
                 out=y_pairs[i][:, j, :].rearrange("m (u p e) -> m u p e", u=2, e=2),
                 in0=sums[i][:, cols(j)].rearrange("m (p u e) -> m u p e", u=2, e=2),
-                in1=recip_rows[:, cols(j)].rearrange("m (p u e) -> m u p e", u=2, e=2),
+                in1=factors,
                 op=ALU.mult,
             )
 
@@ -271,59 +286,78 @@ def tile_cubic_ocean_mode_step_h1_kernel(
                 in_=y_banks[i, half][:].rearrange("p (g u m) -> p g m u", u=2, m=P),
             )
 
-        def quantize_y(i, half):
-            part = slice(2 * half, 2 * half + 2)
+        def quantize_y(i, lo, hi):
             nc.vector.quantize_mx(
-                out=y_codes[:, i, part, :].rearrange("p g m -> p (g m)").bitcast(FP8X4),
-                scales=y_scales[:, i, part, :].rearrange("p g m -> p (g m)"),
-                in_=y_grouped[i][:, part, :].rearrange("p g c -> p (g c)"),
+                out=y_codes[:, i, lo:hi, :].rearrange("p g m -> p (g m)").bitcast(FP8X4),
+                scales=y_scales[:, i, lo:hi, :].rearrange("p g m -> p (g m)"),
+                in_=y_grouped[i][:, lo:hi, :].rearrange("p g c -> p (g c)"),
             )
 
-        def store_planes(i):
-            nc.sync.dma_start(
-                out=out_1.rearrange("g p m t -> p g (m t)").bitcast(I32)[:, :, rows(i)],
-                in_=y_codes[:, i, :, :].bitcast(I32),
-            )
-            for q in range(4):
-                nc.sync.dma_start(
-                    out=out_2[:, 4 * q : 4 * q + 4, rows(i)].rearrange("g r m -> r g m").bitcast(I32),
-                    in_=y_scales[32 * q : 32 * q + 4, i, :, :].bitcast(I32),
+        def quantize_end(i, groups):
+            for g in groups:
+                nc.vector.quantize_mx(
+                    out=end_codes[:, g, rows(i - MERGED)].bitcast(FP8X4),
+                    scales=end_scales[:, g, rows(i - MERGED)],
+                    in_=y_grouped[i][:, g, :],
                 )
+
+        out_words = out_1.rearrange("g p m t -> p g (m t)").bitcast(I32)
+
+        def store_scales(queue, plane, members):
+            for q in range(4):
+                queue.dma_start(
+                    out=out_2[:, 4 * q : 4 * q + 4, members].rearrange("g r m -> r g m").bitcast(I32),
+                    in_=plane[32 * q : 32 * q + 4, :, :].bitcast(I32),
+                )
+
+        def store_planes(i):
+            nc.sync.dma_start(out=out_words[:, :, rows(i)], in_=y_codes[:, i, :, :].bitcast(I32))
+            store_scales(nc.sync, y_scales[:, i, :, :], rows(i))
+
+        def store_end_codes(i, lo, hi):
+            nc.sync.dma_start(
+                out=out_words[:, lo:hi, rows(i)], in_=end_codes[:, lo:hi, rows(i - MERGED)].bitcast(I32)
+            )
 
         def live(i):
             return 0 <= i < TILES
 
         last = TILES - 1
+        recip_bank = []
         transpose_amp(0, pair(1))
         quantize_amp(0, 0)
         quantize_amp(0, 1)
-        spread_recip(0, 0)
-        spread_recip(1, 1)
+        keep_recip(0, 0)
+        keep_recip(1, 1)
         couple(0)
         transpose_amp(1, (2, 3))
         cube(0)
         quantize_amp(1, 0)
         quantize_amp(1, 1)
         transpose_amp(2, (0, 1))
-        transpose_cubes(0)
+        transpose_cubes(0, 0)
+        transpose_cubes(0, 1)
         weigh_cubes(0)
         couple(1)
 
         for c in range(1, TILES + 1):
-            if live(c + 1):
+            if c == 1:
+                quantize_amp(2, 0)
+                quantize_h(0)
+                quantize_amp(2, 1)
+            elif live(c + 1):
+                quantize_h(c - 1)
                 quantize_amp(c + 1, 0)
-            else:
-                quantize_y(c - 3, 0)
-            quantize_h(c - 1)
-            if live(c + 1):
                 quantize_amp(c + 1, 1)
-            if live(c - 2):
-                damp(nc.vector, c - 2, POOL_COLS, N)
+                if live(c - 3):
+                    quantize_y(c - 3, 0, GN)
+            else:
+                quantize_y(c - 3, 0, 2)
+                quantize_h(c - 1)
+                quantize_y(c - 3, 2, GN)
+                damp_last_group(c - 2)
                 store_y(c - 2, 2, 4)
             if live(c - 3):
-                if live(c + 1):
-                    quantize_y(c - 3, 0)
-                quantize_y(c - 3, 1)
                 store_planes(c - 3)
             force(c - 1)
             if live(c - 2):
@@ -333,8 +367,8 @@ def tile_cubic_ocean_mode_step_h1_kernel(
             damp(nc.gpsimd, c - 1, 0, BANK)
             add_slow(c - 1, 1)
             if c == 1:
-                spread_recip(2, 0)
-                spread_recip(3, 1)
+                keep_recip(2, 2)
+                recip_bank.append(spread_recip(3, 3))
             add_slow(c - 1, 2)
             if live(c):
                 damp(nc.gpsimd, c - 1, BANK, POOL_COLS)
@@ -342,14 +376,20 @@ def tile_cubic_ocean_mode_step_h1_kernel(
             add_slow(c - 1, 3)
             if live(c + 2):
                 transpose_amp(c + 2, pair(c + 1))
-            if live(c - 2):
-                for half in range(2):
-                    transpose_y(c - 2, half, half if live(c) else 4 + half)
+            for half in range(2):
+                if live(c - 2):
+                    transpose_y(c - 2, half, 2 * half if live(c) else 4 + half)
                     group_y(c - 2, half)
+                if live(c):
+                    transpose_cubes(c, half)
             if live(c):
-                transpose_cubes(c)
                 weigh_cubes(c)
+            if live(c + 2):
+                damp_last_group(c - 1)
+            if live(c):
                 store_y(c - 1, 0, 2)
+            if live(c + 2):
+                store_y(c - 1, 2, 4)
             if live(c + 1):
                 couple(c + 1)
 
@@ -358,17 +398,19 @@ def tile_cubic_ocean_mode_step_h1_kernel(
         damp(nc.vector, last, BANK, 2 * BANK)
         round_y(last, 1)
         store_y(last, 1, 2)
-        damp_rounded(last, 2)
-        damp_rounded(last, 3)
+        damp_rounded(last, 2, recip_rows[:, cols(2)].rearrange("m (p u e) -> m u p e", u=2, e=2))
+        damp_rounded(last, 3, recip_bank[0][:].rearrange("m (u e p) -> m u p e", u=2, e=2))
         for half in (1, 0):
             transpose_y(last, half, half)
             group_y(last, half)
-        for j in (2, 3):
-            damp(nc.vector, last, j * BANK, (j + 1) * BANK)
-            store_y(last, j, j + 1)
-        quantize_y(last - 1, 0)
-        quantize_y(last - 1, 1)
-        store_planes(last - 1)
-        quantize_y(last, 1)
-        quantize_y(last, 0)
-        store_planes(last)
+        quantize_end(last - 1, range(GN))
+        store_end_codes(last - 1, 0, GN)
+        damp(nc.vector, last, 2 * BANK, 3 * BANK)
+        store_y(last, 2, 3)
+        damp_last_group(last)
+        store_y(last, 3, 4)
+        quantize_end(last, (2, 3))
+        store_end_codes(last, 2, GN)
+        quantize_end(last, (0, 1))
+        store_end_codes(last, 0, 2)
+        store_scales(nc.scalar, end_scales, slice(MERGED * P, M))

@@ -129,10 +129,17 @@ def tile_cubic_ocean_mode_step_h1_kernel(
         def out_blocks(by_slot):
             return by_slot.rearrange("m (t c i) -> m c t i", i=4, t=4)
 
-        a_grouped, a_codes, a_scales = {}, {}, {}
+        a_sorted, a_grouped, a_codes, a_scales = {}, {}, {}, {}
         u_banks, squares, cubes, cube_banks = {}, {}, {}, {}
         h_grouped, h_codes, h_scales = {}, {}, {}
         e_banks, sums, ys, y_pairs, y_banks, y_grouped = {}, {}, {}, {}, {}, {}
+
+        def sort_amp(i, copy):
+            a_sorted[i] = work.tile([P, GK, 2, P], F32, align_bytes=64, name="a_sorted")
+            copy(
+                out=a_sorted[i][:].rearrange("m g u p -> m g p u"),
+                in_=amp_sb[:, i, :].bitcast(F32).rearrange("m (g p u) -> m g p u", p=P, u=2),
+            )
 
         def transpose_amp(i, banks):
             words = amp_sb[:, i, :].bitcast(F32)
@@ -142,9 +149,8 @@ def tile_cubic_ocean_mode_step_h1_kernel(
                 for slot, g in enumerate(groups):
                     for u in range(2):
                         at = (2 * slot + u) * P
-                        nc.tensor.transpose(
-                            turned[:, at : at + P], words[:, 256 * g + u : 256 * (g + 1) : 2], ident[:]
-                        )
+                        source = a_sorted[i][:, g, u, :] if i > 0 else words[:, 256 * g + u : 256 * (g + 1) : 2]
+                        nc.tensor.transpose(turned[:, at : at + P], source, ident[:])
                 width = len(groups)
                 nc.scalar.copy(
                     out=a_grouped[i][:, groups[0] : groups[0] + width, :]
@@ -254,7 +260,7 @@ def tile_cubic_ocean_mode_step_h1_kernel(
 
         def damp_rounded(i, j, factors):
             nc.vector.tensor_tensor(
-                out=y_pairs[i][:, j, :].rearrange("m (u p e) -> m u p e", u=2, e=2),
+                out=y_pairs[i][:, j // 2, :, (j % 2) * P : (j % 2 + 1) * P, :],
                 in0=sums[i][:, cols(j)].rearrange("m (p u e) -> m u p e", u=2, e=2),
                 in1=factors,
                 op=ALU.mult,
@@ -263,18 +269,19 @@ def tile_cubic_ocean_mode_step_h1_kernel(
         def store_y(i, lo, hi):
             nc.sync.dma_start(out=out_0[rows(i), lo * BANK : hi * BANK], in_=ys[i][:, lo * BANK : hi * BANK])
 
-        def round_y(i, j):
-            if j == 0:
-                y_pairs[i] = work.tile([P, GN, BANK], BF16, align_bytes=64, name="y_pairs")
+        def round_y(i, half, lo, hi):
+            if i not in y_pairs:
+                y_pairs[i] = work.tile([P, 2, 2, 2 * P, 2], BF16, align_bytes=64, name="y_pairs")
+            first = 2 * half * BANK
             nc.scalar.activation(
-                out=y_pairs[i][:, j, :].rearrange("m (u p e) -> m p u e", u=2, e=2),
-                in_=ys[i][:, cols(j)].rearrange("m (p u e) -> m p u e", u=2, e=2),
+                out=y_pairs[i][:, half, :, lo * P : hi * P, :].rearrange("m u w e -> m w u e"),
+                in_=ys[i][:, first + lo * BANK : first + hi * BANK].rearrange("m (w u e) -> m w u e", u=2, e=2),
                 func=ACT.Copy,
             )
 
         def transpose_y(i, half, b):
             y_banks[i, half] = bank(b)
-            words = y_pairs[i][:, 2 * half : 2 * half + 2, :].rearrange("m g c -> m (g c)").bitcast(F32)
+            words = y_pairs[i][:, half, :, :, :].rearrange("m u w e -> m (u w e)").bitcast(F32)
             for s in range(4):
                 nc.tensor.transpose(y_banks[i, half][:, s * P : (s + 1) * P], words[:, s * P : (s + 1) * P], ident[:])
 
@@ -283,7 +290,7 @@ def tile_cubic_ocean_mode_step_h1_kernel(
                 y_grouped[i] = work.tile([P, GN, BANK], BF16, align_bytes=64, name="y_grouped")
             nc.scalar.copy(
                 out=y_grouped[i][:, 2 * half : 2 * half + 2, :].bitcast(F32).rearrange("p g (m u) -> p g m u", u=2),
-                in_=y_banks[i, half][:].rearrange("p (g u m) -> p g m u", u=2, m=P),
+                in_=y_banks[i, half][:].rearrange("p (u g m) -> p g m u", u=2, m=P),
             )
 
         def quantize_y(i, lo, hi):
@@ -330,6 +337,8 @@ def tile_cubic_ocean_mode_step_h1_kernel(
         keep_recip(0, 0)
         keep_recip(1, 1)
         couple(0)
+        sort_amp(1, nc.vector.tensor_copy)
+        sort_amp(2, nc.vector.tensor_copy)
         transpose_amp(1, (2, 3))
         cube(0)
         quantize_amp(1, 0)
@@ -337,8 +346,10 @@ def tile_cubic_ocean_mode_step_h1_kernel(
         transpose_amp(2, (0, 1))
         transpose_cubes(0, 0)
         transpose_cubes(0, 1)
+        keep_recip(2, 2)
         weigh_cubes(0)
         couple(1)
+        sort_amp(3, nc.scalar.copy)
 
         for c in range(1, TILES + 1):
             if c == 1:
@@ -361,13 +372,12 @@ def tile_cubic_ocean_mode_step_h1_kernel(
                 store_planes(c - 3)
             force(c - 1)
             if live(c - 2):
-                for j in range(GN):
-                    round_y(c - 2, j)
+                round_y(c - 2, 0, 0, 2)
+                round_y(c - 2, 1, 0, 2)
             add_slow(c - 1, 0)
             damp(nc.gpsimd, c - 1, 0, BANK)
             add_slow(c - 1, 1)
             if c == 1:
-                keep_recip(2, 2)
                 recip_bank.append(spread_recip(3, 3))
             add_slow(c - 1, 2)
             if live(c):
@@ -382,6 +392,8 @@ def tile_cubic_ocean_mode_step_h1_kernel(
                     group_y(c - 2, half)
                 if live(c):
                     transpose_cubes(c, half)
+            if live(c + 3):
+                sort_amp(c + 3, nc.scalar.copy)
             if live(c):
                 weigh_cubes(c)
             if live(c + 2):
@@ -393,10 +405,10 @@ def tile_cubic_ocean_mode_step_h1_kernel(
             if live(c + 1):
                 couple(c + 1)
 
-        round_y(last, 0)
+        round_y(last, 0, 0, 1)
         store_y(last, 0, 1)
         damp(nc.vector, last, BANK, 2 * BANK)
-        round_y(last, 1)
+        round_y(last, 0, 1, 2)
         store_y(last, 1, 2)
         damp_rounded(last, 2, recip_rows[:, cols(2)].rearrange("m (p u e) -> m u p e", u=2, e=2))
         damp_rounded(last, 3, recip_bank[0][:].rearrange("m (u e p) -> m u p e", u=2, e=2))

@@ -10,6 +10,7 @@ F32 = mybir.dt.float32
 BF16 = mybir.dt.bfloat16
 U32 = mybir.dt.uint32
 I32 = mybir.dt.int32
+U16 = mybir.dt.uint16
 U8 = mybir.dt.uint8
 FP8X4 = mybir.dt.float8_e4m3fn_x4
 FP4X4 = mybir.dt.float4_e2m1fn_x4
@@ -19,11 +20,14 @@ ACT = mybir.ActivationFunctionType
 P = 128
 BANK = 512
 TILES = M // P
+PAIR = 2 * P
 GK = K // BANK
 GF = F // BANK
 GN = N // BANK
-POOL_COLS = 3 * BANK
-MERGED = TILES - 2
+MERGED = TILES - 3
+RING = 7
+VECTOR_MEMBERS = 160
+LOOP_MEMBERS = 96
 
 
 def tile_cubic_ocean_mode_step_h1_kernel(
@@ -32,29 +36,38 @@ def tile_cubic_ocean_mode_step_h1_kernel(
     nc = tc.nc
     with ExitStack() as ctx:
         keep = ctx.enter_context(tc.tile_pool(name="keep", bufs=1))
-        work = ctx.enter_context(tc.tile_pool(name="work", bufs=3))
+        work = ctx.enter_context(tc.tile_pool(name="work", bufs=2))
+        deep = ctx.enter_context(tc.tile_pool(name="deep", bufs=3))
         psum = ctx.enter_context(tc.psum_pool(name="psum", bufs=1))
         ctx.enter_context(tc.manual_schedule())
 
-        def bank(b):
+        ring = list(range(RING))
+
+        def ring_bank(hold=False):
+            b = ring.pop(0)
+            if not hold:
+                ring.append(b)
             return psum.tile([P, BANK], F32, name="bank%d" % b)
 
-        c_words = keep.tile([P, GK, 2 * F], U8, align_bytes=64)
-        c_scales = keep.tile([P, GK, F], U8, align_bytes=64)
-        b_words = keep.tile([P, GF, 2 * N], U8, align_bytes=64)
+        c_raw_words = [keep.tile([P, GK, 2 * BANK], U8, align_bytes=64, name="c_raw_words%d" % f) for f in range(GF)]
+        c_raw_scales = keep.tile([P, GK, F], U8, align_bytes=64)
+        c_words = [keep.tile([P, GK, 2 * BANK], U8, align_bytes=64, name="c_words%d" % f) for f in range(GF)]
+        c_scales = [keep.tile([P, GK, BANK], U8, align_bytes=64, name="c_scales%d" % f) for f in range(GF)]
+        b_words = [keep.tile([P, GF, N], U8, align_bytes=64, name="b_words%d" % h) for h in range(2)]
         b_scales = keep.tile([P, GF, N], U8, align_bytes=64)
         y_codes = keep.tile([P, MERGED, GN, P], U32, align_bytes=64)
         y_scales = keep.tile([P, MERGED, GN, P], U8, align_bytes=64)
-        end_codes = keep.tile([P, GN, 2 * P], U32, align_bytes=64)
-        end_scales = keep.tile([P, GN, 2 * P], U8, align_bytes=64)
-        amp_sb = keep.tile([P, TILES, K], BF16, align_bytes=64)
-        slow_sb = keep.tile([P, TILES, N], BF16, align_bytes=64)
+        end_codes = keep.tile([P, GN, (TILES - MERGED) * P], U32, align_bytes=64)
+        end_scales = keep.tile([P, GN, (TILES - MERGED) * P], U8, align_bytes=64)
+        amp_sb = [keep.tile([P, K], BF16, align_bytes=64, name="amp%d" % i) for i in range(TILES)]
+        slow_sb = [keep.tile([P, N], BF16, align_bytes=64, name="slow%d" % i) for i in range(TILES)]
         cubic_sb = keep.tile([P, GF, 4], BF16)
         drag_sb = keep.tile([P, GN, 4], BF16)
         denom = keep.tile([P, GN, 4], F32)
         recip = keep.tile([P, GN, 4], F32)
-        recip_rows = keep.tile([P, POOL_COLS], F32, align_bytes=64)
+        recip_rows = keep.tile([P, 3 * BANK], F32, align_bytes=64)
         ident = keep.tile([P, P], F32, align_bytes=64)
+        recip_banks = {GN - 1: psum.tile([P, BANK], F32, name="recip_bank")}
 
         def rows(i):
             return slice(i * P, (i + 1) * P)
@@ -73,205 +86,198 @@ def tile_cubic_ocean_mode_step_h1_kernel(
             width = words.shape[2] // 2
             part = slice(half * width, (half + 1) * width)
             nc.sync.dma_start(
-                out=words_sb[:, :, part].bitcast(I32), in_=words[:, :, part].rearrange("g p b -> p g b").bitcast(I32)
+                out=words_sb[half][:].bitcast(I32), in_=words[:, :, part].rearrange("g p b -> p g b").bitcast(I32)
             )
 
         def load_amp(i):
-            nc.sync.dma_start(out=amp_sb[:, i, :], in_=amp[rows(i), :])
+            nc.sync.dma_start(out=amp_sb[i][:], in_=amp[rows(i), :])
 
         def load_slow(i):
-            nc.sync.dma_start(out=slow_sb[:, i, :], in_=slow[rows(i), :])
+            nc.sync.dma_start(out=slow_sb[i][:], in_=slow[rows(i), :])
 
-        nc.vector.memset(c_scales[:].bitcast(I32), 0)
-        nc.vector.memset(b_scales[:].bitcast(I32), 0)
-        make_identity(nc, ident[:])
+        def deal_scales(f):
+            nc.vector.tensor_copy(
+                out=c_scales[f][:].rearrange("p g (t c i) -> p c g t i", t=4, i=16),
+                in_=c_raw_scales[:, :, cols(f)].rearrange("p g (c i t) -> p c g t i", t=4, i=16),
+            )
 
-        nc.sync.dma_start(out=amp_sb[:, 0, : 2 * BANK], in_=amp[rows(0), : 2 * BANK])
-        nc.sync.dma_start(out=amp_sb[:, 0, 2 * BANK :], in_=amp[rows(0), 2 * BANK :])
-        nc.sync.dma_start(out=drag_sb[:], in_=drag.rearrange("(g p t) -> p g t", p=P, t=4))
-        load_scales(c_scales, coup_scales)
-        load_words(c_words, coup_words, 0)
-        load_words(c_words, coup_words, 1)
-        load_amp(1)
-        nc.sync.dma_start(out=cubic_sb[:], in_=cubic.rearrange("(g p t) -> p g t", p=P, t=4))
-        load_amp(2)
-        load_scales(b_scales, forc_scales)
-        load_words(b_words, forc_words, 0)
-        load_slow(0)
-        load_words(b_words, forc_words, 1)
-        for i in range(1, TILES):
-            if i + 2 < TILES:
-                load_amp(i + 2)
-            load_slow(i)
+        def deal_words(f):
+            nc.vector.tensor_copy(
+                out=c_words[f][:].bitcast(U16).rearrange("p g (t c i) -> p c g t i", t=4, i=8),
+                in_=c_raw_words[f][:].bitcast(U16).rearrange("p g (c i t) -> p c g t i", t=4, i=8),
+            )
 
-        nc.scalar.activation(out=denom[:], in_=drag_sb[:], func=ACT.Identity, bias=1.0)
-        nc.vector.reciprocal(out=recip[:], in_=denom[:])
-
-        def spread_recip(g, b):
-            spread = bank(b)
+        def spread_recip(g, spread):
             for t in range(4):
                 nc.tensor.transpose(spread[:, t * P : (t + 1) * P], recip[:, g, t : t + 1].to_broadcast([P, P]), ident[:])
-            return spread
 
-        def keep_recip(g, b):
-            spread = spread_recip(g, b)
+        def keep_recip(g):
+            spread = ring_bank()
+            spread_recip(g, spread)
             nc.scalar.copy(
                 out=recip_rows[:, cols(g)].rearrange("m (p t) -> m p t", t=4),
                 in_=spread[:].rearrange("m (t p) -> m p t", t=4),
             )
 
-        def pair(i):
-            return (4, 5) if i % 2 == 0 else (6, 7)
-
-        def in_blocks(natural):
-            return natural.rearrange("m (c i t) -> m c t i", i=4, t=4)
-
-        def out_blocks(by_slot):
-            return by_slot.rearrange("m (t c i) -> m c t i", i=4, t=4)
-
-        a_sorted, a_grouped, a_codes, a_scales = {}, {}, {}, {}
-        u_banks, squares, cubes, cube_banks = {}, {}, {}, {}
-        h_grouped, h_codes, h_scales = {}, {}, {}
+        a_sorted, a_banks, a_grouped, a_codes, a_scales = {}, {}, {}, {}, {}
+        u_banks, squares, h_slots, h_grouped, h_codes, h_scales = {}, {}, {}, {}, {}, {}
         e_banks, sums, ys, y_pairs, y_banks, y_grouped = {}, {}, {}, {}, {}, {}
 
-        def sort_amp(i, copy):
-            a_sorted[i] = work.tile([P, GK, 2, P], F32, align_bytes=64, name="a_sorted")
-            copy(
-                out=a_sorted[i][:].rearrange("m g u p -> m g p u"),
-                in_=amp_sb[:, i, :].bitcast(F32).rearrange("m (g p u) -> m g p u", p=P, u=2),
-            )
-
-        def transpose_amp(i, banks):
-            words = amp_sb[:, i, :].bitcast(F32)
-            a_grouped[i] = work.tile([P, GK, BANK], BF16, align_bytes=64, name="a_grouped")
-            for b, groups in zip(banks, ((0, 1), (2,))):
-                turned = bank(b)
-                for slot, g in enumerate(groups):
-                    for u in range(2):
-                        at = (2 * slot + u) * P
-                        source = a_sorted[i][:, g, u, :] if i > 0 else words[:, 256 * g + u : 256 * (g + 1) : 2]
-                        nc.tensor.transpose(turned[:, at : at + P], source, ident[:])
-                width = len(groups)
+        def sort_amp(n):
+            a_sorted[n] = work.tile([P, GK, 2, P], F32, align_bytes=64, name="a_sorted")
+            for h, lo, hi, at in ((0, 0, 2, 0), (1, 0, 1, 2)) if n % 2 == 0 else ((0, 2, 3, 0), (1, 1, 3, 1)):
+                words = amp_sb[2 * (n // 2) + h][:].bitcast(F32)[:, 256 * lo : 256 * hi]
                 nc.scalar.copy(
-                    out=a_grouped[i][:, groups[0] : groups[0] + width, :]
-                    .bitcast(F32)
-                    .rearrange("p g (m u) -> p g m u", u=2),
-                    in_=turned[:, : 256 * width].rearrange("p (g u m) -> p g m u", u=2, m=P),
+                    out=a_sorted[n][:, at : at + hi - lo, :, :].rearrange("m g u p -> m g p u"),
+                    in_=words.rearrange("m (g p u) -> m g p u", p=P, u=2),
                 )
 
-        def quantize_amp(i, part):
-            if part == 0:
-                a_codes[i] = work.tile([P, GK, P], U32, align_bytes=64, name="a_codes")
-                a_scales[i] = work.tile([P, GK, P], U8, align_bytes=64, name="a_scales")
-            lo, hi = ((0, 2), (2, 3))[part]
+        def amp_pieces(n):
+            return (((0, 0), (0, 1)), ((1, 0),)) if n % 2 == 0 else (((1, 1),), ((2, 0), (2, 1)))
+
+        def transpose_amp(*parts):
+            for n in parts:
+                for b in range(2):
+                    a_banks[n, b] = ring_bank()
+            for tile_h in range(2):
+                for n in parts:
+                    for b, pieces in enumerate(amp_pieces(n)):
+                        for slot, (g, h) in enumerate(pieces):
+                            if h == tile_h:
+                                i = 2 * (n // 2) + h
+                                words = amp_sb[i][:].bitcast(F32)
+                                for u in range(2):
+                                    at = (2 * slot + u) * P
+                                    source = (
+                                        a_sorted[n][:, (g + 2 * h, g - 2 + 2 * h)[n % 2], u, :]
+                                        if n in a_sorted
+                                        else words[:, 256 * g + u : 256 * (g + 1) : 2]
+                                    )
+                                    nc.tensor.transpose(a_banks[n, b][:, at : at + P], source, ident[:])
+
+        def group_amp(n):
+            a_grouped[n] = work.tile([P, 3 * BANK], BF16, align_bytes=64, name="a_grouped")
+            done = 0
+            for b, pieces in enumerate(amp_pieces(n)):
+                width = len(pieces)
+                nc.scalar.copy(
+                    out=a_grouped[n][:, done * BANK : (done + width) * BANK]
+                    .bitcast(F32)
+                    .rearrange("p (s m u) -> p s m u", u=2, m=P),
+                    in_=a_banks[n, b][:, : 256 * width].rearrange("p (s u m) -> p s m u", u=2, m=P),
+                )
+                done = done + width
+
+        def quantize_amp(n):
+            c = n // 2
+            if n % 2 == 0:
+                a_codes[c] = deep.tile([P, GK * PAIR], U32, align_bytes=64, name="a_codes")
+                a_scales[c] = deep.tile([P, GK * PAIR], U8, align_bytes=64, name="a_scales")
+            part = slice((n % 2) * 3 * P, (n % 2 + 1) * 3 * P)
             nc.vector.quantize_mx(
-                out=a_codes[i][:, lo:hi, :].rearrange("p g m -> p (g m)").bitcast(FP8X4),
-                scales=a_scales[i][:, lo:hi, :].rearrange("p g m -> p (g m)"),
-                in_=a_grouped[i][:, lo:hi, :].rearrange("p g c -> p (g c)"),
+                out=a_codes[c][:, part].bitcast(FP8X4), scales=a_scales[c][:, part], in_=a_grouped[n][:]
             )
 
-        def couple(i):
-            squares[i] = work.tile([P, GF, BANK], F32, align_bytes=64, name="squares")
-            for j in range(GF):
-                u_banks[i, j] = bank(pair(i)[j])
+        def couple(n, b):
+            c, f = divmod(n, 2)
+            u_banks[n, b] = ring_bank()
+            for s in range(2):
+                t = 2 * b + s
                 for g in range(GK):
+                    members = slice(g * PAIR, (g + 1) * PAIR)
                     nc.tensor.matmul_mx(
-                        out=u_banks[i, j][:],
-                        lhsT=a_codes[i][:, g, :].bitcast(FP8X4),
-                        lhsT_scale=a_scales[i][:, g, :],
-                        rhs=c_words[:, g, 2 * BANK * j : 2 * BANK * (j + 1)].bitcast(FP4X4),
-                        rhs_scale=c_scales[:, g, cols(j)],
+                        out=u_banks[n, b][:, s * PAIR : (s + 1) * PAIR],
+                        lhsT=c_words[f][:, g, 2 * t * P : 2 * (t + 1) * P].bitcast(FP4X4),
+                        lhsT_scale=c_scales[f][:, g, rows(t)],
+                        rhs=a_codes[c][:, members].bitcast(FP8X4),
+                        rhs_scale=a_scales[c][:, members],
                         start=(g == 0),
                         stop=(g == GK - 1),
                     )
-                nc.scalar.activation(
-                    out=out_blocks(squares[i][:, j, :]),
-                    in_=in_blocks(u_banks[i, j][:]),
-                    func=ACT.Square,
+
+        def square(n, b):
+            squares[n, b] = deep.tile([P, BANK], F32, align_bytes=64, name="squares")
+            nc.scalar.activation(out=squares[n, b][:], in_=u_banks[n, b][:], func=ACT.Square)
+
+        def cube(n, b):
+            if b == 0:
+                h_slots[n] = work.tile([P, 4, PAIR], BF16, align_bytes=64, name="h_slots")
+            for s in range(2):
+                t = 2 * b + s
+                part = slice(s * PAIR, (s + 1) * PAIR)
+                nc.vector.scalar_tensor_tensor(
+                    out=h_slots[n][:, t, :],
+                    in0=u_banks[n, b][:, part],
+                    scalar=cubic_sb[:, n % 2, t : t + 1],
+                    in1=squares[n, b][:, part],
+                    op0=ALU.mult,
+                    op1=ALU.mult,
                 )
 
-        def cube(i):
-            cubes[i] = work.tile([P, GF, BANK], F32, align_bytes=64, name="cubes")
-            for j in range(GF):
-                nc.vector.tensor_tensor(
-                    out=out_blocks(cubes[i][:, j, :]),
-                    in0=in_blocks(u_banks[i, j][:]),
-                    in1=out_blocks(squares[i][:, j, :]),
-                    op=ALU.mult,
-                )
-
-        def transpose_cubes(i, j):
-            cube_banks[i, j] = bank(pair(i)[j])
-            for t in range(4):
-                nc.tensor.transpose(
-                    cube_banks[i, j][:, t * P : (t + 1) * P], cubes[i][:, j, t * P : (t + 1) * P], ident[:]
-                )
-
-        def weigh_cubes(i):
-            h_grouped[i] = work.tile([P, GF, BANK], BF16, align_bytes=64, name="h_grouped")
-            for j in range(GF):
-                nc.vector.tensor_tensor(
-                    out=h_grouped[i][:, j, :].rearrange("p (m t) -> p m t", t=4),
-                    in0=cube_banks[i, j][:].rearrange("p (t m) -> p m t", t=4),
-                    in1=cubic_sb[:, j, :].unsqueeze(1).to_broadcast([P, P, 4]),
-                    op=ALU.mult,
-                )
-
-        def quantize_h(i):
-            h_codes[i] = work.tile([P, GF, P], U32, align_bytes=64, name="h_codes")
-            h_scales[i] = work.tile([P, GF, P], U8, align_bytes=64, name="h_scales")
-            nc.vector.quantize_mx(
-                out=h_codes[i][:].rearrange("p g m -> p (g m)").bitcast(FP8X4),
-                scales=h_scales[i][:].rearrange("p g m -> p (g m)"),
-                in_=h_grouped[i][:].rearrange("p g c -> p (g c)"),
+        def group_h(n, copy, lo, hi):
+            if n not in h_grouped:
+                h_grouped[n] = work.tile([P, PAIR, 4], BF16, align_bytes=64, name="h_grouped")
+            copy(
+                out=h_grouped[n][:, lo:hi, :].rearrange("p (c i) t -> p c t i", i=4),
+                in_=h_slots[n][:, :, lo:hi].rearrange("p t (c i) -> p c t i", i=4),
             )
 
-        def force(i):
-            sums[i] = work.tile([P, N], F32, align_bytes=64, name="sums")
-            ys[i] = work.tile([P, N], F32, align_bytes=64, name="ys")
-            for j in range(GN):
-                e_banks[i, j] = bank((pair(i) + (0, 1))[j])
-                for g in range(GF):
-                    nc.tensor.matmul_mx(
-                        out=e_banks[i, j][:],
-                        lhsT=h_codes[i][:, g, :].bitcast(FP8X4),
-                        lhsT_scale=h_scales[i][:, g, :],
-                        rhs=b_words[:, g, 2 * BANK * j : 2 * BANK * (j + 1)].bitcast(FP4X4),
-                        rhs_scale=b_scales[:, g, cols(j)],
-                        start=(g == 0),
-                        stop=(g == GF - 1),
-                    )
+        def quantize_h(n):
+            h_codes[n] = deep.tile([P, PAIR], U32, align_bytes=64, name="h_codes", bufs=4)
+            h_scales[n] = deep.tile([P, PAIR], U8, align_bytes=64, name="h_scales", bufs=4)
+            nc.vector.quantize_mx(
+                out=h_codes[n][:].bitcast(FP8X4),
+                scales=h_scales[n][:],
+                in_=h_grouped[n][:].rearrange("p m t -> p (m t)"),
+            )
+
+        def force(i, j, passes=range(GF)):
+            if i not in sums:
+                sums[i] = deep.tile([P, N], F32, align_bytes=64, name="sums")
+                ys[i] = deep.tile([P, N], F32, align_bytes=64, name="ys")
+            if (i, j) not in e_banks:
+                e_banks[i, j] = ring_bank()
+            c, h = divmod(i, 2)
+            for f in passes:
+                nc.tensor.matmul_mx(
+                    out=e_banks[i, j][:],
+                    lhsT=h_codes[2 * c + f][:, rows(h)].bitcast(FP8X4),
+                    lhsT_scale=h_scales[2 * c + f][:, rows(h)],
+                    rhs=b_words[j // 2][:, f, 2 * BANK * (j % 2) : 2 * BANK * (j % 2 + 1)].bitcast(FP4X4),
+                    rhs_scale=b_scales[:, f, cols(j)],
+                    start=(f == 0),
+                    stop=(f == GF - 1),
+                )
 
         def add_slow(i, j):
-            nc.vector.tensor_tensor(
-                out=sums[i][:, cols(j)], in0=e_banks[i, j][:], in1=slow_sb[:, i, cols(j)], op=ALU.add
-            )
+            nc.vector.tensor_tensor(out=sums[i][:, cols(j)], in0=e_banks[i, j][:], in1=slow_sb[i][:, cols(j)], op=ALU.add)
 
         def damp(engine, i, lo, hi):
             engine.tensor_tensor(out=ys[i][:, lo:hi], in0=sums[i][:, lo:hi], in1=recip_rows[:, lo:hi], op=ALU.mult)
 
-        def damp_last_group(i):
+        def damp_from_bank(i, g, lo=0):
+            part = slice(g * BANK + lo, (g + 1) * BANK)
             nc.vector.tensor_tensor(
-                out=ys[i][:, POOL_COLS:].rearrange("m (p t) -> m p t", t=4),
-                in0=sums[i][:, POOL_COLS:].rearrange("m (p t) -> m p t", t=4),
-                in1=recip_bank[0][:].rearrange("m (t p) -> m p t", t=4),
+                out=ys[i][:, part].rearrange("m (p t) -> m p t", t=4),
+                in0=sums[i][:, part].rearrange("m (p t) -> m p t", t=4),
+                in1=recip_banks[g][:].rearrange("m (t p) -> m p t", t=4)[:, lo // 4 :, :],
                 op=ALU.mult,
             )
 
-        def damp_rounded(i, j, factors):
+        def damp_rounded(i, g):
             nc.vector.tensor_tensor(
-                out=y_pairs[i][:, j // 2, :, (j % 2) * P : (j % 2 + 1) * P, :],
-                in0=sums[i][:, cols(j)].rearrange("m (p u e) -> m u p e", u=2, e=2),
-                in1=factors,
+                out=y_pairs[i][:, g // 2, :, (g % 2) * P : (g % 2 + 1) * P, :],
+                in0=sums[i][:, cols(g)].rearrange("m (p u e) -> m u p e", u=2, e=2),
+                in1=recip_banks[g][:].rearrange("m (u e p) -> m u p e", u=2, e=2),
                 op=ALU.mult,
             )
 
         def store_y(i, lo, hi):
             nc.sync.dma_start(out=out_0[rows(i), lo * BANK : hi * BANK], in_=ys[i][:, lo * BANK : hi * BANK])
 
-        def round_y(i, half, lo, hi):
+        def round_y(i, half, lo=0, hi=2):
             if i not in y_pairs:
-                y_pairs[i] = work.tile([P, 2, 2, 2 * P, 2], BF16, align_bytes=64, name="y_pairs")
+                y_pairs[i] = deep.tile([P, 2, 2, 2 * P, 2], BF16, align_bytes=64, name="y_pairs")
             first = 2 * half * BANK
             nc.scalar.activation(
                 out=y_pairs[i][:, half, :, lo * P : hi * P, :].rearrange("m u w e -> m w u e"),
@@ -279,34 +285,19 @@ def tile_cubic_ocean_mode_step_h1_kernel(
                 func=ACT.Copy,
             )
 
-        def transpose_y(i, half, b):
-            y_banks[i, half] = bank(b)
+        def transpose_y(i, half):
+            y_banks[i, half] = ring_bank()
             words = y_pairs[i][:, half, :, :, :].rearrange("m u w e -> m (u w e)").bitcast(F32)
             for s in range(4):
                 nc.tensor.transpose(y_banks[i, half][:, s * P : (s + 1) * P], words[:, s * P : (s + 1) * P], ident[:])
 
         def group_y(i, half):
             if i not in y_grouped:
-                y_grouped[i] = work.tile([P, GN, BANK], BF16, align_bytes=64, name="y_grouped")
+                y_grouped[i] = deep.tile([P, GN, BANK], BF16, align_bytes=64, name="y_grouped")
             nc.scalar.copy(
                 out=y_grouped[i][:, 2 * half : 2 * half + 2, :].bitcast(F32).rearrange("p g (m u) -> p g m u", u=2),
                 in_=y_banks[i, half][:].rearrange("p (u g m) -> p g m u", u=2, m=P),
             )
-
-        def quantize_y(i, lo, hi):
-            nc.vector.quantize_mx(
-                out=y_codes[:, i, lo:hi, :].rearrange("p g m -> p (g m)").bitcast(FP8X4),
-                scales=y_scales[:, i, lo:hi, :].rearrange("p g m -> p (g m)"),
-                in_=y_grouped[i][:, lo:hi, :].rearrange("p g c -> p (g c)"),
-            )
-
-        def quantize_end(i, groups):
-            for g in groups:
-                nc.vector.quantize_mx(
-                    out=end_codes[:, g, rows(i - MERGED)].bitcast(FP8X4),
-                    scales=end_scales[:, g, rows(i - MERGED)],
-                    in_=y_grouped[i][:, g, :],
-                )
 
         out_words = out_1.rearrange("g p m t -> p g (m t)").bitcast(I32)
 
@@ -317,11 +308,22 @@ def tile_cubic_ocean_mode_step_h1_kernel(
                     in_=plane[32 * q : 32 * q + 4, :, :].bitcast(I32),
                 )
 
-        def store_planes(i):
+        def quantize_y(i):
+            nc.vector.quantize_mx(
+                out=y_codes[:, i, :, :].rearrange("p g m -> p (g m)").bitcast(FP8X4),
+                scales=y_scales[:, i, :, :].rearrange("p g m -> p (g m)"),
+                in_=y_grouped[i][:].rearrange("p g c -> p (g c)"),
+            )
             nc.sync.dma_start(out=out_words[:, :, rows(i)], in_=y_codes[:, i, :, :].bitcast(I32))
             store_scales(nc.sync, y_scales[:, i, :, :], rows(i))
 
-        def store_end_codes(i, lo, hi):
+        def quantize_end(i, lo, hi):
+            for g in range(lo, hi):
+                nc.vector.quantize_mx(
+                    out=end_codes[:, g, rows(i - MERGED)].bitcast(FP8X4),
+                    scales=end_scales[:, g, rows(i - MERGED)],
+                    in_=y_grouped[i][:, g, :],
+                )
             nc.sync.dma_start(
                 out=out_words[:, lo:hi, rows(i)], in_=end_codes[:, lo:hi, rows(i - MERGED)].bitcast(I32)
             )
@@ -329,100 +331,198 @@ def tile_cubic_ocean_mode_step_h1_kernel(
         def live(i):
             return 0 <= i < TILES
 
-        last = TILES - 1
-        recip_bank = []
-        transpose_amp(0, pair(1))
-        quantize_amp(0, 0)
-        quantize_amp(0, 1)
-        keep_recip(0, 0)
-        keep_recip(1, 1)
-        couple(0)
-        sort_amp(1, nc.vector.tensor_copy)
-        sort_amp(2, nc.vector.tensor_copy)
-        transpose_amp(1, (2, 3))
-        cube(0)
-        quantize_amp(1, 0)
-        quantize_amp(1, 1)
-        transpose_amp(2, (0, 1))
-        transpose_cubes(0, 0)
-        transpose_cubes(0, 1)
-        keep_recip(2, 2)
-        weigh_cubes(0)
-        couple(1)
-        sort_amp(3, nc.scalar.copy)
+        nc.vector.memset(c_raw_scales[:].bitcast(I32), 0)
+        nc.vector.memset(b_scales[:].bitcast(I32), 0)
+        make_identity(nc, ident[:])
 
-        for c in range(1, TILES + 1):
-            if c == 1:
-                quantize_amp(2, 0)
-                quantize_h(0)
-                quantize_amp(2, 1)
-            elif live(c + 1):
-                quantize_h(c - 1)
-                quantize_amp(c + 1, 0)
-                quantize_amp(c + 1, 1)
-                if live(c - 3):
-                    quantize_y(c - 3, 0, GN)
+        load_amp(0)
+        load_amp(1)
+        load_scales(c_raw_scales, coup_scales)
+        load_words(c_raw_words, coup_words, 0)
+        load_amp(2)
+        load_amp(3)
+        load_words(c_raw_words, coup_words, 1)
+        nc.sync.dma_start(out=cubic_sb[:], in_=cubic.rearrange("(g p t) -> p g t", p=P, t=4))
+        nc.sync.dma_start(out=drag_sb[:], in_=drag.rearrange("(g p t) -> p g t", p=P, t=4))
+        load_scales(b_scales, forc_scales)
+        load_words(b_words, forc_words, 0)
+        load_slow(0)
+        load_words(b_words, forc_words, 1)
+        load_amp(4)
+        load_amp(5)
+        load_slow(1)
+        load_slow(2)
+        load_amp(6)
+        load_amp(7)
+        for i in range(3, TILES):
+            load_slow(i)
+
+        deal_scales(0)
+        transpose_amp(0, 1)
+        group_amp(0)
+        group_amp(1)
+        deal_words(0)
+        quantize_amp(0)
+        quantize_amp(1)
+        sort_amp(2)
+        sort_amp(3)
+        deal_scales(1)
+        deal_words(1)
+        nc.scalar.activation(out=denom[:], in_=drag_sb[:], func=ACT.Identity, bias=1.0)
+        nc.vector.reciprocal(out=recip[:], in_=denom[:])
+        for n in range(2):
+            for b in range(2):
+                couple(n, b)
+                square(n, b)
+        cube(0, 0)
+        cube(0, 1)
+        group_h(0, nc.vector.tensor_copy, 0, PAIR)
+        cube(1, 0)
+        quantize_h(0)
+        cube(1, 1)
+        transpose_amp(2)
+        group_amp(2)
+        transpose_amp(3)
+        group_h(1, nc.vector.tensor_copy, 0, VECTOR_MEMBERS)
+        group_h(1, nc.scalar.copy, VECTOR_MEMBERS, PAIR)
+        group_amp(3)
+        spread_recip(3, recip_banks[3])
+        force(0, 0, (0,))
+        force(0, 1, (0,))
+        quantize_amp(2)
+        quantize_h(1)
+        quantize_amp(3)
+        for g in range(3):
+            keep_recip(g)
+        force(0, 0, (1,))
+        force(0, 1, (1,))
+        add_slow(0, 0)
+        add_slow(0, 1)
+        damp(nc.gpsimd, 0, 0, 2 * BANK)
+        store_y(0, 0, 2)
+        sort_amp(4)
+        sort_amp(5)
+        force(0, 2)
+        add_slow(0, 2)
+        damp(nc.gpsimd, 0, 2 * BANK, 3 * BANK)
+        force(0, 3)
+        add_slow(0, 3)
+        damp_from_bank(0, 3)
+        store_y(0, 2, 4)
+        couple(2, 0)
+        square(2, 0)
+        couple(2, 1)
+        square(2, 1)
+        cube(2, 0)
+        cube(2, 1)
+        for n in (4, 5):
+            transpose_amp(n)
+            group_amp(n)
+        group_h(2, nc.vector.tensor_copy, 0, PAIR)
+        couple(3, 0)
+        square(3, 0)
+        quantize_amp(4)
+        quantize_h(2)
+        quantize_amp(5)
+        couple(3, 1)
+        square(3, 1)
+        sort_amp(7)
+        round_y(0, 0)
+        cube(3, 0)
+        force(1, 0)
+        add_slow(1, 0)
+        force(1, 1)
+        cube(3, 1)
+
+        for s in range(1, TILES - 3):
+            if live(s + 5):
+                transpose_amp(s + 5)
+                group_amp(s + 5)
+            group_h(s + 2, nc.vector.tensor_copy, 0, LOOP_MEMBERS if s > 1 else PAIR)
+            if live(s - 2) and live(s + 5):
+                quantize_y(s - 2)
+            quantize_h(s + 2)
+            add_slow(s, 1)
+            damp(nc.gpsimd, s, 0, 2 * BANK)
+            if live(s + 5):
+                quantize_amp(s + 5)
             else:
-                quantize_y(c - 3, 0, 2)
-                quantize_h(c - 1)
-                quantize_y(c - 3, 2, GN)
-                damp_last_group(c - 2)
-                store_y(c - 2, 2, 4)
-            if live(c - 3):
-                store_planes(c - 3)
-            force(c - 1)
-            if live(c - 2):
-                round_y(c - 2, 0, 0, 2)
-                round_y(c - 2, 1, 0, 2)
-            add_slow(c - 1, 0)
-            damp(nc.gpsimd, c - 1, 0, BANK)
-            add_slow(c - 1, 1)
-            if c == 1:
-                recip_bank.append(spread_recip(3, 3))
-            add_slow(c - 1, 2)
-            if live(c):
-                damp(nc.gpsimd, c - 1, BANK, POOL_COLS)
-                cube(c)
-            add_slow(c - 1, 3)
-            if live(c + 2):
-                transpose_amp(c + 2, pair(c + 1))
-            for half in range(2):
-                if live(c - 2):
-                    transpose_y(c - 2, half, 2 * half if live(c) else 4 + half)
-                    group_y(c - 2, half)
-                if live(c):
-                    transpose_cubes(c, half)
-            if live(c + 3):
-                sort_amp(c + 3, nc.scalar.copy)
-            if live(c):
-                weigh_cubes(c)
-            if live(c + 2):
-                damp_last_group(c - 1)
-            if live(c):
-                store_y(c - 1, 0, 2)
-            if live(c + 2):
-                store_y(c - 1, 2, 4)
-            if live(c + 1):
-                couple(c + 1)
+                quantize_y(s - 2)
+            store_y(s, 0, 2)
+            for b in range(2):
+                couple(s + 3, b)
+                square(s + 3, b)
+            round_y(s - 1, 1)
+            cube(s + 3, 0)
+            cube(s + 3, 1)
+            force(s, 2)
+            add_slow(s, 2)
+            damp(nc.gpsimd, s, 2 * BANK, 3 * BANK)
+            force(s, 3)
+            add_slow(s, 3)
+            transpose_y(s - 1, 0)
+            group_y(s - 1, 0)
+            group_h(s + 3, nc.scalar.copy, LOOP_MEMBERS, PAIR)
+            round_y(s, 0)
+            force(s + 1, 0)
+            add_slow(s + 1, 0)
+            force(s + 1, 1)
+            transpose_y(s - 1, 1)
+            group_y(s - 1, 1)
+            damp_from_bank(s, 3)
+            store_y(s, 2, 4)
 
-        round_y(last, 0, 0, 1)
-        store_y(last, 0, 1)
-        damp(nc.vector, last, BANK, 2 * BANK)
-        round_y(last, 0, 1, 2)
-        store_y(last, 1, 2)
-        damp_rounded(last, 2, recip_rows[:, cols(2)].rearrange("m (p u e) -> m u p e", u=2, e=2))
-        damp_rounded(last, 3, recip_bank[0][:].rearrange("m (u e p) -> m u p e", u=2, e=2))
+        recip_banks[2] = ring_bank(hold=True)
+        spread_recip(2, recip_banks[2])
+        last = TILES - 1
+        for s in range(TILES - 3, last):
+            round_y(s - 1, 1)
+            if live(s + 2):
+                group_h(s + 2, nc.vector.tensor_copy, 0, LOOP_MEMBERS)
+                quantize_h(s + 2)
+            add_slow(s, 1)
+            damp(nc.gpsimd, s, 0, 2 * BANK)
+            quantize_y(s - 2)
+            store_y(s, 0, 2)
+            force(s, 2)
+            add_slow(s, 2)
+            damp(nc.gpsimd, s, 2 * BANK, 2 * BANK + PAIR)
+            force(s, 3)
+            add_slow(s, 3)
+            force(s + 1, 0)
+            force(s + 1, 1)
+            for half in range(2):
+                transpose_y(s - 1, half)
+                group_y(s - 1, half)
+            round_y(s, 0)
+            damp_from_bank(s, 2, PAIR)
+            damp_from_bank(s, 3)
+            add_slow(s + 1, 0)
+            store_y(s, 2, 4)
+
+        round_y(last - 1, 1)
+        add_slow(last, 1)
+        damp(nc.gpsimd, last, 0, 2 * BANK)
+        quantize_end(last - 2, 0, GN)
+        force(last, 2)
+        force(last, 3)
+        y_pairs[last] = deep.tile([P, 2, 2, 2 * P, 2], BF16, align_bytes=64, name="y_pairs")
+        for g in (2, 3):
+            add_slow(last, g)
+        for g in (2, 3):
+            damp_rounded(last, g)
+        for half in range(2):
+            transpose_y(last - 1, half)
+            group_y(last - 1, half)
+        round_y(last, 0)
+        store_y(last, 0, 2)
+        for g in (2, 3):
+            damp_from_bank(last, g)
+        store_y(last, 2, 4)
         for half in (1, 0):
-            transpose_y(last, half, half)
+            transpose_y(last, half)
             group_y(last, half)
-        quantize_end(last - 1, range(GN))
-        store_end_codes(last - 1, 0, GN)
-        damp(nc.vector, last, 2 * BANK, 3 * BANK)
-        store_y(last, 2, 3)
-        damp_last_group(last)
-        store_y(last, 3, 4)
-        quantize_end(last, (2, 3))
-        store_end_codes(last, 2, GN)
-        quantize_end(last, (0, 1))
-        store_end_codes(last, 0, 2)
+        quantize_end(last - 1, 0, GN)
+        quantize_end(last, 2, GN)
+        quantize_end(last, 0, 2)
         store_scales(nc.scalar, end_scales, slice(MERGED * P, M))

@@ -24,7 +24,7 @@ PAIR = 2 * P
 GK = K // BANK
 GF = F // BANK
 GN = N // BANK
-MERGED = TILES - 3
+MERGED = TILES - 4
 RING = 7
 VECTOR_MEMBERS = 160
 LOOP_MEMBERS = 96
@@ -324,9 +324,11 @@ def tile_cubic_ocean_mode_step_h1_kernel(
                     scales=end_scales[:, g, rows(i - MERGED)],
                     in_=y_grouped[i][:, g, :],
                 )
-            nc.sync.dma_start(
-                out=out_words[:, lo:hi, rows(i)], in_=end_codes[:, lo:hi, rows(i - MERGED)].bitcast(I32)
-            )
+
+        def store_end(first, count, lo, hi):
+            members = slice(first * P, (first + count) * P)
+            kept = slice((first - MERGED) * P, (first - MERGED + count) * P)
+            nc.sync.dma_start(out=out_words[:, lo:hi, members], in_=end_codes[:, lo:hi, kept].bitcast(I32))
 
         def live(i):
             return 0 <= i < TILES
@@ -418,36 +420,38 @@ def tile_cubic_ocean_mode_step_h1_kernel(
         for n in (4, 5):
             transpose_amp(n)
             group_amp(n)
-        group_h(2, nc.vector.tensor_copy, 0, PAIR)
         couple(3, 0)
         square(3, 0)
         quantize_amp(4)
-        quantize_h(2)
         quantize_amp(5)
+        round_y(0, 0, 0, 1)
         couple(3, 1)
         square(3, 1)
-        sort_amp(7)
-        round_y(0, 0)
+        group_h(2, nc.scalar.copy, 0, PAIR)
         cube(3, 0)
+        cube(3, 1)
         force(1, 0)
         add_slow(1, 0)
         force(1, 1)
-        cube(3, 1)
+        round_y(0, 0, 1, 2)
 
         for s in range(1, TILES - 3):
             if live(s + 5):
                 transpose_amp(s + 5)
                 group_amp(s + 5)
-            group_h(s + 2, nc.vector.tensor_copy, 0, LOOP_MEMBERS if s > 1 else PAIR)
-            if live(s - 2) and live(s + 5):
-                quantize_y(s - 2)
-            quantize_h(s + 2)
-            add_slow(s, 1)
-            damp(nc.gpsimd, s, 0, 2 * BANK)
+            if s > 1:
+                round_y(s - 1, 0)
+            if s <= 3:
+                group_h(s + 2, nc.vector.tensor_copy, 0, PAIR)
+            if s == 1:
+                quantize_h(2)
+            if live(s - 3):
+                quantize_y(s - 3)
             if live(s + 5):
                 quantize_amp(s + 5)
-            else:
-                quantize_y(s - 2)
+            add_slow(s, 1)
+            damp(nc.gpsimd, s, 0, 2 * BANK)
+            quantize_h(s + 2)
             store_y(s, 0, 2)
             for b in range(2):
                 couple(s + 3, b)
@@ -462,8 +466,8 @@ def tile_cubic_ocean_mode_step_h1_kernel(
             add_slow(s, 3)
             transpose_y(s - 1, 0)
             group_y(s - 1, 0)
-            group_h(s + 3, nc.scalar.copy, LOOP_MEMBERS, PAIR)
-            round_y(s, 0)
+            if s >= 3:
+                group_h(s + 3, nc.scalar.copy, 0, PAIR)
             force(s + 1, 0)
             add_slow(s + 1, 0)
             force(s + 1, 1)
@@ -475,18 +479,16 @@ def tile_cubic_ocean_mode_step_h1_kernel(
         recip_banks[2] = ring_bank(hold=True)
         spread_recip(2, recip_banks[2])
         last = TILES - 1
+        round_y(TILES - 4, 0)
         for s in range(TILES - 3, last):
             round_y(s - 1, 1)
             if live(s + 2):
-                group_h(s + 2, nc.vector.tensor_copy, 0, LOOP_MEMBERS)
                 quantize_h(s + 2)
             add_slow(s, 1)
             damp(nc.gpsimd, s, 0, 2 * BANK)
-            quantize_y(s - 2)
-            store_y(s, 0, 2)
+            quantize_y(s - 3)
             force(s, 2)
             add_slow(s, 2)
-            damp(nc.gpsimd, s, 2 * BANK, 2 * BANK + PAIR)
             force(s, 3)
             add_slow(s, 3)
             force(s + 1, 0)
@@ -495,15 +497,16 @@ def tile_cubic_ocean_mode_step_h1_kernel(
                 transpose_y(s - 1, half)
                 group_y(s - 1, half)
             round_y(s, 0)
-            damp_from_bank(s, 2, PAIR)
+            damp_from_bank(s, 2)
             damp_from_bank(s, 3)
             add_slow(s + 1, 0)
-            store_y(s, 2, 4)
+            store_y(s, 0, GN)
 
         round_y(last - 1, 1)
+        quantize_end(last - 3, 0, GN)
+        store_end(last - 3, 1, 0, GN)
         add_slow(last, 1)
         damp(nc.gpsimd, last, 0, 2 * BANK)
-        quantize_end(last - 2, 0, GN)
         force(last, 2)
         force(last, 3)
         y_pairs[last] = deep.tile([P, 2, 2, 2 * P, 2], BF16, align_bytes=64, name="y_pairs")
@@ -522,7 +525,11 @@ def tile_cubic_ocean_mode_step_h1_kernel(
         for half in (1, 0):
             transpose_y(last, half)
             group_y(last, half)
+        quantize_end(last - 2, 0, GN)
         quantize_end(last - 1, 0, GN)
+        store_end(last - 2, 2, 0, GN)
         quantize_end(last, 2, GN)
+        store_end(last, 1, 2, GN)
         quantize_end(last, 0, 2)
+        store_end(last, 1, 0, 2)
         store_scales(nc.scalar, end_scales, slice(MERGED * P, M))

@@ -21,11 +21,13 @@ P = 128
 BANK = 512
 TILES = M // P
 PAIR = 2 * P
+HALF = N // 2
 GK = K // BANK
 GF = F // BANK
 GN = N // BANK
 MERGED = TILES - 4
 RING = 7
+SLABS = 4
 VECTOR_MEMBERS = 160
 LOOP_MEMBERS = 96
 
@@ -119,6 +121,9 @@ def tile_cubic_ocean_mode_step_h1_kernel(
                 in_=spread[:].rearrange("m (t p) -> m p t", t=4),
             )
 
+        def slab(k, shape, dtype):
+            return keep.tile(shape, dtype, align_bytes=64, name="slab%d" % (k % SLABS))
+
         a_sorted, a_banks, a_grouped, a_codes, a_scales = {}, {}, {}, {}, {}
         u_banks, squares, h_slots, h_grouped, h_codes, h_scales = {}, {}, {}, {}, {}, {}
         e_banks, sums, ys, y_pairs, y_banks, y_grouped = {}, {}, {}, {}, {}, {}
@@ -156,7 +161,10 @@ def tile_cubic_ocean_mode_step_h1_kernel(
                                     nc.tensor.transpose(a_banks[n, b][:, at : at + P], source, ident[:])
 
         def group_amp(n):
-            a_grouped[n] = work.tile([P, 3 * BANK], BF16, align_bytes=64, name="a_grouped")
+            if n >= TILES - 2:
+                a_grouped[n] = slab(n - 5, [P, 3 * BANK], BF16)
+            else:
+                a_grouped[n] = work.tile([P, 3 * BANK], BF16, align_bytes=64, name="a_grouped")
             done = 0
             for b, pieces in enumerate(amp_pieces(n)):
                 width = len(pieces)
@@ -234,7 +242,6 @@ def tile_cubic_ocean_mode_step_h1_kernel(
         def force(i, j, passes=range(GF)):
             if i not in sums:
                 sums[i] = deep.tile([P, N], F32, align_bytes=64, name="sums")
-                ys[i] = deep.tile([P, N], F32, align_bytes=64, name="ys")
             if (i, j) not in e_banks:
                 e_banks[i, j] = ring_bank()
             c, h = divmod(i, 2)
@@ -252,15 +259,24 @@ def tile_cubic_ocean_mode_step_h1_kernel(
         def add_slow(i, j):
             nc.vector.tensor_tensor(out=sums[i][:, cols(j)], in0=e_banks[i, j][:], in1=slow_sb[i][:, cols(j)], op=ALU.add)
 
-        def damp(engine, i, lo, hi):
-            engine.tensor_tensor(out=ys[i][:, lo:hi], in0=sums[i][:, lo:hi], in1=recip_rows[:, lo:hi], op=ALU.mult)
+        def y_part(i, lo, hi):
+            half = lo // HALF
+            if (i, half) not in ys:
+                if half == 0 and i < TILES - 1:
+                    ys[i, half] = slab(i, [P, HALF], F32)
+                else:
+                    ys[i, half] = deep.tile([P, HALF], F32, align_bytes=64, name="y_half")
+            return ys[i, half][:, lo - half * HALF : hi - half * HALF]
 
-        def damp_from_bank(i, g, lo=0):
-            part = slice(g * BANK + lo, (g + 1) * BANK)
+        def damp(engine, i, lo, hi):
+            engine.tensor_tensor(out=y_part(i, lo, hi), in0=sums[i][:, lo:hi], in1=recip_rows[:, lo:hi], op=ALU.mult)
+
+        def damp_from_bank(i, g, skip=0):
+            lo, hi = g * BANK + skip, (g + 1) * BANK
             nc.vector.tensor_tensor(
-                out=ys[i][:, part].rearrange("m (p t) -> m p t", t=4),
-                in0=sums[i][:, part].rearrange("m (p t) -> m p t", t=4),
-                in1=recip_banks[g][:].rearrange("m (t p) -> m p t", t=4)[:, lo // 4 :, :],
+                out=y_part(i, lo, hi).rearrange("m (p t) -> m p t", t=4),
+                in0=sums[i][:, lo:hi].rearrange("m (p t) -> m p t", t=4),
+                in1=recip_banks[g][:].rearrange("m (t p) -> m p t", t=4)[:, skip // 4 :, :],
                 op=ALU.mult,
             )
 
@@ -272,16 +288,15 @@ def tile_cubic_ocean_mode_step_h1_kernel(
                 op=ALU.mult,
             )
 
-        def store_y(i, lo, hi):
-            nc.sync.dma_start(out=out_0[rows(i), lo * BANK : hi * BANK], in_=ys[i][:, lo * BANK : hi * BANK])
+        def store_y(i, half):
+            nc.sync.dma_start(out=out_0[rows(i), half * HALF : (half + 1) * HALF], in_=ys[i, half][:])
 
         def round_y(i, half, lo=0, hi=2):
             if i not in y_pairs:
                 y_pairs[i] = deep.tile([P, 2, 2, 2 * P, 2], BF16, align_bytes=64, name="y_pairs")
-            first = 2 * half * BANK
             nc.scalar.activation(
                 out=y_pairs[i][:, half, :, lo * P : hi * P, :].rearrange("m u w e -> m w u e"),
-                in_=ys[i][:, first + lo * BANK : first + hi * BANK].rearrange("m (w u e) -> m w u e", u=2, e=2),
+                in_=ys[i, half][:, lo * BANK : hi * BANK].rearrange("m (w u e) -> m w u e", u=2, e=2),
                 func=ACT.Copy,
             )
 
@@ -293,7 +308,7 @@ def tile_cubic_ocean_mode_step_h1_kernel(
 
         def group_y(i, half):
             if i not in y_grouped:
-                y_grouped[i] = deep.tile([P, GN, BANK], BF16, align_bytes=64, name="y_grouped")
+                y_grouped[i] = slab(i - 1, [P, GN, BANK], BF16)
             nc.scalar.copy(
                 out=y_grouped[i][:, 2 * half : 2 * half + 2, :].bitcast(F32).rearrange("p g (m u) -> p g m u", u=2),
                 in_=y_banks[i, half][:].rearrange("p (u g m) -> p g m u", u=2, m=P),
@@ -385,13 +400,14 @@ def tile_cubic_ocean_mode_step_h1_kernel(
         transpose_amp(2)
         group_amp(2)
         transpose_amp(3)
+        group_amp(3)
         group_h(1, nc.vector.tensor_copy, 0, VECTOR_MEMBERS)
         group_h(1, nc.scalar.copy, VECTOR_MEMBERS, PAIR)
-        group_amp(3)
+        quantize_amp(2)
+        sort_amp(4)
         spread_recip(3, recip_banks[3])
         force(0, 0, (0,))
         force(0, 1, (0,))
-        quantize_amp(2)
         quantize_h(1)
         quantize_amp(3)
         for g in range(3):
@@ -401,16 +417,15 @@ def tile_cubic_ocean_mode_step_h1_kernel(
         add_slow(0, 0)
         add_slow(0, 1)
         damp(nc.gpsimd, 0, 0, 2 * BANK)
-        store_y(0, 0, 2)
-        sort_amp(4)
+        store_y(0, 0)
         sort_amp(5)
+        force(0, 3)
+        add_slow(0, 3)
         force(0, 2)
         add_slow(0, 2)
         damp(nc.gpsimd, 0, 2 * BANK, 3 * BANK)
-        force(0, 3)
-        add_slow(0, 3)
         damp_from_bank(0, 3)
-        store_y(0, 2, 4)
+        store_y(0, 1)
         couple(2, 0)
         square(2, 0)
         couple(2, 1)
@@ -433,29 +448,31 @@ def tile_cubic_ocean_mode_step_h1_kernel(
         force(1, 0)
         add_slow(1, 0)
         force(1, 1)
+        add_slow(1, 1)
         round_y(0, 0, 1, 2)
 
         for s in range(1, TILES - 3):
             if live(s + 5):
                 transpose_amp(s + 5)
                 group_amp(s + 5)
-            if s > 1:
+            if s > 2:
                 round_y(s - 1, 0)
-            if s <= 3:
+            if s % 2 == 1:
                 group_h(s + 2, nc.vector.tensor_copy, 0, PAIR)
             if s == 1:
                 quantize_h(2)
-            if live(s - 3):
-                quantize_y(s - 3)
+            quantize_h(s + 2)
             if live(s + 5):
                 quantize_amp(s + 5)
-            add_slow(s, 1)
-            damp(nc.gpsimd, s, 0, 2 * BANK)
-            quantize_h(s + 2)
-            store_y(s, 0, 2)
+            else:
+                quantize_y(s - 3)
+            damp(nc.gpsimd, s, 0, HALF)
+            store_y(s, 0)
             for b in range(2):
                 couple(s + 3, b)
                 square(s + 3, b)
+            if s == 2:
+                round_y(s - 1, 0)
             round_y(s - 1, 1)
             cube(s + 3, 0)
             cube(s + 3, 1)
@@ -464,17 +481,19 @@ def tile_cubic_ocean_mode_step_h1_kernel(
             damp(nc.gpsimd, s, 2 * BANK, 3 * BANK)
             force(s, 3)
             add_slow(s, 3)
-            transpose_y(s - 1, 0)
-            group_y(s - 1, 0)
-            if s >= 3:
+            if s != 2:
+                transpose_y(s - 1, 0)
+                group_y(s - 1, 0)
                 group_h(s + 3, nc.scalar.copy, 0, PAIR)
             force(s + 1, 0)
             add_slow(s + 1, 0)
             force(s + 1, 1)
-            transpose_y(s - 1, 1)
-            group_y(s - 1, 1)
+            for half in (0, 1) if s == 2 else (1,):
+                transpose_y(s - 1, half)
+                group_y(s - 1, half)
             damp_from_bank(s, 3)
-            store_y(s, 2, 4)
+            store_y(s, 1)
+            add_slow(s + 1, 1)
 
         recip_banks[2] = ring_bank(hold=True)
         spread_recip(2, recip_banks[2])
@@ -484,9 +503,9 @@ def tile_cubic_ocean_mode_step_h1_kernel(
             round_y(s - 1, 1)
             if live(s + 2):
                 quantize_h(s + 2)
-            add_slow(s, 1)
-            damp(nc.gpsimd, s, 0, 2 * BANK)
             quantize_y(s - 3)
+            damp(nc.gpsimd, s, 0, HALF)
+            store_y(s, 0)
             force(s, 2)
             add_slow(s, 2)
             force(s, 3)
@@ -499,14 +518,12 @@ def tile_cubic_ocean_mode_step_h1_kernel(
             round_y(s, 0)
             damp_from_bank(s, 2)
             damp_from_bank(s, 3)
+            store_y(s, 1)
             add_slow(s + 1, 0)
-            store_y(s, 0, GN)
+            add_slow(s + 1, 1)
 
         round_y(last - 1, 1)
-        quantize_end(last - 3, 0, GN)
-        store_end(last - 3, 1, 0, GN)
-        add_slow(last, 1)
-        damp(nc.gpsimd, last, 0, 2 * BANK)
+        damp(nc.gpsimd, last, 0, HALF)
         force(last, 2)
         force(last, 3)
         y_pairs[last] = deep.tile([P, 2, 2, 2 * P, 2], BF16, align_bytes=64, name="y_pairs")
@@ -518,16 +535,18 @@ def tile_cubic_ocean_mode_step_h1_kernel(
             transpose_y(last - 1, half)
             group_y(last - 1, half)
         round_y(last, 0)
-        store_y(last, 0, 2)
+        store_y(last, 0)
         for g in (2, 3):
             damp_from_bank(last, g)
-        store_y(last, 2, 4)
+        store_y(last, 1)
         for half in (1, 0):
             transpose_y(last, half)
             group_y(last, half)
+        quantize_end(last - 3, 0, GN)
         quantize_end(last - 2, 0, GN)
+        store_end(last - 3, 2, 0, GN)
         quantize_end(last - 1, 0, GN)
-        store_end(last - 2, 2, 0, GN)
+        store_end(last - 1, 1, 0, GN)
         quantize_end(last, 2, GN)
         store_end(last, 1, 2, GN)
         quantize_end(last, 0, 2)

@@ -345,6 +345,18 @@ def tile_cubic_ocean_mode_step_h1_kernel(
             kept = slice((first - MERGED) * P, (first - MERGED + count) * P)
             nc.sync.dma_start(out=out_words[:, lo:hi, members], in_=end_codes[:, lo:hi, kept].bitcast(I32))
 
+        def warm_up(count, weights, activations):
+            for g in range(count):
+                nc.tensor.matmul_mx(
+                    out=recip_banks[GN - 1][:],
+                    lhsT=activations[0].bitcast(FP8X4),
+                    lhsT_scale=activations[1],
+                    rhs=weights[0][:, g % 2, : 2 * BANK].bitcast(FP4X4),
+                    rhs_scale=weights[1][:, g % 2, :BANK],
+                    start=True,
+                    stop=True,
+                )
+
         def live(i):
             return 0 <= i < TILES
 
@@ -374,8 +386,12 @@ def tile_cubic_ocean_mode_step_h1_kernel(
         for i in range(3, TILES):
             load_slow(i)
 
+        warm_codes = keep.tile([P, P], U32, align_bytes=64)
+        warm_scales = keep.tile([P, P], U8, align_bytes=64)
+        nc.vector.quantize_mx(out=warm_codes[:].bitcast(FP8X4), scales=warm_scales[:], in_=amp_sb[0][:, :BANK])
         deal_scales(0)
         transpose_amp(0, 1)
+        warm_up(2, (c_raw_words[0], c_raw_scales), (warm_codes[:], warm_scales[:]))
         group_amp(0)
         group_amp(1)
         deal_words(0)
@@ -405,6 +421,7 @@ def tile_cubic_ocean_mode_step_h1_kernel(
         group_h(1, nc.scalar.copy, VECTOR_MEMBERS, PAIR)
         quantize_amp(2)
         sort_amp(4)
+        warm_up(3, (c_raw_words[0], c_raw_scales), (a_codes[0][:, :P], a_scales[0][:, :P]))
         spread_recip(3, recip_banks[3])
         force(0, 0, (0,))
         force(0, 1, (0,))

@@ -53,8 +53,11 @@ def tile_cubic_ocean_mode_step_h1_kernel(
 
         c_raw_words = [keep.tile([P, GK, 2 * BANK], U8, align_bytes=64, name="c_raw_words%d" % f) for f in range(GF)]
         c_raw_scales = keep.tile([P, GK, F], U8, align_bytes=64)
-        c_words = [keep.tile([P, GK, 2 * BANK], U8, align_bytes=64, name="c_words%d" % f) for f in range(GF)]
-        c_scales = [keep.tile([P, GK, BANK], U8, align_bytes=64, name="c_scales%d" % f) for f in range(GF)]
+        c_words, c_scales = {}, {}
+        for f in range(GF):
+            for b in range(2):
+                c_words[f, b] = keep.tile([P, GK, BANK], U8, align_bytes=64, name="c_words%d%d" % (f, b))
+                c_scales[f, b] = keep.tile([P, GK, PAIR], U8, align_bytes=64, name="c_scales%d%d" % (f, b))
         b_words = [keep.tile([P, GF, N], U8, align_bytes=64, name="b_words%d" % h) for h in range(2)]
         b_scales = keep.tile([P, GF, N], U8, align_bytes=64)
         y_codes = keep.tile([P, MERGED, GN, P], U32, align_bytes=64)
@@ -97,16 +100,18 @@ def tile_cubic_ocean_mode_step_h1_kernel(
         def load_slow(i):
             nc.sync.dma_start(out=slow_sb[i][:], in_=slow[rows(i), :])
 
-        def deal_scales(f):
+        def deal_words(f, b):
+            slots = slice(2 * b, 2 * b + 2)
             nc.vector.tensor_copy(
-                out=c_scales[f][:].rearrange("p g (t c i) -> p c g t i", t=4, i=16),
-                in_=c_raw_scales[:, :, cols(f)].rearrange("p g (c i t) -> p c g t i", t=4, i=16),
+                out=c_words[f, b][:].bitcast(U16).rearrange("p g (t c i) -> p c g t i", t=2, i=8),
+                in_=c_raw_words[f][:].bitcast(U16).rearrange("p g (c i t) -> p c g t i", t=4, i=8)[:, :, :, slots, :],
             )
 
-        def deal_words(f):
+        def deal_scales(f, b):
+            slots = slice(2 * b, 2 * b + 2)
             nc.vector.tensor_copy(
-                out=c_words[f][:].bitcast(U16).rearrange("p g (t c i) -> p c g t i", t=4, i=8),
-                in_=c_raw_words[f][:].bitcast(U16).rearrange("p g (c i t) -> p c g t i", t=4, i=8),
+                out=c_scales[f, b][:].rearrange("p g (t c i) -> p c g t i", t=2, i=16),
+                in_=c_raw_scales[:, :, cols(f)].rearrange("p g (c i t) -> p c g t i", t=4, i=16)[:, :, :, slots, :],
             )
 
         def spread_recip(g, spread):
@@ -190,13 +195,12 @@ def tile_cubic_ocean_mode_step_h1_kernel(
             c, f = divmod(n, 2)
             u_banks[n, b] = ring_bank()
             for s in range(2):
-                t = 2 * b + s
                 for g in range(GK):
                     members = slice(g * PAIR, (g + 1) * PAIR)
                     nc.tensor.matmul_mx(
                         out=u_banks[n, b][:, s * PAIR : (s + 1) * PAIR],
-                        lhsT=c_words[f][:, g, 2 * t * P : 2 * (t + 1) * P].bitcast(FP4X4),
-                        lhsT_scale=c_scales[f][:, g, rows(t)],
+                        lhsT=c_words[f, b][:, g, s * PAIR : (s + 1) * PAIR].bitcast(FP4X4),
+                        lhsT_scale=c_scales[f, b][:, g, rows(s)],
                         rhs=a_codes[c][:, members].bitcast(FP8X4),
                         rhs_scale=a_scales[c][:, members],
                         start=(g == 0),
@@ -307,7 +311,10 @@ def tile_cubic_ocean_mode_step_h1_kernel(
                 nc.tensor.transpose(y_banks[i, half][:, s * P : (s + 1) * P], words[:, s * P : (s + 1) * P], ident[:])
 
         def group_y(i, half):
-            if i not in y_grouped:
+            if i == TILES - 3 and half == 0:
+                both = keep.tile([P, GN, 2, BANK], BF16, align_bytes=64)
+                y_grouped[i], y_grouped[i + 1], y_grouped["pair"] = both[:, :, 0, :], both[:, :, 1, :], both
+            elif i not in y_grouped:
                 y_grouped[i] = slab(i - 1, [P, GN, BANK], BF16)
             nc.scalar.copy(
                 out=y_grouped[i][:, 2 * half : 2 * half + 2, :].bitcast(F32).rearrange("p g (m u) -> p g m u", u=2),
@@ -338,6 +345,14 @@ def tile_cubic_ocean_mode_step_h1_kernel(
                     out=end_codes[:, g, rows(i - MERGED)].bitcast(FP8X4),
                     scales=end_scales[:, g, rows(i - MERGED)],
                     in_=y_grouped[i][:, g, :],
+                )
+
+        def quantize_pair():
+            for g in range(GN):
+                nc.vector.quantize_mx(
+                    out=end_codes[:, g, P : P + PAIR].bitcast(FP8X4),
+                    scales=end_scales[:, g, P : P + PAIR],
+                    in_=y_grouped["pair"][:, g, :, :].rearrange("p h c -> p (h c)"),
                 )
 
         def store_end(first, count, lo, hi):
@@ -389,18 +404,22 @@ def tile_cubic_ocean_mode_step_h1_kernel(
         warm_codes = keep.tile([P, P], U32, align_bytes=64)
         warm_scales = keep.tile([P, P], U8, align_bytes=64)
         nc.vector.quantize_mx(out=warm_codes[:].bitcast(FP8X4), scales=warm_scales[:], in_=amp_sb[0][:, :BANK])
-        deal_scales(0)
+        deal_scales(0, 0)
+        deal_scales(0, 1)
+        deal_scales(1, 0)
         transpose_amp(0, 1)
         warm_up(2, (c_raw_words[0], c_raw_scales), (warm_codes[:], warm_scales[:]))
         group_amp(0)
         group_amp(1)
-        deal_words(0)
+        deal_words(0, 0)
         quantize_amp(0)
         quantize_amp(1)
         sort_amp(2)
         sort_amp(3)
-        deal_scales(1)
-        deal_words(1)
+        deal_words(0, 1)
+        deal_scales(1, 1)
+        deal_words(1, 0)
+        deal_words(1, 1)
         nc.scalar.activation(out=denom[:], in_=drag_sb[:], func=ACT.Identity, bias=1.0)
         nc.vector.reciprocal(out=recip[:], in_=denom[:])
         for n in range(2):
@@ -456,7 +475,6 @@ def tile_cubic_ocean_mode_step_h1_kernel(
         square(3, 0)
         quantize_amp(4)
         quantize_amp(5)
-        round_y(0, 0, 0, 1)
         couple(3, 1)
         square(3, 1)
         group_h(2, nc.scalar.copy, 0, PAIR)
@@ -466,7 +484,7 @@ def tile_cubic_ocean_mode_step_h1_kernel(
         add_slow(1, 0)
         force(1, 1)
         add_slow(1, 1)
-        round_y(0, 0, 1, 2)
+        round_y(0, 0)
 
         for s in range(1, TILES - 3):
             if live(s + 5):
@@ -488,6 +506,9 @@ def tile_cubic_ocean_mode_step_h1_kernel(
             for b in range(2):
                 couple(s + 3, b)
                 square(s + 3, b)
+            if live(s - 2):
+                transpose_y(s - 2, 1)
+                group_y(s - 2, 1)
             if s == 2:
                 round_y(s - 1, 0)
             round_y(s - 1, 1)
@@ -505,15 +526,17 @@ def tile_cubic_ocean_mode_step_h1_kernel(
             force(s + 1, 0)
             add_slow(s + 1, 0)
             force(s + 1, 1)
-            for half in (0, 1) if s == 2 else (1,):
-                transpose_y(s - 1, half)
-                group_y(s - 1, half)
+            if s == 2:
+                transpose_y(s - 1, 0)
+                group_y(s - 1, 0)
             damp_from_bank(s, 3)
             store_y(s, 1)
             add_slow(s + 1, 1)
 
         recip_banks[2] = ring_bank(hold=True)
         spread_recip(2, recip_banks[2])
+        transpose_y(TILES - 5, 1)
+        group_y(TILES - 5, 1)
         last = TILES - 1
         round_y(TILES - 4, 0)
         for s in range(TILES - 3, last):
@@ -560,10 +583,9 @@ def tile_cubic_ocean_mode_step_h1_kernel(
             transpose_y(last, half)
             group_y(last, half)
         quantize_end(last - 3, 0, GN)
-        quantize_end(last - 2, 0, GN)
-        store_end(last - 3, 2, 0, GN)
-        quantize_end(last - 1, 0, GN)
-        store_end(last - 1, 1, 0, GN)
+        store_end(last - 3, 1, 0, GN)
+        quantize_pair()
+        store_end(last - 2, 2, 0, GN)
         quantize_end(last, 2, GN)
         store_end(last, 1, 2, GN)
         quantize_end(last, 0, 2)

@@ -25,7 +25,7 @@ HALF = N // 2
 GK = K // BANK
 GF = F // BANK
 GN = N // BANK
-MERGED = TILES - 4
+MERGED = TILES - 3
 RING = 7
 SLABS = 4
 VECTOR_MEMBERS = 160
@@ -350,8 +350,8 @@ def tile_cubic_ocean_mode_step_h1_kernel(
         def quantize_pair():
             for g in range(GN):
                 nc.vector.quantize_mx(
-                    out=end_codes[:, g, P : P + PAIR].bitcast(FP8X4),
-                    scales=end_scales[:, g, P : P + PAIR],
+                    out=end_codes[:, g, :PAIR].bitcast(FP8X4),
+                    scales=end_scales[:, g, :PAIR],
                     in_=y_grouped["pair"][:, g, :, :].rearrange("p h c -> p (h c)"),
                 )
 
@@ -543,11 +543,14 @@ def tile_cubic_ocean_mode_step_h1_kernel(
             round_y(s - 1, 1)
             if live(s + 2):
                 quantize_h(s + 2)
+            if not live(s + 2):
+                quantize_y(s - 2)
             quantize_y(s - 3)
             damp(nc.gpsimd, s, 0, HALF)
             store_y(s, 0)
             force(s, 2)
             add_slow(s, 2)
+            damp(nc.gpsimd, s, HALF, HALF + 192)
             force(s, 3)
             add_slow(s, 3)
             force(s + 1, 0)
@@ -556,7 +559,7 @@ def tile_cubic_ocean_mode_step_h1_kernel(
                 transpose_y(s - 1, half)
                 group_y(s - 1, half)
             round_y(s, 0)
-            damp_from_bank(s, 2)
+            damp_from_bank(s, 2, 192)
             damp_from_bank(s, 3)
             store_y(s, 1)
             add_slow(s + 1, 0)
@@ -582,8 +585,6 @@ def tile_cubic_ocean_mode_step_h1_kernel(
         for half in (1, 0):
             transpose_y(last, half)
             group_y(last, half)
-        quantize_end(last - 3, 0, GN)
-        store_end(last - 3, 1, 0, GN)
         quantize_pair()
         store_end(last - 2, 2, 0, GN)
         quantize_end(last, 2, GN)

@@ -168,6 +168,8 @@ def tile_cubic_ocean_mode_step_h1_kernel(
         def group_amp(n):
             if n >= TILES - 2:
                 a_grouped[n] = slab(n - 5, [P, 3 * BANK], BF16)
+            elif n == 5:
+                a_grouped[n] = slab(3, [P, 3 * BANK], BF16)
             else:
                 a_grouped[n] = work.tile([P, 3 * BANK], BF16, align_bytes=64, name="a_grouped")
             done = 0
@@ -226,8 +228,13 @@ def tile_cubic_ocean_mode_step_h1_kernel(
                     op1=ALU.mult,
                 )
 
+        def pool_copy(out, in_):
+            nc.gpsimd.tensor_scalar(out=out, in0=in_, scalar1=1.0, scalar2=0.0, op0=ALU.mult, op1=ALU.add)
+
         def group_h(n, copy, lo, hi):
-            if n not in h_grouped:
+            if n == 2:
+                h_grouped[n] = slab(3, [P, PAIR, 4], BF16)
+            elif n not in h_grouped:
                 h_grouped[n] = work.tile([P, PAIR, 4], BF16, align_bytes=64, name="h_grouped")
             copy(
                 out=h_grouped[n][:, lo:hi, :].rearrange("p (c i) t -> p c t i", i=4),
@@ -477,7 +484,7 @@ def tile_cubic_ocean_mode_step_h1_kernel(
         quantize_amp(5)
         couple(3, 1)
         square(3, 1)
-        group_h(2, nc.scalar.copy, 0, PAIR)
+        group_h(2, pool_copy, 0, PAIR)
         cube(3, 0)
         cube(3, 1)
         force(1, 0)

@@ -25,11 +25,10 @@ HALF = N // 2
 GK = K // BANK
 GF = F // BANK
 GN = N // BANK
-MERGED = TILES - 3
 RING = 7
-SLABS = 4
-VECTOR_MEMBERS = 160
-LOOP_MEMBERS = 96
+Y_BUFS = 5
+VI = 64
+GATES = ("small0", "small1", "small0", "wide0", "wide1")
 
 
 def tile_cubic_ocean_mode_step_h1_kernel(
@@ -60,10 +59,6 @@ def tile_cubic_ocean_mode_step_h1_kernel(
                 c_scales[f, b] = keep.tile([P, GK, PAIR], U8, align_bytes=64, name="c_scales%d%d" % (f, b))
         b_words = [keep.tile([P, GF, N], U8, align_bytes=64, name="b_words%d" % h) for h in range(2)]
         b_scales = keep.tile([P, GF, N], U8, align_bytes=64)
-        y_codes = keep.tile([P, MERGED, GN, P], U32, align_bytes=64)
-        y_scales = keep.tile([P, MERGED, GN, P], U8, align_bytes=64)
-        end_codes = keep.tile([P, GN, (TILES - MERGED) * P], U32, align_bytes=64)
-        end_scales = keep.tile([P, GN, (TILES - MERGED) * P], U8, align_bytes=64)
         amp_sb = [keep.tile([P, K], BF16, align_bytes=64, name="amp%d" % i) for i in range(TILES)]
         slow_sb = [keep.tile([P, N], BF16, align_bytes=64, name="slow%d" % i) for i in range(TILES)]
         cubic_sb = keep.tile([P, GF, 4], BF16)
@@ -100,9 +95,9 @@ def tile_cubic_ocean_mode_step_h1_kernel(
         def load_slow(i):
             nc.sync.dma_start(out=slow_sb[i][:], in_=slow[rows(i), :])
 
-        def deal_words(f, b):
+        def deal_words(f, b, copy=nc.vector.tensor_copy):
             slots = slice(2 * b, 2 * b + 2)
-            nc.vector.tensor_copy(
+            copy(
                 out=c_words[f, b][:].bitcast(U16).rearrange("p g (t c i) -> p c g t i", t=2, i=8),
                 in_=c_raw_words[f][:].bitcast(U16).rearrange("p g (c i t) -> p c g t i", t=4, i=8)[:, :, :, slots, :],
             )
@@ -118,29 +113,32 @@ def tile_cubic_ocean_mode_step_h1_kernel(
             for t in range(4):
                 nc.tensor.transpose(spread[:, t * P : (t + 1) * P], recip[:, g, t : t + 1].to_broadcast([P, P]), ident[:])
 
-        def keep_recip(g):
-            spread = ring_bank()
-            spread_recip(g, spread)
+        spreads = {}
+
+        def spread_rows(g):
+            spreads[g] = ring_bank()
+            spread_recip(g, spreads[g])
+
+        def keep_recip(g, width=BANK):
+            bank = spreads[g] if g in spreads else recip_banks[g]
             nc.scalar.copy(
-                out=recip_rows[:, cols(g)].rearrange("m (p t) -> m p t", t=4),
-                in_=spread[:].rearrange("m (t p) -> m p t", t=4),
+                out=recip_rows[:, g * BANK : g * BANK + width].rearrange("m (p t) -> m p t", t=4),
+                in_=bank[:].rearrange("m (t p) -> m p t", t=4)[:, : width // 4, :],
             )
 
         def slab(k, shape, dtype):
-            return keep.tile(shape, dtype, align_bytes=64, name="slab%d" % (k % SLABS))
+            return keep.tile(shape, dtype, align_bytes=64, name=k)
 
         a_sorted, a_banks, a_grouped, a_codes, a_scales = {}, {}, {}, {}, {}
         u_banks, squares, h_slots, h_grouped, h_codes, h_scales = {}, {}, {}, {}, {}, {}
-        e_banks, sums, ys, y_pairs, y_banks, y_grouped = {}, {}, {}, {}, {}, {}
+        e_banks, sums, ys, y_pairs, y_banks, y_grouped, y_codes = {}, {}, {}, {}, {}, {}, {}
 
-        def sort_amp(n):
-            a_sorted[n] = work.tile([P, GK, 2, P], F32, align_bytes=64, name="a_sorted")
-            for h, lo, hi, at in ((0, 0, 2, 0), (1, 0, 1, 2)) if n % 2 == 0 else ((0, 2, 3, 0), (1, 1, 3, 1)):
-                words = amp_sb[2 * (n // 2) + h][:].bitcast(F32)[:, 256 * lo : 256 * hi]
-                nc.scalar.copy(
-                    out=a_sorted[n][:, at : at + hi - lo, :, :].rearrange("m g u p -> m g p u"),
-                    in_=words.rearrange("m (g p u) -> m g p u", p=P, u=2),
-                )
+        def sort_amp(i, copy):
+            a_sorted[i] = work.tile([P, GK, 2, P], F32, align_bytes=64, name="a_sorted")
+            copy(
+                out=a_sorted[i][:].rearrange("m g u p -> m g p u"),
+                in_=amp_sb[i][:].bitcast(F32).rearrange("m (g p u) -> m g p u", p=P, u=2),
+            )
 
         def amp_pieces(n):
             return (((0, 0), (0, 1)), ((1, 0),)) if n % 2 == 0 else (((1, 1),), ((2, 0), (2, 1)))
@@ -159,29 +157,24 @@ def tile_cubic_ocean_mode_step_h1_kernel(
                                 for u in range(2):
                                     at = (2 * slot + u) * P
                                     source = (
-                                        a_sorted[n][:, (g + 2 * h, g - 2 + 2 * h)[n % 2], u, :]
-                                        if n in a_sorted
-                                        else words[:, 256 * g + u : 256 * (g + 1) : 2]
+                                        a_sorted[i][:, g, u, :] if i in a_sorted else words[:, 256 * g + u : 256 * (g + 1) : 2]
                                     )
                                     nc.tensor.transpose(a_banks[n, b][:, at : at + P], source, ident[:])
 
-        def group_amp(n):
-            if n >= TILES - 2:
-                a_grouped[n] = slab(n - 5, [P, 3 * BANK], BF16)
-            elif n == 5:
-                a_grouped[n] = slab(3, [P, 3 * BANK], BF16)
-            else:
-                a_grouped[n] = work.tile([P, 3 * BANK], BF16, align_bytes=64, name="a_grouped")
-            done = 0
-            for b, pieces in enumerate(amp_pieces(n)):
-                width = len(pieces)
-                nc.scalar.copy(
-                    out=a_grouped[n][:, done * BANK : (done + width) * BANK]
-                    .bitcast(F32)
-                    .rearrange("p (s m u) -> p s m u", u=2, m=P),
-                    in_=a_banks[n, b][:, : 256 * width].rearrange("p (s u m) -> p s m u", u=2, m=P),
-                )
-                done = done + width
+        def group_amp(n, b, gate=None):
+            if n not in a_grouped:
+                if gate is None:
+                    a_grouped[n] = work.tile([P, 3 * BANK], BF16, align_bytes=64, name="a_grouped")
+                else:
+                    a_grouped[n] = slab(gate, [P, 3 * BANK], BF16)
+            width = len(amp_pieces(n)[b])
+            done = 0 if b == 0 else 3 - width
+            nc.scalar.copy(
+                out=a_grouped[n][:, done * BANK : (done + width) * BANK]
+                .bitcast(F32)
+                .rearrange("p (s m u) -> p s m u", u=2, m=P),
+                in_=a_banks[n, b][:, : 256 * width].rearrange("p (s u m) -> p s m u", u=2, m=P),
+            )
 
         def quantize_amp(n):
             c = n // 2
@@ -231,23 +224,25 @@ def tile_cubic_ocean_mode_step_h1_kernel(
         def pool_copy(out, in_):
             nc.gpsimd.tensor_scalar(out=out, in0=in_, scalar1=1.0, scalar2=0.0, op0=ALU.mult, op1=ALU.add)
 
-        def group_h(n, copy, lo, hi):
-            if n == 2:
-                h_grouped[n] = slab(3, [P, PAIR, 4], BF16)
-            elif n not in h_grouped:
-                h_grouped[n] = work.tile([P, PAIR, 4], BF16, align_bytes=64, name="h_grouped")
+        def group_h(n, copy, lo=0, hi=PAIR, gate=None):
+            if n not in h_grouped:
+                if gate is None:
+                    h_grouped[n] = work.tile([P, PAIR, 4], BF16, align_bytes=64, name="h_grouped")
+                else:
+                    h_grouped[n] = slab(gate, [P, PAIR, 4], BF16)
             copy(
                 out=h_grouped[n][:, lo:hi, :].rearrange("p (c i) t -> p c t i", i=4),
                 in_=h_slots[n][:, :, lo:hi].rearrange("p t (c i) -> p c t i", i=4),
             )
 
-        def quantize_h(n):
-            h_codes[n] = deep.tile([P, PAIR], U32, align_bytes=64, name="h_codes", bufs=4)
-            h_scales[n] = deep.tile([P, PAIR], U8, align_bytes=64, name="h_scales", bufs=4)
+        def quantize_h(n, lo=0, hi=PAIR):
+            if n not in h_codes:
+                h_codes[n] = deep.tile([P, PAIR], U32, align_bytes=64, name="h_codes", bufs=4)
+                h_scales[n] = deep.tile([P, PAIR], U8, align_bytes=64, name="h_scales", bufs=4)
             nc.vector.quantize_mx(
-                out=h_codes[n][:].bitcast(FP8X4),
-                scales=h_scales[n][:],
-                in_=h_grouped[n][:].rearrange("p m t -> p (m t)"),
+                out=h_codes[n][:, lo:hi].bitcast(FP8X4),
+                scales=h_scales[n][:, lo:hi],
+                in_=h_grouped[n][:, lo:hi, :].rearrange("p m t -> p (m t)"),
             )
 
         def force(i, j, passes=range(GF)):
@@ -270,17 +265,18 @@ def tile_cubic_ocean_mode_step_h1_kernel(
         def add_slow(i, j):
             nc.vector.tensor_tensor(out=sums[i][:, cols(j)], in0=e_banks[i, j][:], in1=slow_sb[i][:, cols(j)], op=ALU.add)
 
-        def y_part(i, lo, hi):
-            half = lo // HALF
-            if (i, half) not in ys:
-                if half == 0 and i < TILES - 1:
-                    ys[i, half] = slab(i, [P, HALF], F32)
-                else:
-                    ys[i, half] = deep.tile([P, HALF], F32, align_bytes=64, name="y_half")
-            return ys[i, half][:, lo - half * HALF : hi - half * HALF]
+        def new_y(i, lo, hi, gate=None):
+            if gate is None:
+                ys[i, lo] = (deep.tile([P, hi - lo], F32, align_bytes=64, name="y_piece", bufs=Y_BUFS), hi)
+            else:
+                ys[i, lo] = (slab(gate, [P, hi - lo], F32), hi)
 
-        def damp(engine, i, lo, hi):
-            engine.tensor_tensor(out=y_part(i, lo, hi), in0=sums[i][:, lo:hi], in1=recip_rows[:, lo:hi], op=ALU.mult)
+        def y_part(i, lo, hi):
+            at = max(k[1] for k in ys if k[0] == i and k[1] <= lo)
+            return ys[i, at][0][:, lo - at : hi - at]
+
+        def damp_pool(i, lo, hi):
+            nc.gpsimd.tensor_tensor(out=y_part(i, lo, hi), in0=sums[i][:, lo:hi], in1=recip_rows[:, lo:hi], op=ALU.mult)
 
         def damp_from_bank(i, g, skip=0):
             lo, hi = g * BANK + skip, (g + 1) * BANK
@@ -291,90 +287,92 @@ def tile_cubic_ocean_mode_step_h1_kernel(
                 op=ALU.mult,
             )
 
+        def pairs_of(i):
+            if i not in y_pairs:
+                y_pairs[i] = deep.tile([P, 2, N // 4, 2], BF16, align_bytes=64, name="y_pairs")
+            return y_pairs[i]
+
         def damp_rounded(i, g):
             nc.vector.tensor_tensor(
-                out=y_pairs[i][:, g // 2, :, (g % 2) * P : (g % 2 + 1) * P, :],
+                out=pairs_of(i)[:, :, rows(g), :],
                 in0=sums[i][:, cols(g)].rearrange("m (p u e) -> m u p e", u=2, e=2),
                 in1=recip_banks[g][:].rearrange("m (u e p) -> m u p e", u=2, e=2),
                 op=ALU.mult,
             )
 
-        def store_y(i, half):
-            nc.sync.dma_start(out=out_0[rows(i), half * HALF : (half + 1) * HALF], in_=ys[i, half][:])
+        def store_y(i, lo):
+            nc.sync.dma_start(out=out_0[rows(i), lo : ys[i, lo][1]], in_=ys[i, lo][0][:])
 
-        def round_y(i, half, lo=0, hi=2):
-            if i not in y_pairs:
-                y_pairs[i] = deep.tile([P, 2, 2, 2 * P, 2], BF16, align_bytes=64, name="y_pairs")
+        def round_y(i, lo, hi):
             nc.scalar.activation(
-                out=y_pairs[i][:, half, :, lo * P : hi * P, :].rearrange("m u w e -> m w u e"),
-                in_=ys[i, half][:, lo * BANK : hi * BANK].rearrange("m (w u e) -> m w u e", u=2, e=2),
+                out=pairs_of(i)[:, :, lo // 4 : hi // 4, :].rearrange("m u w e -> m w u e"),
+                in_=y_part(i, lo, hi).rearrange("m (w u e) -> m w u e", u=2, e=2),
                 func=ACT.Copy,
+            )
+
+        def round_pool(i, lo, hi):
+            pool_copy(
+                out=pairs_of(i)[:, :, lo // 4 : hi // 4, :].rearrange("m u w e -> m w u e"),
+                in_=y_part(i, lo, hi).rearrange("m (w u e) -> m w u e", u=2, e=2),
+            )
+
+        def round_vector(i, lo, hi):
+            nc.vector.tensor_copy(
+                out=pairs_of(i)[:, :, lo // 4 : hi // 4, :].rearrange("m u w e -> m w u e"),
+                in_=y_part(i, lo, hi).rearrange("m (w u e) -> m w u e", u=2, e=2),
             )
 
         def transpose_y(i, half):
             y_banks[i, half] = ring_bank()
-            words = y_pairs[i][:, half, :, :, :].rearrange("m u w e -> m (u w e)").bitcast(F32)
-            for s in range(4):
-                nc.tensor.transpose(y_banks[i, half][:, s * P : (s + 1) * P], words[:, s * P : (s + 1) * P], ident[:])
+            words = y_pairs[i][:].rearrange("m u w e -> m u (w e)").bitcast(F32)
+            for u in range(2):
+                for g in range(2):
+                    nc.tensor.transpose(y_banks[i, half][:, rows(2 * u + g)], words[:, u, rows(2 * half + g)], ident[:])
 
-        def group_y(i, half):
-            if i == TILES - 3 and half == 0:
-                both = keep.tile([P, GN, 2, BANK], BF16, align_bytes=64)
-                y_grouped[i], y_grouped[i + 1], y_grouped["pair"] = both[:, :, 0, :], both[:, :, 1, :], both
-            elif i not in y_grouped:
-                y_grouped[i] = slab(i - 1, [P, GN, BANK], BF16)
-            nc.scalar.copy(
-                out=y_grouped[i][:, 2 * half : 2 * half + 2, :].bitcast(F32).rearrange("p g (m u) -> p g m u", u=2),
+        def group_y(i, half, copy=nc.scalar.copy):
+            c, h = divmod(i, 2)
+            if c not in y_grouped:
+                y_grouped[c] = slab("wide%d" % (c % 2), [P, GN, 2, BANK], BF16)
+            copy(
+                out=y_grouped[c][:, 2 * half : 2 * half + 2, h, :].bitcast(F32).rearrange("p g (m u) -> p g m u", u=2),
                 in_=y_banks[i, half][:].rearrange("p (u g m) -> p g m u", u=2, m=P),
             )
 
         out_words = out_1.rearrange("g p m t -> p g (m t)").bitcast(I32)
 
-        def store_scales(queue, plane, members):
+        y_scales = keep.tile([P, GN, M], U8, align_bytes=64)
+
+        def store_scales(queues, members):
             for q in range(4):
-                queue.dma_start(
+                queues[q % len(queues)].dma_start(
                     out=out_2[:, 4 * q : 4 * q + 4, members].rearrange("g r m -> r g m").bitcast(I32),
-                    in_=plane[32 * q : 32 * q + 4, :, :].bitcast(I32),
+                    in_=y_scales[32 * q : 32 * q + 4, :, members].bitcast(I32),
                 )
 
-        def quantize_y(i):
-            nc.vector.quantize_mx(
-                out=y_codes[:, i, :, :].rearrange("p g m -> p (g m)").bitcast(FP8X4),
-                scales=y_scales[:, i, :, :].rearrange("p g m -> p (g m)"),
-                in_=y_grouped[i][:].rearrange("p g c -> p (g c)"),
+        def quantize_y(c, groups=range(GN), lo=0, hi=2):
+            if c not in y_codes:
+                y_codes[c] = work.tile([P, GN, PAIR], U32, align_bytes=64, name="y_codes")
+            for g in groups:
+                nc.vector.quantize_mx(
+                    out=y_codes[c][:, g, lo * P : hi * P].bitcast(FP8X4),
+                    scales=y_scales[:, g, (2 * c + lo) * P : (2 * c + hi) * P],
+                    in_=y_grouped[c][:, g, lo:hi, :].rearrange("p h c -> p (h c)"),
+                )
+
+        def store_codes(c, first=0, last=GN, lo=0, hi=2):
+            members = slice((2 * c + lo) * P, (2 * c + hi) * P)
+            nc.sync.dma_start(
+                out=out_words[:, first:last, members], in_=y_codes[c][:, first:last, lo * P : hi * P].bitcast(I32)
             )
-            nc.sync.dma_start(out=out_words[:, :, rows(i)], in_=y_codes[:, i, :, :].bitcast(I32))
-            store_scales(nc.sync, y_scales[:, i, :, :], rows(i))
 
-        def quantize_end(i, lo, hi):
-            for g in range(lo, hi):
-                nc.vector.quantize_mx(
-                    out=end_codes[:, g, rows(i - MERGED)].bitcast(FP8X4),
-                    scales=end_scales[:, g, rows(i - MERGED)],
-                    in_=y_grouped[i][:, g, :],
-                )
-
-        def quantize_pair():
-            for g in range(GN):
-                nc.vector.quantize_mx(
-                    out=end_codes[:, g, :PAIR].bitcast(FP8X4),
-                    scales=end_scales[:, g, :PAIR],
-                    in_=y_grouped["pair"][:, g, :, :].rearrange("p h c -> p (h c)"),
-                )
-
-        def store_end(first, count, lo, hi):
-            members = slice(first * P, (first + count) * P)
-            kept = slice((first - MERGED) * P, (first - MERGED + count) * P)
-            nc.sync.dma_start(out=out_words[:, lo:hi, members], in_=end_codes[:, lo:hi, kept].bitcast(I32))
-
-        def warm_up(count, weights, activations):
+        def warm_up(count, bank, activations):
             for g in range(count):
                 nc.tensor.matmul_mx(
-                    out=recip_banks[GN - 1][:],
+                    out=bank[:],
                     lhsT=activations[0].bitcast(FP8X4),
                     lhsT_scale=activations[1],
-                    rhs=weights[0][:, g % 2, : 2 * BANK].bitcast(FP4X4),
-                    rhs_scale=weights[1][:, g % 2, :BANK],
+                    rhs=c_raw_words[0][:, g % 2, :].bitcast(FP4X4),
+                    rhs_scale=c_raw_scales[:, g % 2, :BANK],
                     start=True,
                     stop=True,
                 )
@@ -382,10 +380,14 @@ def tile_cubic_ocean_mode_step_h1_kernel(
         def live(i):
             return 0 <= i < TILES
 
+        warm_codes = keep.tile([P, P], U32, align_bytes=64)
+        warm_scales = keep.tile([P, P], U8, align_bytes=64)
+
         nc.vector.memset(c_raw_scales[:].bitcast(I32), 0)
         nc.vector.memset(b_scales[:].bitcast(I32), 0)
         make_identity(nc, ident[:])
 
+        nc.sync.dma_start(out=drag_sb[:], in_=drag.rearrange("(g p t) -> p g t", p=P, t=4))
         load_amp(0)
         load_amp(1)
         load_scales(c_raw_scales, coup_scales)
@@ -394,7 +396,6 @@ def tile_cubic_ocean_mode_step_h1_kernel(
         load_amp(3)
         load_words(c_raw_words, coup_words, 1)
         nc.sync.dma_start(out=cubic_sb[:], in_=cubic.rearrange("(g p t) -> p g t", p=P, t=4))
-        nc.sync.dma_start(out=drag_sb[:], in_=drag.rearrange("(g p t) -> p g t", p=P, t=4))
         load_scales(b_scales, forc_scales)
         load_words(b_words, forc_words, 0)
         load_slow(0)
@@ -408,194 +409,240 @@ def tile_cubic_ocean_mode_step_h1_kernel(
         for i in range(3, TILES):
             load_slow(i)
 
-        warm_codes = keep.tile([P, P], U32, align_bytes=64)
-        warm_scales = keep.tile([P, P], U8, align_bytes=64)
+        nc.vector.tensor_scalar(out=denom[:], in0=drag_sb[:], scalar1=1.0, scalar2=None, op0=ALU.add)
+        nc.vector.reciprocal(out=recip[:], in_=denom[:])
+        spread_rows(0)
+        keep_recip(0)
+        sort_amp(0, nc.vector.tensor_copy)
         nc.vector.quantize_mx(out=warm_codes[:].bitcast(FP8X4), scales=warm_scales[:], in_=amp_sb[0][:, :BANK])
+        sort_amp(1, nc.vector.tensor_copy)
         deal_scales(0, 0)
         deal_scales(0, 1)
-        deal_scales(1, 0)
         transpose_amp(0, 1)
-        warm_up(2, (c_raw_words[0], c_raw_scales), (warm_codes[:], warm_scales[:]))
-        group_amp(0)
-        group_amp(1)
+        spread_recip(3, recip_banks[3])
+        warm_up(2, ring_bank(), (warm_codes[:], warm_scales[:]))
+        group_amp(0, 1)
+        group_amp(0, 0)
+        group_amp(1, 0)
+        group_amp(1, 1)
         deal_words(0, 0)
         quantize_amp(0)
         quantize_amp(1)
-        sort_amp(2)
-        sort_amp(3)
+        sort_amp(2, nc.scalar.copy)
+        sort_amp(3, nc.scalar.copy)
         deal_words(0, 1)
-        deal_scales(1, 1)
+        deal_scales(1, 0)
         deal_words(1, 0)
+        deal_scales(1, 1)
         deal_words(1, 1)
-        nc.scalar.activation(out=denom[:], in_=drag_sb[:], func=ACT.Identity, bias=1.0)
-        nc.vector.reciprocal(out=recip[:], in_=denom[:])
-        for n in range(2):
-            for b in range(2):
-                couple(n, b)
-                square(n, b)
+        for b in range(2):
+            couple(0, b)
+            square(0, b)
+        transpose_amp(2, 3)
+        spread_rows(1)
+        group_amp(2, 1)
+        group_amp(2, 0)
         cube(0, 0)
         cube(0, 1)
+        couple(1, 0)
+        group_amp(3, 0)
+        group_amp(3, 1)
+        square(1, 0)
+        couple(1, 1)
+        square(1, 1)
+        keep_recip(1)
+        quantize_amp(2)
         group_h(0, nc.vector.tensor_copy, 0, PAIR)
+        quantize_amp(3)
         cube(1, 0)
         quantize_h(0)
         cube(1, 1)
-        transpose_amp(2)
-        group_amp(2)
-        transpose_amp(3)
-        group_amp(3)
-        group_h(1, nc.vector.tensor_copy, 0, VECTOR_MEMBERS)
-        group_h(1, nc.scalar.copy, VECTOR_MEMBERS, PAIR)
-        quantize_amp(2)
-        sort_amp(4)
-        warm_up(3, (c_raw_words[0], c_raw_scales), (a_codes[0][:, :P], a_scales[0][:, :P]))
-        spread_recip(3, recip_banks[3])
+        couple(2, 0)
+        couple(2, 1)
+        group_h(1, nc.vector.tensor_copy, 0, P)
+        square(2, 0)
+        group_h(1, nc.scalar.copy, P, PAIR)
+        square(2, 1)
         force(0, 0, (0,))
         force(0, 1, (0,))
-        quantize_h(1)
-        quantize_amp(3)
-        for g in range(3):
-            keep_recip(g)
+        spread_rows(2)
+        keep_recip(2)
+        sort_amp(4, nc.scalar.copy)
+        sort_amp(5, nc.scalar.copy)
+        quantize_h(1, 0, P)
+        cube(2, 0)
+        quantize_h(1, P, PAIR)
         force(0, 0, (1,))
         force(0, 1, (1,))
         add_slow(0, 0)
         add_slow(0, 1)
-        damp(nc.gpsimd, 0, 0, 2 * BANK)
+        new_y(0, 0, HALF)
+        damp_pool(0, 0, HALF)
         store_y(0, 0)
-        sort_amp(5)
+        cube(2, 1)
         force(0, 3)
         add_slow(0, 3)
         force(0, 2)
         add_slow(0, 2)
-        damp(nc.gpsimd, 0, 2 * BANK, 3 * BANK)
+        for b in range(2):
+            couple(3, b)
+            square(3, b)
+        group_h(2, pool_copy)
+        new_y(0, 3 * BANK, N)
         damp_from_bank(0, 3)
-        store_y(0, 1)
-        couple(2, 0)
-        square(2, 0)
-        couple(2, 1)
-        square(2, 1)
-        cube(2, 0)
-        cube(2, 1)
-        for n in (4, 5):
-            transpose_amp(n)
-            group_amp(n)
-        couple(3, 0)
-        square(3, 0)
-        quantize_amp(4)
-        quantize_amp(5)
-        couple(3, 1)
-        square(3, 1)
-        group_h(2, pool_copy, 0, PAIR)
+        store_y(0, 3 * BANK)
+        transpose_amp(4, 5)
+        group_amp(4, 1)
+        group_amp(4, 0)
+        group_amp(5, 0)
+        group_amp(5, 1)
         cube(3, 0)
         cube(3, 1)
         force(1, 0)
         add_slow(1, 0)
-        force(1, 1)
-        add_slow(1, 1)
-        round_y(0, 0)
+        quantize_amp(4)
+        quantize_amp(5)
+        group_h(3, nc.vector.tensor_copy, 0, PAIR, GATES[0])
+        quantize_h(2)
+        quantize_h(3)
+        round_y(0, 0, HALF)
+        round_y(0, 3 * BANK, N)
 
         for s in range(1, TILES - 3):
-            if live(s + 5):
-                transpose_amp(s + 5)
-                group_amp(s + 5)
-            if s > 2:
-                round_y(s - 1, 0)
-            if s % 2 == 1:
-                group_h(s + 2, nc.vector.tensor_copy, 0, PAIR)
-            if s == 1:
-                quantize_h(2)
-            quantize_h(s + 2)
-            if live(s + 5):
-                quantize_amp(s + 5)
-            else:
-                quantize_y(s - 3)
-            damp(nc.gpsimd, s, 0, HALF)
+            new_y(s - 1, HALF, 3 * BANK, GATES[s - 1])
+            damp_pool(s - 1, HALF, 3 * BANK)
+            store_y(s - 1, HALF)
+            for j in (0, 1, 3, 2):
+                if (s, j) != (1, 0):
+                    force(s, j)
+                    add_slow(s, j)
+            new_y(s, 0, HALF)
+            damp_pool(s, 0, HALF)
             store_y(s, 0)
+            new_y(s, 3 * BANK, N)
+            damp_from_bank(s, 3)
+            store_y(s, 3 * BANK)
             for b in range(2):
                 couple(s + 3, b)
                 square(s + 3, b)
+                cube(s + 3, b)
+            if s == 4:
+                round_y(s - 1, HALF, 3 * BANK)
+            if live(s + 5):
+                transpose_amp(s + 5)
             if live(s - 2):
                 transpose_y(s - 2, 1)
+            transpose_y(s - 1, 0)
+            if s == 4:
+                force(5, 0)
+                force(5, 1)
+                transpose_y(s - 1, 1)
+            if live(s + 5):
+                for b in range(2):
+                    group_amp(s + 5, b, GATES[s] if s == 1 else None)
+            if live(s - 2):
                 group_y(s - 2, 1)
-            if s == 2:
-                round_y(s - 1, 0)
-            round_y(s - 1, 1)
-            cube(s + 3, 0)
-            cube(s + 3, 1)
-            force(s, 2)
-            add_slow(s, 2)
-            damp(nc.gpsimd, s, 2 * BANK, 3 * BANK)
-            force(s, 3)
-            add_slow(s, 3)
-            if s != 2:
-                transpose_y(s - 1, 0)
-                group_y(s - 1, 0)
-                group_h(s + 3, nc.scalar.copy, 0, PAIR)
-            force(s + 1, 0)
-            add_slow(s + 1, 0)
-            force(s + 1, 1)
-            if s == 2:
-                transpose_y(s - 1, 0)
-                group_y(s - 1, 0)
-            damp_from_bank(s, 3)
-            store_y(s, 1)
-            add_slow(s + 1, 1)
+            group_y(s - 1, 0)
+            if s == 4:
+                group_y(s - 1, 1)
+            if s % 2 == 0:
+                quantize_h(s + 2)
+                group_h(s + 3, nc.vector.tensor_copy, 0, PAIR, GATES[s] if s == 2 else None)
+            elif VI > 0:
+                group_h(s + 3, nc.vector.tensor_copy, 0, VI)
+            if live(s + 5):
+                quantize_amp(s + 5)
+            if s == 4:
+                quantize_y(1, (0,))
+            if s % 2 == 0:
+                quantize_h(s + 3)
+            if s == 3:
+                quantize_y(0)
+                store_codes(0)
+            if s == 4:
+                quantize_y(1, (1, 2, 3))
+                store_codes(1)
+                store_scales([nc.sync], slice(0, 4 * P))
+            if s != 4:
+                round_y(s - 1, HALF, 3 * BANK)
+            round_y(s, 0, HALF)
+            round_y(s, 3 * BANK, N)
+            if s % 2 == 1:
+                group_h(s + 3, nc.scalar.copy, VI, PAIR)
 
+        new_y(4, HALF, 3 * BANK, GATES[4])
+        damp_pool(4, HALF, 3 * BANK)
+        store_y(4, HALF)
+        add_slow(5, 0)
+        add_slow(5, 1)
+        for j in (3, 2):
+            force(5, j)
+            add_slow(5, j)
+        transpose_y(4, 0)
         recip_banks[2] = ring_bank(hold=True)
         spread_recip(2, recip_banks[2])
-        transpose_y(TILES - 5, 1)
-        group_y(TILES - 5, 1)
+        group_y(4, 0)
+        round_y(4, HALF, 3 * BANK)
+        new_y(5, 0, HALF)
+        damp_pool(5, 0, HALF)
+        store_y(5, 0)
+        new_y(5, HALF, N)
+        damp_from_bank(5, 3)
+        damp_pool(5, HALF, 3 * BANK)
+        store_y(5, HALF)
+        for j in range(GN):
+            force(6, j)
+            add_slow(6, j)
+        transpose_y(4, 1)
+        round_y(5, 3 * BANK, N)
+        group_y(4, 1)
+        round_y(5, 0, HALF)
+        round_y(5, HALF, 3 * BANK)
+        recip_banks[1] = ring_bank(hold=True)
+        spread_recip(1, recip_banks[1])
+        new_y(6, 0, HALF)
+        damp_pool(6, 0, HALF)
+        new_y(6, HALF, N)
+        damp_from_bank(6, 2)
+        damp_from_bank(6, 3)
+        store_y(6, HALF)
+        store_y(6, 0)
         last = TILES - 1
-        round_y(TILES - 4, 0)
-        for s in range(TILES - 3, last):
-            round_y(s - 1, 1)
-            if live(s + 2):
-                quantize_h(s + 2)
-            if not live(s + 2):
-                quantize_y(s - 2)
-            quantize_y(s - 3)
-            damp(nc.gpsimd, s, 0, HALF)
-            store_y(s, 0)
-            force(s, 2)
-            add_slow(s, 2)
-            damp(nc.gpsimd, s, HALF, HALF + 192)
-            force(s, 3)
-            add_slow(s, 3)
-            force(s + 1, 0)
-            force(s + 1, 1)
-            for half in range(2):
-                transpose_y(s - 1, half)
-                group_y(s - 1, half)
-            round_y(s, 0)
-            damp_from_bank(s, 2, 192)
-            damp_from_bank(s, 3)
-            store_y(s, 1)
-            add_slow(s + 1, 0)
-            add_slow(s + 1, 1)
-
-        round_y(last - 1, 1)
-        damp(nc.gpsimd, last, 0, HALF)
-        force(last, 2)
-        force(last, 3)
-        y_pairs[last] = deep.tile([P, 2, 2, 2 * P, 2], BF16, align_bytes=64, name="y_pairs")
-        for g in (2, 3):
-            add_slow(last, g)
-        for g in (2, 3):
-            damp_rounded(last, g)
-        for half in range(2):
-            transpose_y(last - 1, half)
-            group_y(last - 1, half)
-        round_y(last, 0)
+        for j in (0, 1, 2):
+            force(7, j)
+            add_slow(7, j)
+        transpose_y(5, 0)
+        group_y(5, 0)
+        force(7, 3)
+        add_slow(7, 3)
+        round_y(6, HALF, N)
+        transpose_y(5, 1)
+        group_y(5, 1)
+        round_y(6, 0, HALF)
+        new_y(last, 0, HALF)
+        damp_pool(last, 0, BANK)
+        round_pool(last, 0, BANK)
+        damp_from_bank(last, 1)
         store_y(last, 0)
-        for g in (2, 3):
-            damp_from_bank(last, g)
-        store_y(last, 1)
-        for half in (1, 0):
-            transpose_y(last, half)
-            group_y(last, half)
-        quantize_pair()
-        store_end(last - 2, 2, 0, GN)
-        quantize_end(last, 2, GN)
-        store_end(last, 1, 2, GN)
-        quantize_end(last, 0, 2)
-        store_end(last, 1, 0, 2)
-        store_scales(nc.scalar, end_scales, slice(MERGED * P, M))
+        new_y(last, HALF, N)
+        damp_from_bank(last, 2)
+        damp_from_bank(last, 3)
+        store_y(last, HALF)
+        round_vector(last, BANK, HALF)
+        round_vector(last, HALF, N)
+        transpose_y(6, 1)
+        group_y(6, 1)
+        transpose_y(6, 0)
+        group_y(6, 0)
+        quantize_y(2)
+        store_codes(2)
+        transpose_y(last, 0)
+        group_y(last, 0)
+        transpose_y(last, 1)
+        group_y(last, 1)
+        quantize_y(3, range(GN), 0, 1)
+        quantize_y(3, (0, 1), 1, 2)
+        store_codes(3, 0, 2)
+        quantize_y(3, (2, 3), 1, 2)
+        store_codes(3, 2, 4)
+        store_scales([nc.scalar, nc.sync], slice(4 * P, M))

@@ -27,8 +27,12 @@ GF = F // BANK
 GN = N // BANK
 RING = 7
 Y_BUFS = 5
-VI = 64
-GATES = ("small0", "small1", "small0", "wide0", "wide1")
+VI = 96
+GATES = ("small0", "small1", "small0", "wide0", "small1")
+G2 = 160
+V7 = 128
+FIRST_WHOLE = 0
+WARM_ON_SCALES = False
 
 
 def tile_cubic_ocean_mode_step_h1_kernel(
@@ -59,7 +63,7 @@ def tile_cubic_ocean_mode_step_h1_kernel(
                 c_scales[f, b] = keep.tile([P, GK, PAIR], U8, align_bytes=64, name="c_scales%d%d" % (f, b))
         b_words = [keep.tile([P, GF, N], U8, align_bytes=64, name="b_words%d" % h) for h in range(2)]
         b_scales = keep.tile([P, GF, N], U8, align_bytes=64)
-        amp_sb = [keep.tile([P, K], BF16, align_bytes=64, name="amp%d" % i) for i in range(TILES)]
+        amp_sb = {i: keep.tile([P, K], BF16, align_bytes=64, name="amp%d" % i) for i in range(FIRST_WHOLE, TILES)}
         slow_sb = [keep.tile([P, N], BF16, align_bytes=64, name="slow%d" % i) for i in range(TILES)]
         cubic_sb = keep.tile([P, GF, 4], BF16)
         drag_sb = keep.tile([P, GN, 4], BF16)
@@ -138,6 +142,41 @@ def tile_cubic_ocean_mode_step_h1_kernel(
             copy(
                 out=a_sorted[i][:].rearrange("m g u p -> m g p u"),
                 in_=amp_sb[i][:].bitcast(F32).rearrange("m (g p u) -> m g p u", p=P, u=2),
+            )
+
+        first_amp, first_sorted, first_banks, first_grouped = {}, {}, {}, {}
+
+        def load_first(g):
+            first_amp[g] = keep.tile([P, 2, BANK], BF16, align_bytes=64, name="first_amp%d" % g)
+            nc.sync.dma_start(out=first_amp[g][:], in_=amp[:PAIR, cols(g)].rearrange("(h m) k -> m h k", h=2))
+
+        def sort_first(g):
+            first_sorted[g] = deep.tile([P, 2, 2, P], F32, align_bytes=64, name="first_sorted")
+            nc.vector.tensor_copy(
+                out=first_sorted[g][:].rearrange("m h u p -> m h p u"),
+                in_=first_amp[g][:].bitcast(F32).rearrange("m h (p u) -> m h p u", u=2),
+            )
+
+        def transpose_first(g):
+            first_banks[g] = ring_bank()
+            for h in range(2):
+                for u in range(2):
+                    nc.tensor.transpose(first_banks[g][:, rows(2 * h + u)], first_sorted[g][:, h, u, :], ident[:])
+
+        def group_first(g):
+            first_grouped[g] = deep.tile([P, 2 * BANK], BF16, align_bytes=64, name="first_grouped")
+            nc.scalar.copy(
+                out=first_grouped[g][:].bitcast(F32).rearrange("p (h m u) -> p h m u", u=2, m=P),
+                in_=first_banks[g][:].rearrange("p (h u m) -> p h m u", u=2, m=P),
+            )
+
+        def quantize_first(g):
+            if g == 0:
+                a_codes[0] = deep.tile([P, GK * PAIR], U32, align_bytes=64, name="a_codes")
+                a_scales[0] = deep.tile([P, GK * PAIR], U8, align_bytes=64, name="a_scales")
+            part = slice(g * PAIR, (g + 1) * PAIR)
+            nc.vector.quantize_mx(
+                out=a_codes[0][:, part].bitcast(FP8X4), scales=a_scales[0][:, part], in_=first_grouped[g][:]
             )
 
         def amp_pieces(n):
@@ -371,7 +410,7 @@ def tile_cubic_ocean_mode_step_h1_kernel(
                     out=bank[:],
                     lhsT=activations[0].bitcast(FP8X4),
                     lhsT_scale=activations[1],
-                    rhs=c_raw_words[0][:, g % 2, :].bitcast(FP4X4),
+                    rhs=(c_raw_scales if WARM_ON_SCALES else c_raw_words[0])[:, g % 2, :].bitcast(FP4X4),
                     rhs_scale=c_raw_scales[:, g % 2, :BANK],
                     start=True,
                     stop=True,
@@ -487,7 +526,9 @@ def tile_cubic_ocean_mode_step_h1_kernel(
         for b in range(2):
             couple(3, b)
             square(3, b)
-        group_h(2, pool_copy)
+            if b == 0:
+                group_h(2, nc.scalar.copy, G2, PAIR)
+        group_h(2, pool_copy, 0, G2)
         new_y(0, 3 * BANK, N)
         damp_from_bank(0, 3)
         store_y(0, 3 * BANK)
@@ -499,12 +540,13 @@ def tile_cubic_ocean_mode_step_h1_kernel(
         cube(3, 0)
         cube(3, 1)
         force(1, 0)
-        add_slow(1, 0)
         quantize_amp(4)
+        group_h(3, nc.vector.tensor_copy, 0, P, GATES[0])
+        group_h(3, nc.scalar.copy, P, PAIR)
         quantize_amp(5)
-        group_h(3, nc.vector.tensor_copy, 0, PAIR, GATES[0])
         quantize_h(2)
         quantize_h(3)
+        add_slow(1, 0)
         round_y(0, 0, HALF)
         round_y(0, 3 * BANK, N)
 
@@ -547,22 +589,24 @@ def tile_cubic_ocean_mode_step_h1_kernel(
                 group_y(s - 1, 1)
             if s % 2 == 0:
                 quantize_h(s + 2)
-                group_h(s + 3, nc.vector.tensor_copy, 0, PAIR, GATES[s] if s == 2 else None)
-            elif VI > 0:
-                group_h(s + 3, nc.vector.tensor_copy, 0, VI)
+                group_h(s + 3, nc.vector.tensor_copy, 0, PAIR if s == 2 else V7, GATES[s])
+                if s == 4:
+                    group_h(s + 3, nc.scalar.copy, V7, PAIR)
             if live(s + 5):
                 quantize_amp(s + 5)
+            if s == 3:
+                quantize_y(0, (0,))
+            if s % 2 == 1:
+                group_h(s + 3, nc.vector.tensor_copy, 0, VI)
             if s == 4:
-                quantize_y(1, (0,))
+                quantize_y(1)
+                store_codes(1)
+                store_scales([nc.sync], slice(0, 4 * P))
             if s % 2 == 0:
                 quantize_h(s + 3)
             if s == 3:
-                quantize_y(0)
+                quantize_y(0, (1, 2, 3))
                 store_codes(0)
-            if s == 4:
-                quantize_y(1, (1, 2, 3))
-                store_codes(1)
-                store_scales([nc.sync], slice(0, 4 * P))
             if s != 4:
                 round_y(s - 1, HALF, 3 * BANK)
             round_y(s, 0, HALF)
@@ -578,6 +622,8 @@ def tile_cubic_ocean_mode_step_h1_kernel(
         for j in (3, 2):
             force(5, j)
             add_slow(5, j)
+        force(6, 0)
+        force(6, 1)
         transpose_y(4, 0)
         recip_banks[2] = ring_bank(hold=True)
         spread_recip(2, recip_banks[2])
@@ -591,7 +637,8 @@ def tile_cubic_ocean_mode_step_h1_kernel(
         damp_pool(5, HALF, 3 * BANK)
         store_y(5, HALF)
         for j in range(GN):
-            force(6, j)
+            if j > 1:
+                force(6, j)
             add_slow(6, j)
         transpose_y(4, 1)
         round_y(5, 3 * BANK, N)
@@ -634,8 +681,10 @@ def tile_cubic_ocean_mode_step_h1_kernel(
         group_y(6, 1)
         transpose_y(6, 0)
         group_y(6, 0)
-        quantize_y(2)
-        store_codes(2)
+        quantize_y(2, (0, 1))
+        store_codes(2, 0, 2)
+        quantize_y(2, (2, 3))
+        store_codes(2, 2, 4)
         transpose_y(last, 0)
         group_y(last, 0)
         transpose_y(last, 1)

@@ -27,12 +27,14 @@ GF = F // BANK
 GN = N // BANK
 RING = 7
 Y_BUFS = 5
-VI = 96
+VI = {1: 160, 3: 128}
+V3 = 128
 GATES = ("small0", "small1", "small0", "wide0", "small1")
 G2 = 160
 V7 = 128
 FIRST_WHOLE = 0
 WARM_ON_SCALES = False
+PLAIN = ()
 
 
 def tile_cubic_ocean_mode_step_h1_kernel(
@@ -55,7 +57,7 @@ def tile_cubic_ocean_mode_step_h1_kernel(
             return psum.tile([P, BANK], F32, name="bank%d" % b)
 
         c_raw_words = [keep.tile([P, GK, 2 * BANK], U8, align_bytes=64, name="c_raw_words%d" % f) for f in range(GF)]
-        c_raw_scales = keep.tile([P, GK, F], U8, align_bytes=64)
+        c_raw_scales = [keep.tile([P, GK, BANK], U8, align_bytes=64, name="c_raw_scales%d" % f) for f in range(GF)]
         c_words, c_scales = {}, {}
         for f in range(GF):
             for b in range(2):
@@ -80,7 +82,7 @@ def tile_cubic_ocean_mode_step_h1_kernel(
             return slice(g * BANK, (g + 1) * BANK)
 
         def load_scales(plane, scales):
-            for q in range(4):
+            for q in (0, 2, 1, 3):
                 nc.sync.dma_start(
                     out=plane[32 * q : 32 * q + 4, :, :].bitcast(I32),
                     in_=scales[:, 4 * q : 4 * q + 4, :].rearrange("g r n -> r g n").bitcast(I32),
@@ -110,7 +112,7 @@ def tile_cubic_ocean_mode_step_h1_kernel(
             slots = slice(2 * b, 2 * b + 2)
             nc.vector.tensor_copy(
                 out=c_scales[f, b][:].rearrange("p g (t c i) -> p c g t i", t=2, i=16),
-                in_=c_raw_scales[:, :, cols(f)].rearrange("p g (c i t) -> p c g t i", t=4, i=16)[:, :, :, slots, :],
+                in_=c_raw_scales[f][:].rearrange("p g (c i t) -> p c g t i", t=4, i=16)[:, :, :, slots, :],
             )
 
         def spread_recip(g, spread):
@@ -343,6 +345,10 @@ def tile_cubic_ocean_mode_step_h1_kernel(
             nc.sync.dma_start(out=out_0[rows(i), lo : ys[i, lo][1]], in_=ys[i, lo][0][:])
 
         def round_y(i, lo, hi):
+            if i in PLAIN:
+                flat = pairs_of(i)[:].rearrange("m u w e -> m (u w e)")
+                nc.scalar.activation(out=flat[:, lo:hi], in_=y_part(i, lo, hi), func=ACT.Copy)
+                return
             nc.scalar.activation(
                 out=pairs_of(i)[:, :, lo // 4 : hi // 4, :].rearrange("m u w e -> m w u e"),
                 in_=y_part(i, lo, hi).rearrange("m (w u e) -> m w u e", u=2, e=2),
@@ -366,7 +372,11 @@ def tile_cubic_ocean_mode_step_h1_kernel(
             words = y_pairs[i][:].rearrange("m u w e -> m u (w e)").bitcast(F32)
             for u in range(2):
                 for g in range(2):
-                    nc.tensor.transpose(y_banks[i, half][:, rows(2 * u + g)], words[:, u, rows(2 * half + g)], ident[:])
+                    source = words[:, u, rows(2 * half + g)]
+                    if i in PLAIN:
+                        at = PAIR * (2 * half + g)
+                        source = words.rearrange("m u w -> m (u w)")[:, at + u : at + PAIR : 2]
+                    nc.tensor.transpose(y_banks[i, half][:, rows(2 * u + g)], source, ident[:])
 
         def group_y(i, half, copy=nc.scalar.copy):
             c, h = divmod(i, 2)
@@ -410,8 +420,8 @@ def tile_cubic_ocean_mode_step_h1_kernel(
                     out=bank[:],
                     lhsT=activations[0].bitcast(FP8X4),
                     lhsT_scale=activations[1],
-                    rhs=(c_raw_scales if WARM_ON_SCALES else c_raw_words[0])[:, g % 2, :].bitcast(FP4X4),
-                    rhs_scale=c_raw_scales[:, g % 2, :BANK],
+                    rhs=c_raw_words[0][:, g % 2, :].bitcast(FP4X4),
+                    rhs_scale=c_raw_scales[0][:, g % 2, :],
                     start=True,
                     stop=True,
                 )
@@ -422,17 +432,19 @@ def tile_cubic_ocean_mode_step_h1_kernel(
         warm_codes = keep.tile([P, P], U32, align_bytes=64)
         warm_scales = keep.tile([P, P], U8, align_bytes=64)
 
-        nc.vector.memset(c_raw_scales[:].bitcast(I32), 0)
+        for f in range(GF):
+            nc.vector.memset(c_raw_scales[f][:].bitcast(I32), 0)
         nc.vector.memset(b_scales[:].bitcast(I32), 0)
         make_identity(nc, ident[:])
 
         nc.sync.dma_start(out=drag_sb[:], in_=drag.rearrange("(g p t) -> p g t", p=P, t=4))
         load_amp(0)
         load_amp(1)
-        load_scales(c_raw_scales, coup_scales)
+        load_scales(c_raw_scales[0], coup_scales[:, :, cols(0)])
         load_words(c_raw_words, coup_words, 0)
         load_amp(2)
         load_amp(3)
+        load_scales(c_raw_scales[1], coup_scales[:, :, cols(1)])
         load_words(c_raw_words, coup_words, 1)
         nc.sync.dma_start(out=cubic_sb[:], in_=cubic.rearrange("(g p t) -> p g t", p=P, t=4))
         load_scales(b_scales, forc_scales)
@@ -465,14 +477,14 @@ def tile_cubic_ocean_mode_step_h1_kernel(
         group_amp(1, 0)
         group_amp(1, 1)
         deal_words(0, 0)
+        deal_words(0, 1)
         quantize_amp(0)
         quantize_amp(1)
         sort_amp(2, nc.scalar.copy)
         sort_amp(3, nc.scalar.copy)
-        deal_words(0, 1)
         deal_scales(1, 0)
-        deal_words(1, 0)
         deal_scales(1, 1)
+        deal_words(1, 0)
         deal_words(1, 1)
         for b in range(2):
             couple(0, b)
@@ -541,8 +553,9 @@ def tile_cubic_ocean_mode_step_h1_kernel(
         cube(3, 1)
         force(1, 0)
         quantize_amp(4)
-        group_h(3, nc.vector.tensor_copy, 0, P, GATES[0])
-        group_h(3, nc.scalar.copy, P, PAIR)
+        group_h(3, nc.vector.tensor_copy, 0, V3, GATES[0])
+        if V3 < PAIR:
+            group_h(3, nc.scalar.copy, V3, PAIR)
         quantize_amp(5)
         quantize_h(2)
         quantize_h(3)
@@ -590,14 +603,14 @@ def tile_cubic_ocean_mode_step_h1_kernel(
             if s % 2 == 0:
                 quantize_h(s + 2)
                 group_h(s + 3, nc.vector.tensor_copy, 0, PAIR if s == 2 else V7, GATES[s])
-                if s == 4:
+                if s == 4 and V7 < PAIR:
                     group_h(s + 3, nc.scalar.copy, V7, PAIR)
             if live(s + 5):
                 quantize_amp(s + 5)
             if s == 3:
                 quantize_y(0, (0,))
             if s % 2 == 1:
-                group_h(s + 3, nc.vector.tensor_copy, 0, VI)
+                group_h(s + 3, nc.vector.tensor_copy, 0, VI[s])
             if s == 4:
                 quantize_y(1)
                 store_codes(1)
@@ -611,8 +624,8 @@ def tile_cubic_ocean_mode_step_h1_kernel(
                 round_y(s - 1, HALF, 3 * BANK)
             round_y(s, 0, HALF)
             round_y(s, 3 * BANK, N)
-            if s % 2 == 1:
-                group_h(s + 3, nc.scalar.copy, VI, PAIR)
+            if s % 2 == 1 and VI[s] < PAIR:
+                group_h(s + 3, nc.scalar.copy, VI[s], PAIR)
 
         new_y(4, HALF, 3 * BANK, GATES[4])
         damp_pool(4, HALF, 3 * BANK)

@@ -68,8 +68,8 @@ def tile_cubic_ocean_mode_step_h1_kernel(
         amp_sb = {i: keep.tile([P, K], BF16, align_bytes=64, name="amp%d" % i) for i in range(FIRST_WHOLE, TILES)}
         slow_sb = [keep.tile([P, N], BF16, align_bytes=64, name="slow%d" % i) for i in range(TILES)]
         cubic_sb = keep.tile([P, GF, 4], BF16)
-        drag_sb = keep.tile([P, GN, 4], BF16)
-        denom = keep.tile([P, GN, 4], F32)
+        drag_rows = keep.tile([P, P], BF16, align_bytes=64)
+        denom_rows = keep.tile([P, P], F32, align_bytes=64)
         recip = keep.tile([P, GN, 4], F32)
         recip_rows = keep.tile([P, 3 * BANK], F32, align_bytes=64)
         ident = keep.tile([P, P], F32, align_bytes=64)
@@ -128,8 +128,7 @@ def tile_cubic_ocean_mode_step_h1_kernel(
         def keep_recip(g, width=BANK):
             bank = spreads[g] if g in spreads else recip_banks[g]
             nc.scalar.copy(
-                out=recip_rows[:, g * BANK : g * BANK + width].rearrange("m (p t) -> m p t", t=4),
-                in_=bank[:].rearrange("m (t p) -> m p t", t=4)[:, : width // 4, :],
+                out=recip_rows[:, g * BANK : g * BANK + width], in_=bank[:, :width]
             )
 
         def slab(k, shape, dtype):
@@ -322,24 +321,13 @@ def tile_cubic_ocean_mode_step_h1_kernel(
         def damp_from_bank(i, g, skip=0):
             lo, hi = g * BANK + skip, (g + 1) * BANK
             nc.vector.tensor_tensor(
-                out=y_part(i, lo, hi).rearrange("m (p t) -> m p t", t=4),
-                in0=sums[i][:, lo:hi].rearrange("m (p t) -> m p t", t=4),
-                in1=recip_banks[g][:].rearrange("m (t p) -> m p t", t=4)[:, skip // 4 :, :],
-                op=ALU.mult,
+                out=y_part(i, lo, hi), in0=sums[i][:, lo:hi], in1=recip_banks[g][:, skip:], op=ALU.mult
             )
 
         def pairs_of(i):
             if i not in y_pairs:
                 y_pairs[i] = deep.tile([P, 2, N // 4, 2], BF16, align_bytes=64, name="y_pairs")
             return y_pairs[i]
-
-        def damp_rounded(i, g):
-            nc.vector.tensor_tensor(
-                out=pairs_of(i)[:, :, rows(g), :],
-                in0=sums[i][:, cols(g)].rearrange("m (p u e) -> m u p e", u=2, e=2),
-                in1=recip_banks[g][:].rearrange("m (u e p) -> m u p e", u=2, e=2),
-                op=ALU.mult,
-            )
 
         def store_y(i, lo):
             nc.sync.dma_start(out=out_0[rows(i), lo : ys[i, lo][1]], in_=ys[i, lo][0][:])
@@ -432,12 +420,13 @@ def tile_cubic_ocean_mode_step_h1_kernel(
         warm_codes = keep.tile([P, P], U32, align_bytes=64)
         warm_scales = keep.tile([P, P], U8, align_bytes=64)
 
+        nc.gpsimd.memset(drag_rows[:].bitcast(I32), 0)
         for f in range(GF):
             nc.vector.memset(c_raw_scales[f][:].bitcast(I32), 0)
         nc.vector.memset(b_scales[:].bitcast(I32), 0)
         make_identity(nc, ident[:])
 
-        nc.sync.dma_start(out=drag_sb[:], in_=drag.rearrange("(g p t) -> p g t", p=P, t=4))
+        nc.sync.dma_start(out=drag_rows[: N // P, :], in_=drag.rearrange("(j p) -> j p", p=P))
         load_amp(0)
         load_amp(1)
         load_scales(c_raw_scales[0], coup_scales[:, :, cols(0)])
@@ -460,8 +449,10 @@ def tile_cubic_ocean_mode_step_h1_kernel(
         for i in range(3, TILES):
             load_slow(i)
 
-        nc.vector.tensor_scalar(out=denom[:], in0=drag_sb[:], scalar1=1.0, scalar2=None, op0=ALU.add)
-        nc.vector.reciprocal(out=recip[:], in_=denom[:])
+        nc.vector.tensor_scalar(out=denom_rows[:], in0=drag_rows[:], scalar1=1.0, scalar2=None, op0=ALU.add)
+        denom_bank = ring_bank()
+        nc.tensor.transpose(denom_bank[:, :P], denom_rows[:], ident[:])
+        nc.vector.reciprocal(out=recip[:].rearrange("p g t -> p (g t)"), in_=denom_bank[:, : N // P])
         spread_rows(0)
         keep_recip(0)
         sort_amp(0, nc.vector.tensor_copy)

@@ -26,15 +26,15 @@ GK = K // BANK
 GF = F // BANK
 GN = N // BANK
 RING = 7
-Y_BUFS = 5
-VI = {1: 160, 3: 128}
+VI = {1: 128, 3: 96}
 V3 = 128
-GATES = ("small0", "small1", "small0", "wide0", "small1")
-G2 = 160
 V7 = 128
-FIRST_WHOLE = 0
-WARM_ON_SCALES = False
+G2 = 160
 PLAIN = ()
+GATES = ("small0", "small1", "sorted0", "wide0", "sorted1")
+SUMS = 8
+AMPS = 4
+CODES = ("y_codes0", "y_codes1", "c_raw_words0", "c_raw_words1")
 
 
 def tile_cubic_ocean_mode_step_h1_kernel(
@@ -65,8 +65,8 @@ def tile_cubic_ocean_mode_step_h1_kernel(
                 c_scales[f, b] = keep.tile([P, GK, PAIR], U8, align_bytes=64, name="c_scales%d%d" % (f, b))
         b_words = [keep.tile([P, GF, N], U8, align_bytes=64, name="b_words%d" % h) for h in range(2)]
         b_scales = keep.tile([P, GF, N], U8, align_bytes=64)
-        amp_sb = {i: keep.tile([P, K], BF16, align_bytes=64, name="amp%d" % i) for i in range(FIRST_WHOLE, TILES)}
-        slow_sb = [keep.tile([P, N], BF16, align_bytes=64, name="slow%d" % i) for i in range(TILES)]
+        amp_sb = {}
+        slow_sb = {}
         cubic_sb = keep.tile([P, GF, 4], BF16)
         drag_rows = keep.tile([P, P], BF16, align_bytes=64)
         denom_rows = keep.tile([P, P], F32, align_bytes=64)
@@ -96,10 +96,16 @@ def tile_cubic_ocean_mode_step_h1_kernel(
             )
 
         def load_amp(i):
+            amp_sb[i] = keep.tile([P, K], BF16, align_bytes=64, name="amp%d" % (i % AMPS))
             nc.sync.dma_start(out=amp_sb[i][:], in_=amp[rows(i), :])
 
-        def load_slow(i):
-            nc.sync.dma_start(out=slow_sb[i][:], in_=slow[rows(i), :])
+        def load_slow(first, count):
+            tiles = keep.tile([P, count, N], BF16, align_bytes=64, name="slow%d" % first)
+            nc.sync.dma_start(
+                out=tiles[:], in_=slow[first * P : (first + count) * P, :].rearrange("(i m) n -> m i n", m=P)
+            )
+            for i in range(count):
+                slow_sb[first + i] = tiles[:, i, :]
 
         def deal_words(f, b, copy=nc.vector.tensor_copy):
             slots = slice(2 * b, 2 * b + 2)
@@ -136,48 +142,13 @@ def tile_cubic_ocean_mode_step_h1_kernel(
 
         a_sorted, a_banks, a_grouped, a_codes, a_scales = {}, {}, {}, {}, {}
         u_banks, squares, h_slots, h_grouped, h_codes, h_scales = {}, {}, {}, {}, {}, {}
-        e_banks, sums, ys, y_pairs, y_banks, y_grouped, y_codes = {}, {}, {}, {}, {}, {}, {}
+        e_banks, sums, thirds, y_pairs, y_banks, y_grouped, y_codes = {}, {}, {}, {}, {}, {}, {}
 
         def sort_amp(i, copy):
-            a_sorted[i] = work.tile([P, GK, 2, P], F32, align_bytes=64, name="a_sorted")
+            a_sorted[i] = slab("sorted%d" % (i % 2), [P, GK, 2, P], F32)
             copy(
                 out=a_sorted[i][:].rearrange("m g u p -> m g p u"),
                 in_=amp_sb[i][:].bitcast(F32).rearrange("m (g p u) -> m g p u", p=P, u=2),
-            )
-
-        first_amp, first_sorted, first_banks, first_grouped = {}, {}, {}, {}
-
-        def load_first(g):
-            first_amp[g] = keep.tile([P, 2, BANK], BF16, align_bytes=64, name="first_amp%d" % g)
-            nc.sync.dma_start(out=first_amp[g][:], in_=amp[:PAIR, cols(g)].rearrange("(h m) k -> m h k", h=2))
-
-        def sort_first(g):
-            first_sorted[g] = deep.tile([P, 2, 2, P], F32, align_bytes=64, name="first_sorted")
-            nc.vector.tensor_copy(
-                out=first_sorted[g][:].rearrange("m h u p -> m h p u"),
-                in_=first_amp[g][:].bitcast(F32).rearrange("m h (p u) -> m h p u", u=2),
-            )
-
-        def transpose_first(g):
-            first_banks[g] = ring_bank()
-            for h in range(2):
-                for u in range(2):
-                    nc.tensor.transpose(first_banks[g][:, rows(2 * h + u)], first_sorted[g][:, h, u, :], ident[:])
-
-        def group_first(g):
-            first_grouped[g] = deep.tile([P, 2 * BANK], BF16, align_bytes=64, name="first_grouped")
-            nc.scalar.copy(
-                out=first_grouped[g][:].bitcast(F32).rearrange("p (h m u) -> p h m u", u=2, m=P),
-                in_=first_banks[g][:].rearrange("p (h u m) -> p h m u", u=2, m=P),
-            )
-
-        def quantize_first(g):
-            if g == 0:
-                a_codes[0] = deep.tile([P, GK * PAIR], U32, align_bytes=64, name="a_codes")
-                a_scales[0] = deep.tile([P, GK * PAIR], U8, align_bytes=64, name="a_scales")
-            part = slice(g * PAIR, (g + 1) * PAIR)
-            nc.vector.quantize_mx(
-                out=a_codes[0][:, part].bitcast(FP8X4), scales=a_scales[0][:, part], in_=first_grouped[g][:]
             )
 
         def amp_pieces(n):
@@ -287,7 +258,7 @@ def tile_cubic_ocean_mode_step_h1_kernel(
 
         def force(i, j, passes=range(GF)):
             if i not in sums:
-                sums[i] = deep.tile([P, N], F32, align_bytes=64, name="sums")
+                sums[i] = keep.tile([P, N], F32, align_bytes=64, name="sums%d" % (i % SUMS))
             if (i, j) not in e_banks:
                 e_banks[i, j] = ring_bank()
             c, h = divmod(i, 2)
@@ -305,15 +276,13 @@ def tile_cubic_ocean_mode_step_h1_kernel(
         def add_slow(i, j):
             nc.vector.tensor_tensor(out=sums[i][:, cols(j)], in0=e_banks[i, j][:], in1=slow_sb[i][:, cols(j)], op=ALU.add)
 
-        def new_y(i, lo, hi, gate=None):
-            if gate is None:
-                ys[i, lo] = (deep.tile([P, hi - lo], F32, align_bytes=64, name="y_piece", bufs=Y_BUFS), hi)
-            else:
-                ys[i, lo] = (slab(gate, [P, hi - lo], F32), hi)
+        def gate_third(i, gate):
+            thirds[i] = slab(gate, [P, BANK], F32)
 
         def y_part(i, lo, hi):
-            at = max(k[1] for k in ys if k[0] == i and k[1] <= lo)
-            return ys[i, at][0][:, lo - at : hi - at]
+            if i in thirds and lo == HALF:
+                return thirds[i][:]
+            return sums[i][:, lo:hi]
 
         def damp_pool(i, lo, hi):
             nc.gpsimd.tensor_tensor(out=y_part(i, lo, hi), in0=sums[i][:, lo:hi], in1=recip_rows[:, lo:hi], op=ALU.mult)
@@ -329,8 +298,8 @@ def tile_cubic_ocean_mode_step_h1_kernel(
                 y_pairs[i] = deep.tile([P, 2, N // 4, 2], BF16, align_bytes=64, name="y_pairs")
             return y_pairs[i]
 
-        def store_y(i, lo):
-            nc.sync.dma_start(out=out_0[rows(i), lo : ys[i, lo][1]], in_=ys[i, lo][0][:])
+        def store_y(i, lo, hi):
+            nc.sync.dma_start(out=out_0[rows(i), lo:hi], in_=y_part(i, lo, hi))
 
         def round_y(i, lo, hi):
             if i in PLAIN:
@@ -388,7 +357,7 @@ def tile_cubic_ocean_mode_step_h1_kernel(
 
         def quantize_y(c, groups=range(GN), lo=0, hi=2):
             if c not in y_codes:
-                y_codes[c] = work.tile([P, GN, PAIR], U32, align_bytes=64, name="y_codes")
+                y_codes[c] = keep.tile([P, GN, PAIR], U32, align_bytes=64, name=CODES[c])
             for g in groups:
                 nc.vector.quantize_mx(
                     out=y_codes[c][:, g, lo * P : hi * P].bitcast(FP8X4),
@@ -438,16 +407,15 @@ def tile_cubic_ocean_mode_step_h1_kernel(
         nc.sync.dma_start(out=cubic_sb[:], in_=cubic.rearrange("(g p t) -> p g t", p=P, t=4))
         load_scales(b_scales, forc_scales)
         load_words(b_words, forc_words, 0)
-        load_slow(0)
+        load_slow(0, 1)
         load_words(b_words, forc_words, 1)
         load_amp(4)
         load_amp(5)
-        load_slow(1)
-        load_slow(2)
+        load_slow(1, 2)
         load_amp(6)
         load_amp(7)
-        for i in range(3, TILES):
-            load_slow(i)
+        load_slow(3, 2)
+        load_slow(5, 3)
 
         nc.vector.tensor_scalar(out=denom_rows[:], in0=drag_rows[:], scalar1=1.0, scalar2=None, op0=ALU.add)
         denom_bank = ring_bank()
@@ -518,9 +486,8 @@ def tile_cubic_ocean_mode_step_h1_kernel(
         force(0, 1, (1,))
         add_slow(0, 0)
         add_slow(0, 1)
-        new_y(0, 0, HALF)
         damp_pool(0, 0, HALF)
-        store_y(0, 0)
+        store_y(0, 0, HALF)
         cube(2, 1)
         force(0, 3)
         add_slow(0, 3)
@@ -532,9 +499,8 @@ def tile_cubic_ocean_mode_step_h1_kernel(
             if b == 0:
                 group_h(2, nc.scalar.copy, G2, PAIR)
         group_h(2, pool_copy, 0, G2)
-        new_y(0, 3 * BANK, N)
         damp_from_bank(0, 3)
-        store_y(0, 3 * BANK)
+        store_y(0, 3 * BANK, N)
         transpose_amp(4, 5)
         group_amp(4, 1)
         group_amp(4, 0)
@@ -555,19 +521,17 @@ def tile_cubic_ocean_mode_step_h1_kernel(
         round_y(0, 3 * BANK, N)
 
         for s in range(1, TILES - 3):
-            new_y(s - 1, HALF, 3 * BANK, GATES[s - 1])
+            gate_third(s - 1, GATES[s - 1])
             damp_pool(s - 1, HALF, 3 * BANK)
-            store_y(s - 1, HALF)
+            store_y(s - 1, HALF, 3 * BANK)
             for j in (0, 1, 3, 2):
                 if (s, j) != (1, 0):
                     force(s, j)
                     add_slow(s, j)
-            new_y(s, 0, HALF)
             damp_pool(s, 0, HALF)
-            store_y(s, 0)
-            new_y(s, 3 * BANK, N)
+            store_y(s, 0, HALF)
             damp_from_bank(s, 3)
-            store_y(s, 3 * BANK)
+            store_y(s, 3 * BANK, N)
             for b in range(2):
                 couple(s + 3, b)
                 square(s + 3, b)
@@ -618,9 +582,9 @@ def tile_cubic_ocean_mode_step_h1_kernel(
             if s % 2 == 1 and VI[s] < PAIR:
                 group_h(s + 3, nc.scalar.copy, VI[s], PAIR)
 
-        new_y(4, HALF, 3 * BANK, GATES[4])
+        gate_third(4, GATES[4])
         damp_pool(4, HALF, 3 * BANK)
-        store_y(4, HALF)
+        store_y(4, HALF, 3 * BANK)
         add_slow(5, 0)
         add_slow(5, 1)
         for j in (3, 2):
@@ -633,13 +597,11 @@ def tile_cubic_ocean_mode_step_h1_kernel(
         spread_recip(2, recip_banks[2])
         group_y(4, 0)
         round_y(4, HALF, 3 * BANK)
-        new_y(5, 0, HALF)
         damp_pool(5, 0, HALF)
-        store_y(5, 0)
-        new_y(5, HALF, N)
+        store_y(5, 0, HALF)
         damp_from_bank(5, 3)
         damp_pool(5, HALF, 3 * BANK)
-        store_y(5, HALF)
+        store_y(5, HALF, N)
         for j in range(GN):
             if j > 1:
                 force(6, j)
@@ -651,13 +613,11 @@ def tile_cubic_ocean_mode_step_h1_kernel(
         round_y(5, HALF, 3 * BANK)
         recip_banks[1] = ring_bank(hold=True)
         spread_recip(1, recip_banks[1])
-        new_y(6, 0, HALF)
         damp_pool(6, 0, HALF)
-        new_y(6, HALF, N)
         damp_from_bank(6, 2)
         damp_from_bank(6, 3)
-        store_y(6, HALF)
-        store_y(6, 0)
+        store_y(6, HALF, N)
+        store_y(6, 0, HALF)
         last = TILES - 1
         for j in (0, 1, 2):
             force(7, j)
@@ -670,15 +630,13 @@ def tile_cubic_ocean_mode_step_h1_kernel(
         transpose_y(5, 1)
         group_y(5, 1)
         round_y(6, 0, HALF)
-        new_y(last, 0, HALF)
         damp_pool(last, 0, BANK)
         round_pool(last, 0, BANK)
         damp_from_bank(last, 1)
-        store_y(last, 0)
-        new_y(last, HALF, N)
+        store_y(last, 0, HALF)
         damp_from_bank(last, 2)
         damp_from_bank(last, 3)
-        store_y(last, HALF)
+        store_y(last, HALF, N)
         round_vector(last, BANK, HALF)
         round_vector(last, HALF, N)
         transpose_y(6, 1)

@@ -151,6 +151,41 @@ def tile_cubic_ocean_mode_step_h1_kernel(
                 in_=amp_sb[i][:].bitcast(F32).rearrange("m (g p u) -> m g p u", p=P, u=2),
             )
 
+        first_amp, first_sorted, first_banks, first_grouped = {}, {}, {}, {}
+
+        def load_first(g):
+            first_amp[g] = keep.tile([P, 2, BANK], BF16, align_bytes=64, name=("amp0", "amp1", "small0")[g])
+            nc.sync.dma_start(out=first_amp[g][:], in_=amp[:PAIR, cols(g)].rearrange("(h m) k -> m h k", h=2))
+
+        def sort_first(g):
+            first_sorted[g] = deep.tile([P, 2, 2, P], F32, align_bytes=64, name="squares")
+            nc.vector.tensor_copy(
+                out=first_sorted[g][:].rearrange("m h u p -> m h p u"),
+                in_=first_amp[g][:].bitcast(F32).rearrange("m h (p u) -> m h p u", u=2),
+            )
+
+        def transpose_first(g):
+            first_banks[g] = ring_bank()
+            for h in range(2):
+                for u in range(2):
+                    nc.tensor.transpose(first_banks[g][:, rows(2 * h + u)], first_sorted[g][:, h, u, :], ident[:])
+
+        def group_first(g):
+            first_grouped[g] = deep.tile([P, 2 * BANK], BF16, align_bytes=64, name="y_pairs")
+            nc.scalar.copy(
+                out=first_grouped[g][:].bitcast(F32).rearrange("p (h m u) -> p h m u", u=2, m=P),
+                in_=first_banks[g][:].rearrange("p (h u m) -> p h m u", u=2, m=P),
+            )
+
+        def quantize_first(g):
+            if g == 0:
+                a_codes[0] = deep.tile([P, GK * PAIR], U32, align_bytes=64, name="a_codes")
+                a_scales[0] = deep.tile([P, GK * PAIR], U8, align_bytes=64, name="a_scales")
+            part = slice(g * PAIR, (g + 1) * PAIR)
+            nc.vector.quantize_mx(
+                out=a_codes[0][:, part].bitcast(FP8X4), scales=a_scales[0][:, part], in_=first_grouped[g][:]
+            )
+
         def amp_pieces(n):
             return (((0, 0), (0, 1)), ((1, 0),)) if n % 2 == 0 else (((1, 1),), ((2, 0), (2, 1)))
 
@@ -286,6 +321,9 @@ def tile_cubic_ocean_mode_step_h1_kernel(
 
         def damp_pool(i, lo, hi):
             nc.gpsimd.tensor_tensor(out=y_part(i, lo, hi), in0=sums[i][:, lo:hi], in1=recip_rows[:, lo:hi], op=ALU.mult)
+
+        def damp_from_rows(i, lo, hi):
+            nc.vector.tensor_tensor(out=sums[i][:, lo:hi], in0=sums[i][:, lo:hi], in1=recip_rows[:, lo:hi], op=ALU.mult)
 
         def damp_from_bank(i, g, skip=0):
             lo, hi = g * BANK + skip, (g + 1) * BANK
@@ -560,12 +598,12 @@ def tile_cubic_ocean_mode_step_h1_kernel(
                 group_h(s + 3, nc.vector.tensor_copy, 0, PAIR if s == 2 else V7, GATES[s])
                 if s == 4 and V7 < PAIR:
                     group_h(s + 3, nc.scalar.copy, V7, PAIR)
-            if live(s + 5):
-                quantize_amp(s + 5)
             if s == 3:
                 quantize_y(0, (0,))
             if s % 2 == 1:
                 group_h(s + 3, nc.vector.tensor_copy, 0, VI[s])
+            if live(s + 5):
+                quantize_amp(s + 5)
             if s == 4:
                 quantize_y(1)
                 store_codes(1)

@@ -26,7 +26,7 @@ GK = K // BANK
 GF = F // BANK
 GN = N // BANK
 RING = 7
-VI = {1: 128, 3: 96}
+VI = {1: 128, 3: 64}
 V3 = 128
 V7 = 128
 G2 = 160
@@ -35,6 +35,7 @@ GATES = ("small0", "small1", "sorted0", "wide0", "sorted1")
 SUMS = 8
 AMPS = 4
 CODES = ("y_codes0", "y_codes1", "c_raw_words0", "c_raw_words1")
+H_SLABS = ("wide1", "small0", "sorted0", "sorted1")
 
 
 def tile_cubic_ocean_mode_step_h1_kernel(
@@ -60,9 +61,8 @@ def tile_cubic_ocean_mode_step_h1_kernel(
         c_raw_scales = [keep.tile([P, GK, BANK], U8, align_bytes=64, name="c_raw_scales%d" % f) for f in range(GF)]
         c_words, c_scales = {}, {}
         for f in range(GF):
-            for b in range(2):
-                c_words[f, b] = keep.tile([P, GK, BANK], U8, align_bytes=64, name="c_words%d%d" % (f, b))
-                c_scales[f, b] = keep.tile([P, GK, PAIR], U8, align_bytes=64, name="c_scales%d%d" % (f, b))
+            c_words[f] = keep.tile([P, GK, 2 * BANK], U8, align_bytes=64, name="c_words%d" % f)
+            c_scales[f] = keep.tile([P, GK, BANK], U8, align_bytes=64, name="c_scales%d" % f)
         b_words = [keep.tile([P, GF, N], U8, align_bytes=64, name="b_words%d" % h) for h in range(2)]
         b_scales = keep.tile([P, GF, N], U8, align_bytes=64)
         amp_sb = {}
@@ -107,18 +107,16 @@ def tile_cubic_ocean_mode_step_h1_kernel(
             for i in range(count):
                 slow_sb[first + i] = tiles[:, i, :]
 
-        def deal_words(f, b, copy=nc.vector.tensor_copy):
-            slots = slice(2 * b, 2 * b + 2)
-            copy(
-                out=c_words[f, b][:].bitcast(U16).rearrange("p g (t c i) -> p c g t i", t=2, i=8),
-                in_=c_raw_words[f][:].bitcast(U16).rearrange("p g (c i t) -> p c g t i", t=4, i=8)[:, :, :, slots, :],
+        def deal_words(f):
+            nc.vector.tensor_copy(
+                out=c_words[f][:].bitcast(U16).rearrange("p g (t c i) -> p c g t i", t=4, i=8),
+                in_=c_raw_words[f][:].bitcast(U16).rearrange("p g (c i t) -> p c g t i", t=4, i=8),
             )
 
-        def deal_scales(f, b):
-            slots = slice(2 * b, 2 * b + 2)
+        def deal_scales(f):
             nc.vector.tensor_copy(
-                out=c_scales[f, b][:].rearrange("p g (t c i) -> p c g t i", t=2, i=16),
-                in_=c_raw_scales[f][:].rearrange("p g (c i t) -> p c g t i", t=4, i=16)[:, :, :, slots, :],
+                out=c_scales[f][:].rearrange("p g (t c i) -> p c g t i", t=4, i=16),
+                in_=c_raw_scales[f][:].rearrange("p g (c i t) -> p c g t i", t=4, i=16),
             )
 
         def spread_recip(g, spread):
@@ -240,8 +238,8 @@ def tile_cubic_ocean_mode_step_h1_kernel(
                     members = slice(g * PAIR, (g + 1) * PAIR)
                     nc.tensor.matmul_mx(
                         out=u_banks[n, b][:, s * PAIR : (s + 1) * PAIR],
-                        lhsT=c_words[f, b][:, g, s * PAIR : (s + 1) * PAIR].bitcast(FP4X4),
-                        lhsT_scale=c_scales[f, b][:, g, rows(s)],
+                        lhsT=c_words[f][:, g, (2 * b + s) * PAIR : (2 * b + s + 1) * PAIR].bitcast(FP4X4),
+                        lhsT_scale=c_scales[f][:, g, rows(2 * b + s)],
                         rhs=a_codes[c][:, members].bitcast(FP8X4),
                         rhs_scale=a_scales[c][:, members],
                         start=(g == 0),
@@ -270,25 +268,23 @@ def tile_cubic_ocean_mode_step_h1_kernel(
         def pool_copy(out, in_):
             nc.gpsimd.tensor_scalar(out=out, in0=in_, scalar1=1.0, scalar2=0.0, op0=ALU.mult, op1=ALU.add)
 
-        def group_h(n, copy, lo=0, hi=PAIR, gate=None):
-            if n not in h_grouped:
-                if gate is None:
-                    h_grouped[n] = work.tile([P, PAIR, 4], BF16, align_bytes=64, name="h_grouped")
-                else:
-                    h_grouped[n] = slab(gate, [P, PAIR, 4], BF16)
+        def group_h(n, copy, lo=0, hi=PAIR):
+            c, f = divmod(n, GF)
+            if c not in h_grouped:
+                h_grouped[c] = slab(H_SLABS[c], [P, GF, PAIR, 4], BF16)
             copy(
-                out=h_grouped[n][:, lo:hi, :].rearrange("p (c i) t -> p c t i", i=4),
+                out=h_grouped[c][:, f, lo:hi, :].rearrange("p (c i) t -> p c t i", i=4),
                 in_=h_slots[n][:, :, lo:hi].rearrange("p t (c i) -> p c t i", i=4),
             )
 
-        def quantize_h(n, lo=0, hi=PAIR):
-            if n not in h_codes:
-                h_codes[n] = deep.tile([P, PAIR], U32, align_bytes=64, name="h_codes", bufs=4)
-                h_scales[n] = deep.tile([P, PAIR], U8, align_bytes=64, name="h_scales", bufs=4)
+        def quantize_h(c, lo=0, hi=GF * PAIR):
+            if c not in h_codes:
+                h_codes[c] = work.tile([P, GF * PAIR], U32, align_bytes=64, name="h_codes")
+                h_scales[c] = work.tile([P, GF * PAIR], U8, align_bytes=64, name="h_scales")
             nc.vector.quantize_mx(
-                out=h_codes[n][:, lo:hi].bitcast(FP8X4),
-                scales=h_scales[n][:, lo:hi],
-                in_=h_grouped[n][:, lo:hi, :].rearrange("p m t -> p (m t)"),
+                out=h_codes[c][:, lo:hi].bitcast(FP8X4),
+                scales=h_scales[c][:, lo:hi],
+                in_=h_grouped[c][:].rearrange("p f m t -> p (f m t)")[:, 4 * lo : 4 * hi],
             )
 
         def force(i, j, passes=range(GF)):
@@ -300,8 +296,8 @@ def tile_cubic_ocean_mode_step_h1_kernel(
             for f in passes:
                 nc.tensor.matmul_mx(
                     out=e_banks[i, j][:],
-                    lhsT=h_codes[2 * c + f][:, rows(h)].bitcast(FP8X4),
-                    lhsT_scale=h_scales[2 * c + f][:, rows(h)],
+                    lhsT=h_codes[c][:, rows(2 * f + h)].bitcast(FP8X4),
+                    lhsT_scale=h_scales[c][:, rows(2 * f + h)],
                     rhs=b_words[j // 2][:, f, 2 * BANK * (j % 2) : 2 * BANK * (j % 2 + 1)].bitcast(FP4X4),
                     rhs_scale=b_scales[:, f, cols(j)],
                     start=(f == 0),
@@ -440,9 +436,9 @@ def tile_cubic_ocean_mode_step_h1_kernel(
         load_words(c_raw_words, coup_words, 0)
         load_amp(2)
         load_amp(3)
-        load_scales(c_raw_scales[1], coup_scales[:, :, cols(1)])
         load_words(c_raw_words, coup_words, 1)
         nc.sync.dma_start(out=cubic_sb[:], in_=cubic.rearrange("(g p t) -> p g t", p=P, t=4))
+        load_scales(c_raw_scales[1], coup_scales[:, :, cols(1)])
         load_scales(b_scales, forc_scales)
         load_words(b_words, forc_words, 0)
         load_slow(0, 1)
@@ -452,8 +448,6 @@ def tile_cubic_ocean_mode_step_h1_kernel(
         load_slow(1, 2)
         load_amp(6)
         load_amp(7)
-        load_slow(3, 2)
-        load_slow(5, 3)
 
         nc.vector.tensor_scalar(out=denom_rows[:], in0=drag_rows[:], scalar1=1.0, scalar2=None, op0=ALU.add)
         denom_bank = ring_bank()
@@ -464,8 +458,7 @@ def tile_cubic_ocean_mode_step_h1_kernel(
         sort_amp(0, nc.vector.tensor_copy)
         nc.vector.quantize_mx(out=warm_codes[:].bitcast(FP8X4), scales=warm_scales[:], in_=amp_sb[0][:, :BANK])
         sort_amp(1, nc.vector.tensor_copy)
-        deal_scales(0, 0)
-        deal_scales(0, 1)
+        deal_scales(0)
         transpose_amp(0, 1)
         spread_recip(3, recip_banks[3])
         warm_up(2, ring_bank(), (warm_codes[:], warm_scales[:]))
@@ -473,16 +466,13 @@ def tile_cubic_ocean_mode_step_h1_kernel(
         group_amp(0, 0)
         group_amp(1, 0)
         group_amp(1, 1)
-        deal_words(0, 0)
-        deal_words(0, 1)
+        deal_words(0)
         quantize_amp(0)
         quantize_amp(1)
         sort_amp(2, nc.scalar.copy)
         sort_amp(3, nc.scalar.copy)
-        deal_scales(1, 0)
-        deal_scales(1, 1)
-        deal_words(1, 0)
-        deal_words(1, 1)
+        deal_words(1)
+        deal_scales(1)
         for b in range(2):
             couple(0, b)
             square(0, b)
@@ -503,7 +493,7 @@ def tile_cubic_ocean_mode_step_h1_kernel(
         group_h(0, nc.vector.tensor_copy, 0, PAIR)
         quantize_amp(3)
         cube(1, 0)
-        quantize_h(0)
+        quantize_h(0, 0, PAIR)
         cube(1, 1)
         couple(2, 0)
         couple(2, 1)
@@ -517,9 +507,9 @@ def tile_cubic_ocean_mode_step_h1_kernel(
         keep_recip(2)
         sort_amp(4, nc.scalar.copy)
         sort_amp(5, nc.scalar.copy)
-        quantize_h(1, 0, P)
+        quantize_h(0, PAIR, PAIR + P)
         cube(2, 0)
-        quantize_h(1, P, PAIR)
+        quantize_h(0, PAIR + P, 2 * PAIR)
         force(0, 0, (1,))
         force(0, 1, (1,))
         add_slow(0, 0)
@@ -539,6 +529,7 @@ def tile_cubic_ocean_mode_step_h1_kernel(
         group_h(2, pool_copy, 0, G2)
         damp_from_bank(0, 3)
         store_y(0, 3 * BANK, N)
+        load_slow(3, 2)
         transpose_amp(4, 5)
         group_amp(4, 1)
         group_amp(4, 0)
@@ -548,12 +539,11 @@ def tile_cubic_ocean_mode_step_h1_kernel(
         cube(3, 1)
         force(1, 0)
         quantize_amp(4)
-        group_h(3, nc.vector.tensor_copy, 0, V3, GATES[0])
+        group_h(3, nc.vector.tensor_copy, 0, V3)
         if V3 < PAIR:
             group_h(3, nc.scalar.copy, V3, PAIR)
         quantize_amp(5)
-        quantize_h(2)
-        quantize_h(3)
+        quantize_h(1)
         add_slow(1, 0)
         round_y(0, 0, HALF)
         round_y(0, 3 * BANK, N)
@@ -570,6 +560,8 @@ def tile_cubic_ocean_mode_step_h1_kernel(
             store_y(s, 0, HALF)
             damp_from_bank(s, 3)
             store_y(s, 3 * BANK, N)
+            if s == 1:
+                load_slow(5, 3)
             for b in range(2):
                 couple(s + 3, b)
                 square(s + 3, b)
@@ -578,9 +570,12 @@ def tile_cubic_ocean_mode_step_h1_kernel(
                 round_y(s - 1, HALF, 3 * BANK)
             if live(s + 5):
                 transpose_amp(s + 5)
+            if s == 3:
+                transpose_y(1, 0)
             if live(s - 2):
                 transpose_y(s - 2, 1)
-            transpose_y(s - 1, 0)
+            if s != 2:
+                transpose_y(s - 1, 0)
             if s == 4:
                 force(5, 0)
                 force(5, 1)
@@ -588,30 +583,30 @@ def tile_cubic_ocean_mode_step_h1_kernel(
             if live(s + 5):
                 for b in range(2):
                     group_amp(s + 5, b, GATES[s] if s == 1 else None)
+            if s == 3:
+                group_y(1, 0)
             if live(s - 2):
                 group_y(s - 2, 1)
-            group_y(s - 1, 0)
+            if s != 2:
+                group_y(s - 1, 0)
             if s == 4:
                 group_y(s - 1, 1)
             if s % 2 == 0:
-                quantize_h(s + 2)
-                group_h(s + 3, nc.vector.tensor_copy, 0, PAIR if s == 2 else V7, GATES[s])
+                group_h(s + 2, nc.vector.tensor_copy, 0, VI[s - 1])
+                group_h(s + 3, nc.vector.tensor_copy, 0, PAIR if s == 2 else V7)
                 if s == 4 and V7 < PAIR:
                     group_h(s + 3, nc.scalar.copy, V7, PAIR)
-            if s == 3:
-                quantize_y(0, (0,))
-            if s % 2 == 1:
-                group_h(s + 3, nc.vector.tensor_copy, 0, VI[s])
             if live(s + 5):
                 quantize_amp(s + 5)
             if s == 4:
+                quantize_h(3, 0, PAIR)
                 quantize_y(1)
                 store_codes(1)
                 store_scales([nc.sync], slice(0, 4 * P))
             if s % 2 == 0:
-                quantize_h(s + 3)
+                quantize_h(s // 2 + 1, 0 if s == 2 else PAIR)
             if s == 3:
-                quantize_y(0, (1, 2, 3))
+                quantize_y(0)
                 store_codes(0)
             if s != 4:
                 round_y(s - 1, HALF, 3 * BANK)
@@ -689,9 +684,8 @@ def tile_cubic_ocean_mode_step_h1_kernel(
         group_y(last, 0)
         transpose_y(last, 1)
         group_y(last, 1)
-        quantize_y(3, range(GN), 0, 1)
-        quantize_y(3, (0, 1), 1, 2)
+        quantize_y(3, (0, 1))
         store_codes(3, 0, 2)
-        quantize_y(3, (2, 3), 1, 2)
+        quantize_y(3, (2, 3))
         store_codes(3, 2, 4)
         store_scales([nc.scalar, nc.sync], slice(4 * P, M))

@@ -27,15 +27,16 @@ GF = F // BANK
 GN = N // BANK
 RING = 7
 VI = {1: 128, 3: 64}
-V3 = 128
-V7 = 128
+V3 = 208
+V7 = 176
 G2 = 160
 PLAIN = ()
-GATES = ("small0", "small1", "sorted0", "wide0", "sorted1")
+GATES = ("small0", "small1", "small2", "wide0", "wide1")
 SUMS = 8
 AMPS = 4
 CODES = ("y_codes0", "y_codes1", "c_raw_words0", "c_raw_words1")
-H_SLABS = ("wide1", "small0", "sorted0", "sorted1")
+H_SLABS = ("wide1", "wide0", "sorted0", "sorted1")
+POOL_END = 1536
 
 
 def tile_cubic_ocean_mode_step_h1_kernel(
@@ -308,7 +309,7 @@ def tile_cubic_ocean_mode_step_h1_kernel(
             nc.vector.tensor_tensor(out=sums[i][:, cols(j)], in0=e_banks[i, j][:], in1=slow_sb[i][:, cols(j)], op=ALU.add)
 
         def gate_third(i, gate):
-            thirds[i] = slab(gate, [P, BANK], F32)
+            thirds[i] = slab(gate, [P, POOL_END - HALF], F32)
 
         def y_part(i, lo, hi):
             if i in thirds and lo == HALF:
@@ -533,7 +534,7 @@ def tile_cubic_ocean_mode_step_h1_kernel(
         transpose_amp(4, 5)
         group_amp(4, 1)
         group_amp(4, 0)
-        group_amp(5, 0)
+        group_amp(5, 0, GATES[0])
         group_amp(5, 1)
         cube(3, 0)
         cube(3, 1)
@@ -582,7 +583,7 @@ def tile_cubic_ocean_mode_step_h1_kernel(
                 transpose_y(s - 1, 1)
             if live(s + 5):
                 for b in range(2):
-                    group_amp(s + 5, b, GATES[s] if s == 1 else None)
+                    group_amp(s + 5, b, GATES[s])
             if s == 3:
                 group_y(1, 0)
             if live(s - 2):
@@ -592,22 +593,23 @@ def tile_cubic_ocean_mode_step_h1_kernel(
             if s == 4:
                 group_y(s - 1, 1)
             if s % 2 == 0:
-                group_h(s + 2, nc.vector.tensor_copy, 0, VI[s - 1])
+                quantize_h(s // 2 + 1, 0, PAIR)
                 group_h(s + 3, nc.vector.tensor_copy, 0, PAIR if s == 2 else V7)
                 if s == 4 and V7 < PAIR:
                     group_h(s + 3, nc.scalar.copy, V7, PAIR)
             if live(s + 5):
                 quantize_amp(s + 5)
             if s == 4:
-                quantize_h(3, 0, PAIR)
                 quantize_y(1)
                 store_codes(1)
                 store_scales([nc.sync], slice(0, 4 * P))
             if s % 2 == 0:
-                quantize_h(s // 2 + 1, 0 if s == 2 else PAIR)
+                quantize_h(s // 2 + 1, PAIR)
             if s == 3:
                 quantize_y(0)
                 store_codes(0)
+            if s % 2 == 1:
+                group_h(s + 3, nc.vector.tensor_copy, 0, VI[s])
             if s != 4:
                 round_y(s - 1, HALF, 3 * BANK)
             round_y(s, 0, HALF)

@@ -21,22 +21,12 @@ P = 128
 BANK = 512
 TILES = M // P
 PAIR = 2 * P
-HALF = N // 2
+PAIRS = TILES // 2
 GK = K // BANK
 GF = F // BANK
 GN = N // BANK
 RING = 7
-VI = {1: 128, 3: 64}
-V3 = 208
-V7 = 176
-G2 = 160
-PLAIN = ()
-GATES = ("small0", "small1", "small2", "wide0", "wide1")
-SUMS = 8
-AMPS = 4
-CODES = ("y_codes0", "y_codes1", "c_raw_words0", "c_raw_words1")
-H_SLABS = ("wide1", "wide0", "sorted0", "sorted1")
-POOL_END = 1536
+SHARE = (128, 256, 256)
 
 
 def tile_cubic_ocean_mode_step_h1_kernel(
@@ -58,29 +48,35 @@ def tile_cubic_ocean_mode_step_h1_kernel(
                 ring.append(b)
             return psum.tile([P, BANK], F32, name="bank%d" % b)
 
-        c_raw_words = [keep.tile([P, GK, 2 * BANK], U8, align_bytes=64, name="c_raw_words%d" % f) for f in range(GF)]
-        c_raw_scales = [keep.tile([P, GK, BANK], U8, align_bytes=64, name="c_raw_scales%d" % f) for f in range(GF)]
-        c_words, c_scales = {}, {}
-        for f in range(GF):
-            c_words[f] = keep.tile([P, GK, 2 * BANK], U8, align_bytes=64, name="c_words%d" % f)
-            c_scales[f] = keep.tile([P, GK, BANK], U8, align_bytes=64, name="c_scales%d" % f)
-        b_words = [keep.tile([P, GF, N], U8, align_bytes=64, name="b_words%d" % h) for h in range(2)]
-        b_scales = keep.tile([P, GF, N], U8, align_bytes=64)
-        amp_sb = {}
-        slow_sb = {}
-        cubic_sb = keep.tile([P, GF, 4], BF16)
-        drag_rows = keep.tile([P, P], BF16, align_bytes=64)
-        denom_rows = keep.tile([P, P], F32, align_bytes=64)
-        recip = keep.tile([P, GN, 4], F32)
-        recip_rows = keep.tile([P, 3 * BANK], F32, align_bytes=64)
-        ident = keep.tile([P, P], F32, align_bytes=64)
-        recip_banks = {GN - 1: psum.tile([P, BANK], F32, name="recip_bank")}
-
         def rows(i):
             return slice(i * P, (i + 1) * P)
 
-        def cols(g):
-            return slice(g * BANK, (g + 1) * BANK)
+        def cols(g, count=1):
+            return slice(g * BANK, (g + count) * BANK)
+
+        def named(name, shape, dtype):
+            return keep.tile(shape, dtype, align_bytes=64, name=name)
+
+        c_raw_words = [named("c_raw_words%d" % f, [P, GK, 2 * BANK], U8) for f in range(GF)]
+        c_raw_scales = [named("c_raw_scales%d" % f, [P, GK, BANK], U8) for f in range(GF)]
+        c_words = {(f, b): named("c_words%d%d" % (f, b), [P, GK, BANK], U8) for f in range(GF) for b in range(2)}
+        c_scales = [named("c_scales%d" % f, [P, GK, BANK], U8) for f in range(GF)]
+        b_words = [named("b_words%d" % h, [P, GF, N], U8) for h in range(2)]
+        b_scales = named("b_scales", [P, GF, N], U8)
+        cubic_sb = named("cubic_sb", [P, GF, 4], BF16)
+        drag_sb = named("drag_sb", [P, GN, 4], BF16)
+        denom = named("denom", [P, GN, 4], F32)
+        recip = named("recip", [P, GN, 4], F32)
+        recip_rows = named("recip_rows", [P, 3 * BANK], F32)
+        ident = named("ident", [P, P], F32)
+        y_scales = named("y_scales", [P, GN, M], U8)
+        warm_codes = named("warm_codes", [P, P], U32)
+        warm_scales = named("warm_scales", [P, P], U8)
+        recip_banks = {GN - 1: psum.tile([P, BANK], F32, name="recip_bank")}
+        amp_sb, slow_sb, spreads, a_sorted = {}, {}, {}, {}
+        a_banks, a_grouped, a_codes, a_scales = {}, {}, {}, {}
+        u_banks, squares, h_slots, h_grouped, h_codes, h_scales = {}, {}, {}, {}, {}, {}
+        e_banks, sums, moved, y_pairs, y_banks, y_grouped, y_codes = {}, {}, {}, {}, {}, {}, {}
 
         def load_scales(plane, scales):
             for q in (0, 2, 1, 3):
@@ -97,21 +93,23 @@ def tile_cubic_ocean_mode_step_h1_kernel(
             )
 
         def load_amp(i):
-            amp_sb[i] = keep.tile([P, K], BF16, align_bytes=64, name="amp%d" % (i % AMPS))
+            amp_sb[i] = named("amp%d" % (i % 6), [P, K], BF16)
             nc.sync.dma_start(out=amp_sb[i][:], in_=amp[rows(i), :])
 
         def load_slow(first, count):
-            tiles = keep.tile([P, count, N], BF16, align_bytes=64, name="slow%d" % first)
+            tiles = named("slow%d" % first, [P, count, N], BF16)
             nc.sync.dma_start(
                 out=tiles[:], in_=slow[first * P : (first + count) * P, :].rearrange("(i m) n -> m i n", m=P)
             )
             for i in range(count):
                 slow_sb[first + i] = tiles[:, i, :]
 
-        def deal_words(f):
-            nc.vector.tensor_copy(
-                out=c_words[f][:].bitcast(U16).rearrange("p g (t c i) -> p c g t i", t=4, i=8),
-                in_=c_raw_words[f][:].bitcast(U16).rearrange("p g (c i t) -> p c g t i", t=4, i=8),
+        def deal_words(f, b, copy):
+            copy(
+                out=c_words[f, b][:].bitcast(U16).rearrange("p g (t c i) -> p c g t i", t=2, i=8),
+                in_=c_raw_words[f][:].bitcast(U16).rearrange("p g (c i t) -> p c g t i", t=4, i=8)[
+                    :, :, :, 2 * b : 2 * b + 2, :
+                ],
             )
 
         def deal_scales(f):
@@ -120,115 +118,52 @@ def tile_cubic_ocean_mode_step_h1_kernel(
                 in_=c_raw_scales[f][:].rearrange("p g (c i t) -> p c g t i", t=4, i=16),
             )
 
-        def spread_recip(g, spread):
+        def spread_recip(g, bank):
             for t in range(4):
-                nc.tensor.transpose(spread[:, t * P : (t + 1) * P], recip[:, g, t : t + 1].to_broadcast([P, P]), ident[:])
+                nc.tensor.transpose(bank[:, rows(t)], recip[:, g, t : t + 1].to_broadcast([P, P]), ident[:])
 
-        spreads = {}
+        def natural(bank):
+            return bank[:].rearrange("m (t p) -> m p t", t=4)
 
         def spread_rows(g):
             spreads[g] = ring_bank()
             spread_recip(g, spreads[g])
 
-        def keep_recip(g, width=BANK):
-            bank = spreads[g] if g in spreads else recip_banks[g]
-            nc.scalar.copy(
-                out=recip_rows[:, g * BANK : g * BANK + width], in_=bank[:, :width]
-            )
-
-        def slab(k, shape, dtype):
-            return keep.tile(shape, dtype, align_bytes=64, name=k)
-
-        a_sorted, a_banks, a_grouped, a_codes, a_scales = {}, {}, {}, {}, {}
-        u_banks, squares, h_slots, h_grouped, h_codes, h_scales = {}, {}, {}, {}, {}, {}
-        e_banks, sums, thirds, y_pairs, y_banks, y_grouped, y_codes = {}, {}, {}, {}, {}, {}, {}
+        def keep_recip(g):
+            nc.scalar.copy(out=recip_rows[:, cols(g)].rearrange("m (p t) -> m p t", t=4), in_=natural(spreads[g]))
 
         def sort_amp(i, copy):
-            a_sorted[i] = slab("sorted%d" % (i % 2), [P, GK, 2, P], F32)
-            copy(
-                out=a_sorted[i][:].rearrange("m g u p -> m g p u"),
-                in_=amp_sb[i][:].bitcast(F32).rearrange("m (g p u) -> m g p u", p=P, u=2),
-            )
+            a_sorted[i] = named("a_sorted%d" % (i % 2), [P, GK, 2, P], F32)
+            copy(out=a_sorted[i][:], in_=amp_sb[i][:].bitcast(F32).rearrange("m (g p u) -> m g u p", p=P, u=2))
 
-        first_amp, first_sorted, first_banks, first_grouped = {}, {}, {}, {}
-
-        def load_first(g):
-            first_amp[g] = keep.tile([P, 2, BANK], BF16, align_bytes=64, name=("amp0", "amp1", "small0")[g])
-            nc.sync.dma_start(out=first_amp[g][:], in_=amp[:PAIR, cols(g)].rearrange("(h m) k -> m h k", h=2))
-
-        def sort_first(g):
-            first_sorted[g] = deep.tile([P, 2, 2, P], F32, align_bytes=64, name="squares")
-            nc.vector.tensor_copy(
-                out=first_sorted[g][:].rearrange("m h u p -> m h p u"),
-                in_=first_amp[g][:].bitcast(F32).rearrange("m h (p u) -> m h p u", u=2),
-            )
-
-        def transpose_first(g):
-            first_banks[g] = ring_bank()
+        def transpose_amp(c, groups):
+            for g in groups:
+                a_banks[c, g] = ring_bank()
             for h in range(2):
-                for u in range(2):
-                    nc.tensor.transpose(first_banks[g][:, rows(2 * h + u)], first_sorted[g][:, h, u, :], ident[:])
+                i = 2 * c + h
+                words = amp_sb[i][:].bitcast(F32)
+                for g in groups:
+                    for u in range(2):
+                        source = a_sorted[i][:, g, u, :] if i in a_sorted else words[:, PAIR * g + u : PAIR * (g + 1) : 2]
+                        nc.tensor.transpose(a_banks[c, g][:, rows(2 * h + u)], source, ident[:])
 
-        def group_first(g):
-            first_grouped[g] = deep.tile([P, 2 * BANK], BF16, align_bytes=64, name="y_pairs")
+        def group_amp(c, g):
+            if c not in a_grouped:
+                a_grouped[c] = named("a_grouped%d" % (c % 2), [P, GK, 2 * BANK], BF16)
             nc.scalar.copy(
-                out=first_grouped[g][:].bitcast(F32).rearrange("p (h m u) -> p h m u", u=2, m=P),
-                in_=first_banks[g][:].rearrange("p (h u m) -> p h m u", u=2, m=P),
+                out=a_grouped[c][:, g, :].bitcast(F32).rearrange("p (h m u) -> p h m u", u=2, m=P),
+                in_=a_banks[c, g][:].rearrange("p (h u m) -> p h m u", u=2, m=P),
             )
 
-        def quantize_first(g):
-            if g == 0:
-                a_codes[0] = deep.tile([P, GK * PAIR], U32, align_bytes=64, name="a_codes")
-                a_scales[0] = deep.tile([P, GK * PAIR], U8, align_bytes=64, name="a_scales")
-            part = slice(g * PAIR, (g + 1) * PAIR)
+        def quantize_amp(c, first, count):
+            if c not in a_codes:
+                a_codes[c] = work.tile([P, GK * PAIR], U32, align_bytes=64, name="a_codes")
+                a_scales[c] = work.tile([P, GK * PAIR], U8, align_bytes=64, name="a_scales")
+            part = slice(first * PAIR, (first + count) * PAIR)
             nc.vector.quantize_mx(
-                out=a_codes[0][:, part].bitcast(FP8X4), scales=a_scales[0][:, part], in_=first_grouped[g][:]
-            )
-
-        def amp_pieces(n):
-            return (((0, 0), (0, 1)), ((1, 0),)) if n % 2 == 0 else (((1, 1),), ((2, 0), (2, 1)))
-
-        def transpose_amp(*parts):
-            for n in parts:
-                for b in range(2):
-                    a_banks[n, b] = ring_bank()
-            for tile_h in range(2):
-                for n in parts:
-                    for b, pieces in enumerate(amp_pieces(n)):
-                        for slot, (g, h) in enumerate(pieces):
-                            if h == tile_h:
-                                i = 2 * (n // 2) + h
-                                words = amp_sb[i][:].bitcast(F32)
-                                for u in range(2):
-                                    at = (2 * slot + u) * P
-                                    source = (
-                                        a_sorted[i][:, g, u, :] if i in a_sorted else words[:, 256 * g + u : 256 * (g + 1) : 2]
-                                    )
-                                    nc.tensor.transpose(a_banks[n, b][:, at : at + P], source, ident[:])
-
-        def group_amp(n, b, gate=None):
-            if n not in a_grouped:
-                if gate is None:
-                    a_grouped[n] = work.tile([P, 3 * BANK], BF16, align_bytes=64, name="a_grouped")
-                else:
-                    a_grouped[n] = slab(gate, [P, 3 * BANK], BF16)
-            width = len(amp_pieces(n)[b])
-            done = 0 if b == 0 else 3 - width
-            nc.scalar.copy(
-                out=a_grouped[n][:, done * BANK : (done + width) * BANK]
-                .bitcast(F32)
-                .rearrange("p (s m u) -> p s m u", u=2, m=P),
-                in_=a_banks[n, b][:, : 256 * width].rearrange("p (s u m) -> p s m u", u=2, m=P),
-            )
-
-        def quantize_amp(n):
-            c = n // 2
-            if n % 2 == 0:
-                a_codes[c] = deep.tile([P, GK * PAIR], U32, align_bytes=64, name="a_codes")
-                a_scales[c] = deep.tile([P, GK * PAIR], U8, align_bytes=64, name="a_scales")
-            part = slice((n % 2) * 3 * P, (n % 2 + 1) * 3 * P)
-            nc.vector.quantize_mx(
-                out=a_codes[c][:, part].bitcast(FP8X4), scales=a_scales[c][:, part], in_=a_grouped[n][:]
+                out=a_codes[c][:, part].bitcast(FP8X4),
+                scales=a_scales[c][:, part],
+                in_=a_grouped[c][:, first : first + count, :].rearrange("p g x -> p (g x)"),
             )
 
         def couple(n, b):
@@ -239,7 +174,7 @@ def tile_cubic_ocean_mode_step_h1_kernel(
                     members = slice(g * PAIR, (g + 1) * PAIR)
                     nc.tensor.matmul_mx(
                         out=u_banks[n, b][:, s * PAIR : (s + 1) * PAIR],
-                        lhsT=c_words[f][:, g, (2 * b + s) * PAIR : (2 * b + s + 1) * PAIR].bitcast(FP4X4),
+                        lhsT=c_words[f, b][:, g, s * PAIR : (s + 1) * PAIR].bitcast(FP4X4),
                         lhsT_scale=c_scales[f][:, g, rows(2 * b + s)],
                         rhs=a_codes[c][:, members].bitcast(FP8X4),
                         rhs_scale=a_scales[c][:, members],
@@ -266,19 +201,16 @@ def tile_cubic_ocean_mode_step_h1_kernel(
                     op1=ALU.mult,
                 )
 
-        def pool_copy(out, in_):
-            nc.gpsimd.tensor_scalar(out=out, in0=in_, scalar1=1.0, scalar2=0.0, op0=ALU.mult, op1=ALU.add)
-
-        def group_h(n, copy, lo=0, hi=PAIR):
+        def group_h(n, copy, lo, hi):
             c, f = divmod(n, GF)
             if c not in h_grouped:
-                h_grouped[c] = slab(H_SLABS[c], [P, GF, PAIR, 4], BF16)
+                h_grouped[c] = named("h_grouped%d" % (c % 2), [P, GF, PAIR, 4], BF16)
             copy(
                 out=h_grouped[c][:, f, lo:hi, :].rearrange("p (c i) t -> p c t i", i=4),
                 in_=h_slots[n][:, :, lo:hi].rearrange("p t (c i) -> p c t i", i=4),
             )
 
-        def quantize_h(c, lo=0, hi=GF * PAIR):
+        def quantize_h(c, lo, hi):
             if c not in h_codes:
                 h_codes[c] = work.tile([P, GF * PAIR], U32, align_bytes=64, name="h_codes")
                 h_scales[c] = work.tile([P, GF * PAIR], U8, align_bytes=64, name="h_scales")
@@ -289,8 +221,6 @@ def tile_cubic_ocean_mode_step_h1_kernel(
             )
 
         def force(i, j, passes=range(GF)):
-            if i not in sums:
-                sums[i] = keep.tile([P, N], F32, align_bytes=64, name="sums%d" % (i % SUMS))
             if (i, j) not in e_banks:
                 e_banks[i, j] = ring_bank()
             c, h = divmod(i, 2)
@@ -305,83 +235,82 @@ def tile_cubic_ocean_mode_step_h1_kernel(
                     stop=(f == GF - 1),
                 )
 
+        def sum_part(i, g, count):
+            if i < 2 * last:
+                if i not in sums:
+                    sums[i] = named("sums%d" % (i % 4), [P, N], F32)
+                return sums[i][:, cols(g, count)]
+            if g not in last_sums:
+                last_sums[g] = named("last_sums%d" % g, [P, 2, BANK], F32)
+            return last_sums[g][:, i % 2, :]
+
         def add_slow(i, j):
-            nc.vector.tensor_tensor(out=sums[i][:, cols(j)], in0=e_banks[i, j][:], in1=slow_sb[i][:, cols(j)], op=ALU.add)
+            nc.vector.tensor_tensor(out=sum_part(i, j, 1), in0=e_banks[i, j][:], in1=slow_sb[i][:, cols(j)], op=ALU.add)
 
-        def gate_third(i, gate):
-            thirds[i] = slab(gate, [P, POOL_END - HALF], F32)
+        def y_part(i, g, count):
+            if (i, g) in moved:
+                return moved[i, g][:]
+            return sum_part(i, g, count)
 
-        def y_part(i, lo, hi):
-            if i in thirds and lo == HALF:
-                return thirds[i][:]
-            return sums[i][:, lo:hi]
-
-        def damp_pool(i, lo, hi):
-            nc.gpsimd.tensor_tensor(out=y_part(i, lo, hi), in0=sums[i][:, lo:hi], in1=recip_rows[:, lo:hi], op=ALU.mult)
-
-        def damp_from_rows(i, lo, hi):
-            nc.vector.tensor_tensor(out=sums[i][:, lo:hi], in0=sums[i][:, lo:hi], in1=recip_rows[:, lo:hi], op=ALU.mult)
-
-        def damp_from_bank(i, g, skip=0):
-            lo, hi = g * BANK + skip, (g + 1) * BANK
-            nc.vector.tensor_tensor(
-                out=y_part(i, lo, hi), in0=sums[i][:, lo:hi], in1=recip_banks[g][:, skip:], op=ALU.mult
+        def damp_pool(i, g, count, into=None):
+            if into is not None:
+                moved[i, g] = named(into, [P, count * BANK], F32)
+            nc.gpsimd.tensor_tensor(
+                out=y_part(i, g, count),
+                in0=sum_part(i, g, count),
+                in1=recip_rows[:, cols(g, count)],
+                op=ALU.mult,
             )
 
-        def pairs_of(i):
-            if i not in y_pairs:
-                y_pairs[i] = deep.tile([P, 2, N // 4, 2], BF16, align_bytes=64, name="y_pairs")
-            return y_pairs[i]
+        def damp_pool_last(g):
+            part = last_sums[g][:]
+            factors = recip_rows[:, cols(g)].unsqueeze(1).to_broadcast([P, 2, BANK])
+            nc.gpsimd.tensor_tensor(out=part, in0=part, in1=factors, op=ALU.mult)
 
-        def store_y(i, lo, hi):
-            nc.sync.dma_start(out=out_0[rows(i), lo:hi], in_=y_part(i, lo, hi))
+        def damp_vector(i, g):
+            part = y_part(i, g, 1).rearrange("m (p t) -> m p t", t=4)
+            nc.vector.tensor_tensor(out=part, in0=part, in1=natural(recip_banks[g]), op=ALU.mult)
 
-        def round_y(i, lo, hi):
-            if i in PLAIN:
-                flat = pairs_of(i)[:].rearrange("m u w e -> m (u w e)")
-                nc.scalar.activation(out=flat[:, lo:hi], in_=y_part(i, lo, hi), func=ACT.Copy)
-                return
-            nc.scalar.activation(
-                out=pairs_of(i)[:, :, lo // 4 : hi // 4, :].rearrange("m u w e -> m w u e"),
-                in_=y_part(i, lo, hi).rearrange("m (w u e) -> m w u e", u=2, e=2),
-                func=ACT.Copy,
-            )
+        def store_y(i, g, count):
+            nc.sync.dma_start(out=out_0[rows(i), cols(g, count)], in_=y_part(i, g, count))
 
-        def round_pool(i, lo, hi):
-            pool_copy(
-                out=pairs_of(i)[:, :, lo // 4 : hi // 4, :].rearrange("m u w e -> m w u e"),
-                in_=y_part(i, lo, hi).rearrange("m (w u e) -> m w u e", u=2, e=2),
-            )
+        def pairs_of(c):
+            if c not in y_pairs:
+                y_pairs[c] = work.tile([P, GN, 2, 2, P, 2], BF16, align_bytes=64, name="y_pairs")
+            return y_pairs[c]
 
-        def round_vector(i, lo, hi):
-            nc.vector.tensor_copy(
-                out=pairs_of(i)[:, :, lo // 4 : hi // 4, :].rearrange("m u w e -> m w u e"),
-                in_=y_part(i, lo, hi).rearrange("m (w u e) -> m w u e", u=2, e=2),
-            )
-
-        def transpose_y(i, half):
-            y_banks[i, half] = ring_bank()
-            words = y_pairs[i][:].rearrange("m u w e -> m u (w e)").bitcast(F32)
-            for u in range(2):
-                for g in range(2):
-                    source = words[:, u, rows(2 * half + g)]
-                    if i in PLAIN:
-                        at = PAIR * (2 * half + g)
-                        source = words.rearrange("m u w -> m (u w)")[:, at + u : at + PAIR : 2]
-                    nc.tensor.transpose(y_banks[i, half][:, rows(2 * u + g)], source, ident[:])
-
-        def group_y(i, half, copy=nc.scalar.copy):
-            c, h = divmod(i, 2)
-            if c not in y_grouped:
-                y_grouped[c] = slab("wide%d" % (c % 2), [P, GN, 2, BANK], BF16)
+        def round_y(i, g, count, copy=nc.scalar.copy):
             copy(
-                out=y_grouped[c][:, 2 * half : 2 * half + 2, h, :].bitcast(F32).rearrange("p g (m u) -> p g m u", u=2),
-                in_=y_banks[i, half][:].rearrange("p (u g m) -> p g m u", u=2, m=P),
+                out=pairs_of(i // 2)[:, g : g + count, i % 2, :, :, :],
+                in_=y_part(i, g, count).rearrange("m (g w u e) -> m g u w e", u=2, e=2, w=P),
+            )
+
+        def round_last(g, copy=nc.scalar.copy):
+            copy(
+                out=pairs_of(last)[:, g, :, :, :, :],
+                in_=last_sums[g][:].rearrange("m h (w u e) -> m h u w e", u=2, e=2),
+            )
+
+        def store_last(g):
+            nc.sync.dma_start(
+                out=out_0[last * PAIR :, cols(g)].rearrange("(h m) n -> m h n", h=2), in_=last_sums[g][:]
+            )
+
+        def transpose_y(c, g):
+            y_banks[c, g] = ring_bank()
+            for h in range(2):
+                words = y_pairs[c][:, g, h, :, :, :].rearrange("m u w e -> m u (w e)").bitcast(F32)
+                for u in range(2):
+                    nc.tensor.transpose(y_banks[c, g][:, rows(2 * h + u)], words[:, u, :], ident[:])
+
+        def group_y(c, g, copy=nc.scalar.copy):
+            y_grouped[c, g] = named("y_grouped%d%d" % (c % 2, g), [P, 2 * BANK], BF16)
+            copy(
+                out=y_grouped[c, g][:].bitcast(F32).rearrange("p (h m u) -> p h m u", u=2, m=P),
+                in_=y_banks[c, g][:].rearrange("p (h u m) -> p h m u", u=2, m=P),
             )
 
         out_words = out_1.rearrange("g p m t -> p g (m t)").bitcast(I32)
-
-        y_scales = keep.tile([P, GN, M], U8, align_bytes=64)
 
         def store_scales(queues, members):
             for q in range(4):
@@ -390,304 +319,241 @@ def tile_cubic_ocean_mode_step_h1_kernel(
                     in_=y_scales[32 * q : 32 * q + 4, :, members].bitcast(I32),
                 )
 
-        def quantize_y(c, groups=range(GN), lo=0, hi=2):
+        def quantize_y(c, groups):
             if c not in y_codes:
-                y_codes[c] = keep.tile([P, GN, PAIR], U32, align_bytes=64, name=CODES[c])
+                y_codes[c] = named(("y_codes0", "c_raw_words0", "c_raw_words1", "y_codes0")[c], [P, GN, PAIR], U32)
             for g in groups:
                 nc.vector.quantize_mx(
-                    out=y_codes[c][:, g, lo * P : hi * P].bitcast(FP8X4),
-                    scales=y_scales[:, g, (2 * c + lo) * P : (2 * c + hi) * P],
-                    in_=y_grouped[c][:, g, lo:hi, :].rearrange("p h c -> p (h c)"),
+                    out=y_codes[c][:, g, :].bitcast(FP8X4),
+                    scales=y_scales[:, g, c * PAIR : (c + 1) * PAIR],
+                    in_=y_grouped[c, g][:],
                 )
 
-        def store_codes(c, first=0, last=GN, lo=0, hi=2):
-            members = slice((2 * c + lo) * P, (2 * c + hi) * P)
+        def store_codes(c, first, count):
             nc.sync.dma_start(
-                out=out_words[:, first:last, members], in_=y_codes[c][:, first:last, lo * P : hi * P].bitcast(I32)
+                out=out_words[:, first : first + count, c * PAIR : (c + 1) * PAIR],
+                in_=y_codes[c][:, first : first + count, :].bitcast(I32),
             )
 
-        def warm_up(count, bank, activations):
+        def warm_up(count):
+            bank = ring_bank()
             for g in range(count):
                 nc.tensor.matmul_mx(
                     out=bank[:],
-                    lhsT=activations[0].bitcast(FP8X4),
-                    lhsT_scale=activations[1],
-                    rhs=c_raw_words[0][:, g % 2, :].bitcast(FP4X4),
-                    rhs_scale=c_raw_scales[0][:, g % 2, :],
+                    lhsT=warm_codes[:].bitcast(FP8X4),
+                    lhsT_scale=warm_scales[:],
+                    rhs=c_raw_words[0][:, g, :].bitcast(FP4X4),
+                    rhs_scale=c_raw_scales[0][:, g, :],
                     start=True,
                     stop=True,
                 )
 
-        def live(i):
-            return 0 <= i < TILES
+        last, last_sums = PAIRS - 1, {}
+        vcopy, scopy = nc.vector.tensor_copy, nc.scalar.copy
 
-        warm_codes = keep.tile([P, P], U32, align_bytes=64)
-        warm_scales = keep.tile([P, P], U8, align_bytes=64)
-
-        nc.gpsimd.memset(drag_rows[:].bitcast(I32), 0)
         for f in range(GF):
             nc.vector.memset(c_raw_scales[f][:].bitcast(I32), 0)
         nc.vector.memset(b_scales[:].bitcast(I32), 0)
         make_identity(nc, ident[:])
 
-        nc.sync.dma_start(out=drag_rows[: N // P, :], in_=drag.rearrange("(j p) -> j p", p=P))
+        nc.sync.dma_start(out=drag_sb[:], in_=drag.rearrange("(g p t) -> p g t", p=P, t=4))
         load_amp(0)
         load_amp(1)
         load_scales(c_raw_scales[0], coup_scales[:, :, cols(0)])
         load_words(c_raw_words, coup_words, 0)
-        load_amp(2)
-        load_amp(3)
-        load_words(c_raw_words, coup_words, 1)
-        nc.sync.dma_start(out=cubic_sb[:], in_=cubic.rearrange("(g p t) -> p g t", p=P, t=4))
         load_scales(c_raw_scales[1], coup_scales[:, :, cols(1)])
+        load_amp(2)
+        nc.sync.dma_start(out=cubic_sb[:], in_=cubic.rearrange("(g p t) -> p g t", p=P, t=4))
+        load_words(c_raw_words, coup_words, 1)
+        for i in (3, 4, 5):
+            load_amp(i)
         load_scales(b_scales, forc_scales)
         load_words(b_words, forc_words, 0)
         load_slow(0, 1)
         load_words(b_words, forc_words, 1)
-        load_amp(4)
-        load_amp(5)
-        load_slow(1, 2)
+        load_slow(1, 1)
         load_amp(6)
         load_amp(7)
+        load_slow(2, 2)
 
-        nc.vector.tensor_scalar(out=denom_rows[:], in0=drag_rows[:], scalar1=1.0, scalar2=None, op0=ALU.add)
-        denom_bank = ring_bank()
-        nc.tensor.transpose(denom_bank[:, :P], denom_rows[:], ident[:])
-        nc.vector.reciprocal(out=recip[:].rearrange("p g t -> p (g t)"), in_=denom_bank[:, : N // P])
-        spread_rows(0)
-        keep_recip(0)
-        sort_amp(0, nc.vector.tensor_copy)
+        nc.vector.tensor_scalar(out=denom[:], in0=drag_sb[:], scalar1=1.0, scalar2=None, op0=ALU.add)
+        nc.vector.reciprocal(out=recip[:], in_=denom[:])
         nc.vector.quantize_mx(out=warm_codes[:].bitcast(FP8X4), scales=warm_scales[:], in_=amp_sb[0][:, :BANK])
-        sort_amp(1, nc.vector.tensor_copy)
+        transpose_amp(0, range(GK))
+        for g in range(GK):
+            group_amp(0, g)
+        spread_rows(0)
+        warm_up(2)
         deal_scales(0)
-        transpose_amp(0, 1)
-        spread_recip(3, recip_banks[3])
-        warm_up(2, ring_bank(), (warm_codes[:], warm_scales[:]))
-        group_amp(0, 1)
-        group_amp(0, 0)
-        group_amp(1, 0)
-        group_amp(1, 1)
-        deal_words(0)
-        quantize_amp(0)
-        quantize_amp(1)
-        sort_amp(2, nc.scalar.copy)
-        sort_amp(3, nc.scalar.copy)
-        deal_words(1)
+        deal_words(0, 0, vcopy)
+        for g in range(GK):
+            quantize_amp(0, g, 1)
+        deal_words(0, 1, vcopy)
+        keep_recip(0)
+        sort_amp(2, scopy)
         deal_scales(1)
+        deal_words(1, 0, vcopy)
         for b in range(2):
             couple(0, b)
             square(0, b)
-        transpose_amp(2, 3)
-        spread_rows(1)
-        group_amp(2, 1)
-        group_amp(2, 0)
+        transpose_amp(1, range(GK))
+        for g in range(GK):
+            group_amp(1, g)
         cube(0, 0)
+        deal_words(1, 1, vcopy)
         cube(0, 1)
+        quantize_amp(1, 0, 1)
+        group_h(0, vcopy, 0, PAIR)
+        sort_amp(4, scopy)
         couple(1, 0)
-        group_amp(3, 0)
-        group_amp(3, 1)
         square(1, 0)
         couple(1, 1)
         square(1, 1)
-        keep_recip(1)
-        quantize_amp(2)
-        group_h(0, nc.vector.tensor_copy, 0, PAIR)
-        quantize_amp(3)
+        quantize_amp(1, 1, 2)
         cube(1, 0)
         quantize_h(0, 0, PAIR)
         cube(1, 1)
-        couple(2, 0)
-        couple(2, 1)
-        group_h(1, nc.vector.tensor_copy, 0, P)
-        square(2, 0)
-        group_h(1, nc.scalar.copy, P, PAIR)
-        square(2, 1)
-        force(0, 0, (0,))
-        force(0, 1, (0,))
-        spread_rows(2)
-        keep_recip(2)
-        sort_amp(4, nc.scalar.copy)
-        sort_amp(5, nc.scalar.copy)
-        quantize_h(0, PAIR, PAIR + P)
-        cube(2, 0)
-        quantize_h(0, PAIR + P, 2 * PAIR)
-        force(0, 0, (1,))
-        force(0, 1, (1,))
-        add_slow(0, 0)
-        add_slow(0, 1)
-        damp_pool(0, 0, HALF)
-        store_y(0, 0, HALF)
-        cube(2, 1)
-        force(0, 3)
-        add_slow(0, 3)
-        force(0, 2)
-        add_slow(0, 2)
+        transpose_amp(2, range(GK))
+        spread_rows(1)
+        for g in range(GK):
+            group_amp(2, g)
+        quantize_amp(2, 0, 1)
+        group_h(1, vcopy, 0, PAIR)
+        quantize_amp(2, 1, 1)
+        quantize_h(0, PAIR, 2 * PAIR)
+        quantize_amp(2, 2, 1)
         for b in range(2):
-            couple(3, b)
-            square(3, b)
-            if b == 0:
-                group_h(2, nc.scalar.copy, G2, PAIR)
-        group_h(2, pool_copy, 0, G2)
-        damp_from_bank(0, 3)
-        store_y(0, 3 * BANK, N)
-        load_slow(3, 2)
-        transpose_amp(4, 5)
-        group_amp(4, 1)
-        group_amp(4, 0)
-        group_amp(5, 0, GATES[0])
-        group_amp(5, 1)
-        cube(3, 0)
-        cube(3, 1)
-        force(1, 0)
-        quantize_amp(4)
-        group_h(3, nc.vector.tensor_copy, 0, V3)
-        if V3 < PAIR:
-            group_h(3, nc.scalar.copy, V3, PAIR)
-        quantize_amp(5)
-        quantize_h(1)
-        add_slow(1, 0)
-        round_y(0, 0, HALF)
-        round_y(0, 3 * BANK, N)
+            couple(2, b)
+            square(2, b)
+        keep_recip(1)
 
-        for s in range(1, TILES - 3):
-            gate_third(s - 1, GATES[s - 1])
-            damp_pool(s - 1, HALF, 3 * BANK)
-            store_y(s - 1, HALF, 3 * BANK)
-            for j in (0, 1, 3, 2):
-                if (s, j) != (1, 0):
-                    force(s, j)
-                    add_slow(s, j)
-            damp_pool(s, 0, HALF)
-            store_y(s, 0, HALF)
-            damp_from_bank(s, 3)
-            store_y(s, 3 * BANK, N)
-            if s == 1:
-                load_slow(5, 3)
+        for c in range(PAIRS - 1):
+            i, n = 2 * c, 2 * c + 2
+            if c > 0:
+                damp_pool(i - 1, 1, 2, ("h_grouped1", "y_grouped02")[c - 1])
+                store_y(i - 1, 1, 2)
+                round_y(i - 2, 0, GN)
+                round_y(i - 1, 0, 1)
+                round_y(i - 1, 3, 1)
+            cube(n, 0)
+            for f in range(GF):
+                for j in range(3):
+                    force(i, j, (f,))
+            if c == 0:
+                spread_rows(2)
+                spread_recip(GN - 1, recip_banks[GN - 1])
+                keep_recip(2)
+            for j in range(3):
+                add_slow(i, j)
+            damp_pool(i, 0, 3)
+            cube(n, 1)
+            force(i, 3)
+            add_slow(i, 3)
+            if c > 0:
+                round_y(i - 1, 1, 2)
+            group_h(n, scopy, 0, PAIR)
+            if c == 0:
+                sort_amp(6, scopy)
+            for j in (0, 3, 1, 2):
+                force(i + 1, j)
+                add_slow(i + 1, j)
+                if j == 0:
+                    damp_vector(i, 3)
+            store_y(i, 0, GN)
+            if c == 0:
+                load_slow(4, 4)
+            damp_pool(i + 1, 0, 1)
+            store_y(i + 1, 0, 1)
+            if c < PAIRS - 2:
+                damp_vector(i + 1, 3)
+                store_y(i + 1, 3, 1)
             for b in range(2):
-                couple(s + 3, b)
-                square(s + 3, b)
-                cube(s + 3, b)
-            if s == 4:
-                round_y(s - 1, HALF, 3 * BANK)
-            if live(s + 5):
-                transpose_amp(s + 5)
-            if s == 3:
-                transpose_y(1, 0)
-            if live(s - 2):
-                transpose_y(s - 2, 1)
-            if s != 2:
-                transpose_y(s - 1, 0)
-            if s == 4:
-                force(5, 0)
-                force(5, 1)
-                transpose_y(s - 1, 1)
-            if live(s + 5):
+                couple(n + 1, b)
+                square(n + 1, b)
+                cube(n + 1, b)
+            for g in range(GK if c == 0 else GN):
+                if c == 0:
+                    transpose_amp(3, (g,))
+                    group_amp(3, g)
+                else:
+                    transpose_y(c - 1, g)
+                    group_y(c - 1, g)
+                if g == 2 and SHARE[c] < PAIR:
+                    group_h(n + 1, scopy, SHARE[c], PAIR)
+            if c == PAIRS - 2:
+                round_y(i, 0, GN)
+            if c < PAIRS - 2:
                 for b in range(2):
-                    group_amp(s + 5, b, GATES[s])
-            if s == 3:
-                group_y(1, 0)
-            if live(s - 2):
-                group_y(s - 2, 1)
-            if s != 2:
-                group_y(s - 1, 0)
-            if s == 4:
-                group_y(s - 1, 1)
-            if s % 2 == 0:
-                quantize_h(s // 2 + 1, 0, PAIR)
-                group_h(s + 3, nc.vector.tensor_copy, 0, PAIR if s == 2 else V7)
-                if s == 4 and V7 < PAIR:
-                    group_h(s + 3, nc.scalar.copy, V7, PAIR)
-            if live(s + 5):
-                quantize_amp(s + 5)
-            if s == 4:
-                quantize_y(1)
-                store_codes(1)
-                store_scales([nc.sync], slice(0, 4 * P))
-            if s % 2 == 0:
-                quantize_h(s // 2 + 1, PAIR)
-            if s == 3:
-                quantize_y(0)
-                store_codes(0)
-            if s % 2 == 1:
-                group_h(s + 3, nc.vector.tensor_copy, 0, VI[s])
-            if s != 4:
-                round_y(s - 1, HALF, 3 * BANK)
-            round_y(s, 0, HALF)
-            round_y(s, 3 * BANK, N)
-            if s % 2 == 1 and VI[s] < PAIR:
-                group_h(s + 3, nc.scalar.copy, VI[s], PAIR)
+                    couple(n + 2, b)
+                    square(n + 2, b)
+            quantize_h(c + 1, 0, PAIR)
+            group_h(n + 1, vcopy, 0, SHARE[c])
+            if c == 0:
+                quantize_amp(3, 0, 2)
+                quantize_h(c + 1, PAIR, 2 * PAIR)
+                quantize_amp(3, 2, 1)
+            else:
+                quantize_y(c - 1, (0,))
+                quantize_h(c + 1, PAIR, 2 * PAIR)
+                quantize_y(c - 1, (1, 2, 3))
+                store_codes(c - 1, 0, GN)
+        store_scales([nc.sync], slice(0, 2 * PAIR))
 
-        gate_third(4, GATES[4])
-        damp_pool(4, HALF, 3 * BANK)
-        store_y(4, HALF, 3 * BANK)
-        add_slow(5, 0)
-        add_slow(5, 1)
-        for j in (3, 2):
-            force(5, j)
-            add_slow(5, j)
-        force(6, 0)
-        force(6, 1)
-        transpose_y(4, 0)
+        damp_pool(5, 1, 2, "y_grouped12")
+        damp_vector(5, 3)
+        store_y(5, 3, 1)
+        store_y(5, 1, 2)
+        round_y(5, 0, 1)
+        round_y(5, 3, 1)
         recip_banks[2] = ring_bank(hold=True)
         spread_recip(2, recip_banks[2])
-        group_y(4, 0)
-        round_y(4, HALF, 3 * BANK)
-        damp_pool(5, 0, HALF)
-        store_y(5, 0, HALF)
-        damp_from_bank(5, 3)
-        damp_pool(5, HALF, 3 * BANK)
-        store_y(5, HALF, N)
-        for j in range(GN):
-            if j > 1:
-                force(6, j)
-            add_slow(6, j)
-        transpose_y(4, 1)
-        round_y(5, 3 * BANK, N)
-        group_y(4, 1)
-        round_y(5, 0, HALF)
-        round_y(5, HALF, 3 * BANK)
-        recip_banks[1] = ring_bank(hold=True)
-        spread_recip(1, recip_banks[1])
-        damp_pool(6, 0, HALF)
-        damp_from_bank(6, 2)
-        damp_from_bank(6, 3)
-        store_y(6, HALF, N)
-        store_y(6, 0, HALF)
-        last = TILES - 1
-        for j in (0, 1, 2):
-            force(7, j)
-            add_slow(7, j)
-        transpose_y(5, 0)
-        group_y(5, 0)
+        first = ((6, 0), (7, 0), (6, 3))
+        for f in range(GF):
+            for i, j in first:
+                force(i, j, (f,))
         force(7, 3)
-        add_slow(7, 3)
-        round_y(6, HALF, N)
-        transpose_y(5, 1)
-        group_y(5, 1)
-        round_y(6, 0, HALF)
-        damp_pool(last, 0, BANK)
-        round_pool(last, 0, BANK)
-        damp_from_bank(last, 1)
-        store_y(last, 0, HALF)
-        damp_from_bank(last, 2)
-        damp_from_bank(last, 3)
-        store_y(last, HALF, N)
-        round_vector(last, BANK, HALF)
-        round_vector(last, HALF, N)
-        transpose_y(6, 1)
-        group_y(6, 1)
-        transpose_y(6, 0)
-        group_y(6, 0)
-        quantize_y(2, (0, 1))
-        store_codes(2, 0, 2)
-        quantize_y(2, (2, 3))
-        store_codes(2, 2, 4)
-        transpose_y(last, 0)
-        group_y(last, 0)
-        transpose_y(last, 1)
-        group_y(last, 1)
-        quantize_y(3, (0, 1))
-        store_codes(3, 0, 2)
-        quantize_y(3, (2, 3))
-        store_codes(3, 2, 4)
-        store_scales([nc.scalar, nc.sync], slice(4 * P, M))
+        for j in (0, 3):
+            for i in (6, 7):
+                add_slow(i, j)
+        damp_pool_last(0)
+        force(6, 1)
+        add_slow(6, 1)
+        for g in (0, 3):
+            transpose_y(2, g)
+            group_y(2, g)
+        damp_vector(6, 3)
+        force(7, 1)
+        add_slow(7, 1)
+        damp_pool_last(1)
+        damp_vector(7, 3)
+        store_last(3)
+        store_last(0)
+        round_y(5, 1, 2)
+        for i in (6, 7):
+            force(i, 2)
+            add_slow(i, 2)
+        store_last(1)
+        for g in (1, 2):
+            transpose_y(2, g)
+        round_last(3)
+        round_last(0)
+        for g in (1, 2):
+            group_y(2, g)
+        for i in (6, 7):
+            damp_vector(i, 2)
+        store_last(2)
+        for g in (3, 0):
+            transpose_y(last, g)
+            group_y(last, g)
+        round_last(1, vcopy)
+        round_last(2, vcopy)
+        quantize_y(2, (0, 3, 1, 2))
+        store_codes(2, 0, GN)
+        for g in (1, 2):
+            transpose_y(last, g)
+            group_y(last, g)
+        quantize_y(last, (3, 0, 1))
+        store_codes(last, 0, 2)
+        quantize_y(last, (2,))
+        store_codes(last, 2, 2)
+        store_scales([nc.scalar, nc.sync], slice(2 * PAIR, M))

@@ -134,7 +134,10 @@ def tile_cubic_ocean_mode_step_h1_kernel(
 
         def sort_amp(i, copy):
             a_sorted[i] = named("a_sorted%d" % (i % 2), [P, GK, 2, P], F32)
-            copy(out=a_sorted[i][:], in_=amp_sb[i][:].bitcast(F32).rearrange("m (g p u) -> m g u p", p=P, u=2))
+            copy(
+                out=a_sorted[i][:].rearrange("m g u p -> m g p u"),
+                in_=amp_sb[i][:].bitcast(F32).rearrange("m (g p u) -> m g p u", p=P, u=2),
+            )
 
         def transpose_amp(c, groups):
             for g in groups:
@@ -274,21 +277,22 @@ def tile_cubic_ocean_mode_step_h1_kernel(
         def store_y(i, g, count):
             nc.sync.dma_start(out=out_0[rows(i), cols(g, count)], in_=y_part(i, g, count))
 
-        def pairs_of(c):
-            if c not in y_pairs:
-                y_pairs[c] = work.tile([P, GN, 2, 2, P, 2], BF16, align_bytes=64, name="y_pairs")
-            return y_pairs[c]
+        def round_copy(out, in_):
+            nc.scalar.activation(out=out, in_=in_, func=ACT.Copy)
 
-        def round_y(i, g, count, copy=nc.scalar.copy):
-            copy(
-                out=pairs_of(i // 2)[:, g : g + count, i % 2, :, :, :],
-                in_=y_part(i, g, count).rearrange("m (g w u e) -> m g u w e", u=2, e=2, w=P),
+        def round_y(i, g, count):
+            if i not in y_pairs:
+                y_pairs[i] = named("y_pairs%d" % (i % 4), [P, 2, N // 4, 2], BF16)
+            round_copy(
+                out=y_pairs[i][:, :, g * P : (g + count) * P, :].rearrange("m u w e -> m w u e"),
+                in_=y_part(i, g, count).rearrange("m (w u e) -> m w u e", u=2, e=2),
             )
 
-        def round_last(g, copy=nc.scalar.copy):
+        def round_last(g, copy=round_copy):
+            last_pairs[g] = named("last_pairs%d" % g, [P, 2, PAIR, 2], BF16)
             copy(
-                out=pairs_of(last)[:, g, :, :, :, :],
-                in_=last_sums[g][:].rearrange("m h (w u e) -> m h u w e", u=2, e=2),
+                out=last_pairs[g][:].rearrange("m u w e -> m w u e"),
+                in_=last_sums[g][:].rearrange("m h (w u e) -> m (h w) u e", u=2, e=2),
             )
 
         def store_last(g):
@@ -299,9 +303,10 @@ def tile_cubic_ocean_mode_step_h1_kernel(
         def transpose_y(c, g):
             y_banks[c, g] = ring_bank()
             for h in range(2):
-                words = y_pairs[c][:, g, h, :, :, :].rearrange("m u w e -> m u (w e)").bitcast(F32)
+                pairs, at = (last_pairs[g], h) if c == last else (y_pairs[2 * c + h], g)
+                words = pairs[:].rearrange("m u w e -> m u (w e)").bitcast(F32)
                 for u in range(2):
-                    nc.tensor.transpose(y_banks[c, g][:, rows(2 * h + u)], words[:, u, :], ident[:])
+                    nc.tensor.transpose(y_banks[c, g][:, rows(2 * h + u)], words[:, u, rows(at)], ident[:])
 
         def group_y(c, g, copy=nc.scalar.copy):
             y_grouped[c, g] = named("y_grouped%d%d" % (c % 2, g), [P, 2 * BANK], BF16)
@@ -348,7 +353,7 @@ def tile_cubic_ocean_mode_step_h1_kernel(
                     stop=True,
                 )
 
-        last, last_sums = PAIRS - 1, {}
+        last, last_sums, last_pairs = PAIRS - 1, {}, {}
         vcopy, scopy = nc.vector.tensor_copy, nc.scalar.copy
 
         for f in range(GF):

@@ -64,16 +64,17 @@ def tile_cubic_ocean_mode_step_h1_kernel(
         b_words = [named("b_words%d" % h, [P, GF, N], U8) for h in range(2)]
         b_scales = named("b_scales", [P, GF, N], U8)
         cubic_sb = named("cubic_sb", [P, GF, 4], BF16)
-        drag_sb = named("drag_sb", [P, GN, 4], BF16)
-        denom = named("denom", [P, GN, 4], F32)
+        drag_rows = named("drag_rows", [P, P], BF16)
+        denom_rows = named("denom_rows", [P, P], F32)
         recip = named("recip", [P, GN, 4], F32)
+        recip_blocks = named("recip_blocks", [P, P], F32)
         recip_rows = named("recip_rows", [P, 3 * BANK], F32)
         ident = named("ident", [P, P], F32)
         y_scales = named("y_scales", [P, GN, M], U8)
         warm_codes = named("warm_codes", [P, P], U32)
         warm_scales = named("warm_scales", [P, P], U8)
         recip_banks = {GN - 1: psum.tile([P, BANK], F32, name="recip_bank")}
-        amp_sb, slow_sb, spreads, a_sorted = {}, {}, {}, {}
+        amp_sb, slow_sb, a_sorted = {}, {}, {}
         a_banks, a_grouped, a_codes, a_scales = {}, {}, {}, {}
         u_banks, squares, h_slots, h_grouped, h_codes, h_scales = {}, {}, {}, {}, {}, {}
         e_banks, sums, moved, y_pairs, y_banks, y_grouped, y_codes = {}, {}, {}, {}, {}, {}, {}
@@ -93,7 +94,7 @@ def tile_cubic_ocean_mode_step_h1_kernel(
             )
 
         def load_amp(i):
-            amp_sb[i] = named("amp%d" % (i % 6), [P, K], BF16)
+            amp_sb[i] = named("amp%d" % (i % 5), [P, K], BF16)
             nc.sync.dma_start(out=amp_sb[i][:], in_=amp[rows(i), :])
 
         def load_slow(first, count):
@@ -122,16 +123,6 @@ def tile_cubic_ocean_mode_step_h1_kernel(
             for t in range(4):
                 nc.tensor.transpose(bank[:, rows(t)], recip[:, g, t : t + 1].to_broadcast([P, P]), ident[:])
 
-        def natural(bank):
-            return bank[:].rearrange("m (t p) -> m p t", t=4)
-
-        def spread_rows(g):
-            spreads[g] = ring_bank()
-            spread_recip(g, spreads[g])
-
-        def keep_recip(g):
-            nc.scalar.copy(out=recip_rows[:, cols(g)].rearrange("m (p t) -> m p t", t=4), in_=natural(spreads[g]))
-
         def sort_amp(i, copy):
             a_sorted[i] = named("a_sorted%d" % (i % 2), [P, GK, 2, P], F32)
             copy(
@@ -139,16 +130,15 @@ def tile_cubic_ocean_mode_step_h1_kernel(
                 in_=amp_sb[i][:].bitcast(F32).rearrange("m (g p u) -> m g p u", p=P, u=2),
             )
 
-        def transpose_amp(c, groups):
-            for g in groups:
-                a_banks[c, g] = ring_bank()
-            for h in range(2):
+        def transpose_amp(c, groups, tiles=range(2)):
+            for g, h in [(g, h) for g in groups for h in tiles]:
+                if (c, g) not in a_banks:
+                    a_banks[c, g] = ring_bank()
                 i = 2 * c + h
                 words = amp_sb[i][:].bitcast(F32)
-                for g in groups:
-                    for u in range(2):
-                        source = a_sorted[i][:, g, u, :] if i in a_sorted else words[:, PAIR * g + u : PAIR * (g + 1) : 2]
-                        nc.tensor.transpose(a_banks[c, g][:, rows(2 * h + u)], source, ident[:])
+                for u in range(2):
+                    source = a_sorted[i][:, g, u, :] if i in a_sorted else words[:, PAIR * g + u : PAIR * (g + 1) : 2]
+                    nc.tensor.transpose(a_banks[c, g][:, rows(2 * h + u)], source, ident[:])
 
         def group_amp(c, g):
             if c not in a_grouped:
@@ -271,8 +261,8 @@ def tile_cubic_ocean_mode_step_h1_kernel(
             nc.gpsimd.tensor_tensor(out=part, in0=part, in1=factors, op=ALU.mult)
 
         def damp_vector(i, g):
-            part = y_part(i, g, 1).rearrange("m (p t) -> m p t", t=4)
-            nc.vector.tensor_tensor(out=part, in0=part, in1=natural(recip_banks[g]), op=ALU.mult)
+            part = y_part(i, g, 1)
+            nc.vector.tensor_tensor(out=part, in0=part, in1=recip_banks[g][:], op=ALU.mult)
 
         def store_y(i, g, count):
             nc.sync.dma_start(out=out_0[rows(i), cols(g, count)], in_=y_part(i, g, count))
@@ -334,10 +324,9 @@ def tile_cubic_ocean_mode_step_h1_kernel(
                     in_=y_grouped[c, g][:],
                 )
 
-        def store_codes(c, first, count):
+        def store_codes(c, groups):
             nc.sync.dma_start(
-                out=out_words[:, first : first + count, c * PAIR : (c + 1) * PAIR],
-                in_=y_codes[c][:, first : first + count, :].bitcast(I32),
+                out=out_words[:, groups, c * PAIR : (c + 1) * PAIR], in_=y_codes[c][:, groups, :].bitcast(I32)
             )
 
         def warm_up(count):
@@ -356,46 +345,56 @@ def tile_cubic_ocean_mode_step_h1_kernel(
         last, last_sums, last_pairs = PAIRS - 1, {}, {}
         vcopy, scopy = nc.vector.tensor_copy, nc.scalar.copy
 
+        nc.vector.memset(drag_rows[:].bitcast(I32), 0)
         for f in range(GF):
             nc.vector.memset(c_raw_scales[f][:].bitcast(I32), 0)
         nc.vector.memset(b_scales[:].bitcast(I32), 0)
         make_identity(nc, ident[:])
 
-        nc.sync.dma_start(out=drag_sb[:], in_=drag.rearrange("(g p t) -> p g t", p=P, t=4))
         load_amp(0)
+        nc.sync.dma_start(out=drag_rows[: N // P, :], in_=drag.rearrange("(j p) -> j p", p=P))
         load_amp(1)
         load_scales(c_raw_scales[0], coup_scales[:, :, cols(0)])
         load_words(c_raw_words, coup_words, 0)
-        load_scales(c_raw_scales[1], coup_scales[:, :, cols(1)])
         load_amp(2)
+        load_amp(3)
+        load_scales(c_raw_scales[1], coup_scales[:, :, cols(1)])
         nc.sync.dma_start(out=cubic_sb[:], in_=cubic.rearrange("(g p t) -> p g t", p=P, t=4))
         load_words(c_raw_words, coup_words, 1)
-        for i in (3, 4, 5):
+        nc.vector.tensor_scalar(out=denom_rows[:], in0=drag_rows[:], scalar1=1.0, scalar2=None, op0=ALU.add)
+        nc.vector.quantize_mx(out=warm_codes[:].bitcast(FP8X4), scales=warm_scales[:], in_=amp_sb[0][:, :BANK])
+        nc.vector.reciprocal(out=recip_blocks[:], in_=denom_rows[:])
+        parked = out_0[M - 1, :]
+        nc.sync.dma_start(out=parked.rearrange("(j p) -> j p", p=P), in_=recip_blocks[: N // P, :])
+        for i in (4, 5):
             load_amp(i)
         load_scales(b_scales, forc_scales)
         load_words(b_words, forc_words, 0)
         load_slow(0, 1)
         load_words(b_words, forc_words, 1)
+        nc.sync.dma_start(out=recip_rows[:], in_=parked[: 3 * BANK].partition_broadcast(P))
         load_slow(1, 1)
         load_amp(6)
         load_amp(7)
         load_slow(2, 2)
 
-        nc.vector.tensor_scalar(out=denom[:], in0=drag_sb[:], scalar1=1.0, scalar2=None, op0=ALU.add)
-        nc.vector.reciprocal(out=recip[:], in_=denom[:])
-        nc.vector.quantize_mx(out=warm_codes[:].bitcast(FP8X4), scales=warm_scales[:], in_=amp_sb[0][:, :BANK])
-        transpose_amp(0, range(GK))
-        for g in range(GK):
-            group_amp(0, g)
-        spread_rows(0)
+        transpose_amp(0, range(GK), (0,))
+        transpose_amp(0, range(GK), (1,))
+        recip_bank = ring_bank()
+        nc.tensor.transpose(recip_bank[:, :P], recip_blocks[:], ident[:])
+        group_amp(0, 0)
+        group_amp(0, 1)
+        nc.scalar.copy(out=recip[:].rearrange("p g t -> p (g t)"), in_=recip_bank[:, : N // P])
+        group_amp(0, 2)
         warm_up(2)
+        spread_recip(GN - 1, recip_banks[GN - 1])
         deal_scales(0)
         deal_words(0, 0, vcopy)
         for g in range(GK):
             quantize_amp(0, g, 1)
         deal_words(0, 1, vcopy)
-        keep_recip(0)
         sort_amp(2, scopy)
+        sort_amp(3, scopy)
         deal_scales(1)
         deal_words(1, 0, vcopy)
         for b in range(2):
@@ -409,7 +408,6 @@ def tile_cubic_ocean_mode_step_h1_kernel(
         cube(0, 1)
         quantize_amp(1, 0, 1)
         group_h(0, vcopy, 0, PAIR)
-        sort_amp(4, scopy)
         couple(1, 0)
         square(1, 0)
         couple(1, 1)
@@ -419,7 +417,6 @@ def tile_cubic_ocean_mode_step_h1_kernel(
         quantize_h(0, 0, PAIR)
         cube(1, 1)
         transpose_amp(2, range(GK))
-        spread_rows(1)
         for g in range(GK):
             group_amp(2, g)
         quantize_amp(2, 0, 1)
@@ -430,7 +427,8 @@ def tile_cubic_ocean_mode_step_h1_kernel(
         for b in range(2):
             couple(2, b)
             square(2, b)
-        keep_recip(1)
+        cube(2, 0)
+        cube(2, 1)
 
         for c in range(PAIRS - 1):
             i, n = 2 * c, 2 * c + 2
@@ -440,18 +438,15 @@ def tile_cubic_ocean_mode_step_h1_kernel(
                 round_y(i - 2, 0, GN)
                 round_y(i - 1, 0, 1)
                 round_y(i - 1, 3, 1)
-            cube(n, 0)
+                cube(n, 0)
             for f in range(GF):
                 for j in range(3):
                     force(i, j, (f,))
-            if c == 0:
-                spread_rows(2)
-                spread_recip(GN - 1, recip_banks[GN - 1])
-                keep_recip(2)
             for j in range(3):
                 add_slow(i, j)
             damp_pool(i, 0, 3)
-            cube(n, 1)
+            if c > 0:
+                cube(n, 1)
             force(i, 3)
             add_slow(i, 3)
             if c > 0:
@@ -459,6 +454,7 @@ def tile_cubic_ocean_mode_step_h1_kernel(
             group_h(n, scopy, 0, PAIR)
             if c == 0:
                 sort_amp(6, scopy)
+                sort_amp(7, scopy)
             for j in (0, 3, 1, 2):
                 force(i + 1, j)
                 add_slow(i + 1, j)
@@ -501,7 +497,7 @@ def tile_cubic_ocean_mode_step_h1_kernel(
                 quantize_y(c - 1, (0,))
                 quantize_h(c + 1, PAIR, 2 * PAIR)
                 quantize_y(c - 1, (1, 2, 3))
-                store_codes(c - 1, 0, GN)
+                store_codes(c - 1, slice(0, GN))
         store_scales([nc.sync], slice(0, 2 * PAIR))
 
         damp_pool(5, 1, 2, "y_grouped12")
@@ -512,12 +508,12 @@ def tile_cubic_ocean_mode_step_h1_kernel(
         round_y(5, 3, 1)
         recip_banks[2] = ring_bank(hold=True)
         spread_recip(2, recip_banks[2])
-        first = ((6, 0), (7, 0), (6, 3))
+        first = ((6, 0), (7, 0), (6, 2))
         for f in range(GF):
             for i, j in first:
                 force(i, j, (f,))
-        force(7, 3)
-        for j in (0, 3):
+        force(7, 2)
+        for j in (0, 2):
             for i in (6, 7):
                 add_slow(i, j)
         damp_pool_last(0)
@@ -526,39 +522,41 @@ def tile_cubic_ocean_mode_step_h1_kernel(
         for g in (0, 3):
             transpose_y(2, g)
             group_y(2, g)
-        damp_vector(6, 3)
+        damp_vector(6, 2)
         force(7, 1)
         add_slow(7, 1)
         damp_pool_last(1)
-        damp_vector(7, 3)
-        store_last(3)
+        damp_vector(7, 2)
+        store_last(2)
         store_last(0)
         round_y(5, 1, 2)
         for i in (6, 7):
-            force(i, 2)
-            add_slow(i, 2)
+            force(i, 3)
+            add_slow(i, 3)
         store_last(1)
         for g in (1, 2):
             transpose_y(2, g)
-        round_last(3)
+        round_last(2)
         round_last(0)
         for g in (1, 2):
             group_y(2, g)
         for i in (6, 7):
-            damp_vector(i, 2)
-        store_last(2)
-        for g in (3, 0):
+            damp_vector(i, 3)
+        store_last(3)
+        for g in (2, 0):
             transpose_y(last, g)
             group_y(last, g)
         round_last(1, vcopy)
-        round_last(2, vcopy)
-        quantize_y(2, (0, 3, 1, 2))
-        store_codes(2, 0, GN)
-        for g in (1, 2):
+        round_last(3, vcopy)
+        quantize_y(2, (0, 3))
+        store_codes(2, slice(0, GN, 3))
+        quantize_y(2, (1, 2))
+        store_codes(2, slice(1, 3))
+        for g in (1, 3):
             transpose_y(last, g)
             group_y(last, g)
-        quantize_y(last, (3, 0, 1))
-        store_codes(last, 0, 2)
-        quantize_y(last, (2,))
-        store_codes(last, 2, 2)
-        store_scales([nc.scalar, nc.sync], slice(2 * PAIR, M))
+        quantize_y(last, (2, 0, 1))
+        store_codes(last, slice(0, 3))
+        quantize_y(last, (3,))
+        store_scales([nc.scalar], slice(2 * PAIR, M))
+        store_codes(last, slice(3, GN))

@@ -26,7 +26,8 @@ GK = K // BANK
 GF = F // BANK
 GN = N // BANK
 RING = 7
-SHARE = (128, 256, 256)
+POOL_END = 1536
+SHARE = (192, 256, 256)
 
 
 def tile_cubic_ocean_mode_step_h1_kernel(
@@ -68,7 +69,7 @@ def tile_cubic_ocean_mode_step_h1_kernel(
         denom_rows = named("denom_rows", [P, P], F32)
         recip = named("recip", [P, GN, 4], F32)
         recip_blocks = named("recip_blocks", [P, P], F32)
-        recip_rows = named("recip_rows", [P, 3 * BANK], F32)
+        recip_rows = named("recip_rows", [P, POOL_END], F32)
         ident = named("ident", [P, P], F32)
         y_scales = named("y_scales", [P, GN, M], U8)
         warm_codes = named("warm_codes", [P, P], U32)
@@ -228,54 +229,53 @@ def tile_cubic_ocean_mode_step_h1_kernel(
                     stop=(f == GF - 1),
                 )
 
-        def sum_part(i, g, count):
+        def sum_part(i, lo, hi):
             if i < 2 * last:
                 if i not in sums:
                     sums[i] = named("sums%d" % (i % 4), [P, N], F32)
-                return sums[i][:, cols(g, count)]
+                return sums[i][:, lo:hi]
+            g = lo // BANK
             if g not in last_sums:
                 last_sums[g] = named("last_sums%d" % g, [P, 2, BANK], F32)
             return last_sums[g][:, i % 2, :]
 
         def add_slow(i, j):
-            nc.vector.tensor_tensor(out=sum_part(i, j, 1), in0=e_banks[i, j][:], in1=slow_sb[i][:, cols(j)], op=ALU.add)
-
-        def y_part(i, g, count):
-            if (i, g) in moved:
-                return moved[i, g][:]
-            return sum_part(i, g, count)
-
-        def damp_pool(i, g, count, into=None):
-            if into is not None:
-                moved[i, g] = named(into, [P, count * BANK], F32)
-            nc.gpsimd.tensor_tensor(
-                out=y_part(i, g, count),
-                in0=sum_part(i, g, count),
-                in1=recip_rows[:, cols(g, count)],
-                op=ALU.mult,
+            nc.vector.tensor_tensor(
+                out=sum_part(i, j * BANK, (j + 1) * BANK), in0=e_banks[i, j][:], in1=slow_sb[i][:, cols(j)], op=ALU.add
             )
+
+        def y_part(i, lo, hi):
+            if (i, lo) in moved:
+                return moved[i, lo][:]
+            return sum_part(i, lo, hi)
+
+        def damp_pool(i, lo, hi, into=None):
+            if into is not None:
+                moved[i, lo] = named(into, [P, hi - lo], F32)
+            nc.gpsimd.tensor_tensor(out=y_part(i, lo, hi), in0=sum_part(i, lo, hi), in1=recip_rows[:, lo:hi], op=ALU.mult)
 
         def damp_pool_last(g):
             part = last_sums[g][:]
             factors = recip_rows[:, cols(g)].unsqueeze(1).to_broadcast([P, 2, BANK])
             nc.gpsimd.tensor_tensor(out=part, in0=part, in1=factors, op=ALU.mult)
 
-        def damp_vector(i, g):
-            part = y_part(i, g, 1)
-            nc.vector.tensor_tensor(out=part, in0=part, in1=recip_banks[g][:], op=ALU.mult)
+        def damp_vector(i, lo, hi):
+            part = y_part(i, lo, hi)
+            g = lo // BANK
+            nc.vector.tensor_tensor(out=part, in0=part, in1=recip_banks[g][:, lo - g * BANK :], op=ALU.mult)
 
-        def store_y(i, g, count):
-            nc.sync.dma_start(out=out_0[rows(i), cols(g, count)], in_=y_part(i, g, count))
+        def store_y(i, lo, hi):
+            nc.sync.dma_start(out=out_0[rows(i), lo:hi], in_=y_part(i, lo, hi))
 
         def round_copy(out, in_):
             nc.scalar.activation(out=out, in_=in_, func=ACT.Copy)
 
-        def round_y(i, g, count):
+        def round_y(i, lo, hi):
             if i not in y_pairs:
                 y_pairs[i] = named("y_pairs%d" % (i % 4), [P, 2, N // 4, 2], BF16)
             round_copy(
-                out=y_pairs[i][:, :, g * P : (g + count) * P, :].rearrange("m u w e -> m w u e"),
-                in_=y_part(i, g, count).rearrange("m (w u e) -> m w u e", u=2, e=2),
+                out=y_pairs[i][:, :, lo // 4 : hi // 4, :].rearrange("m u w e -> m w u e"),
+                in_=y_part(i, lo, hi).rearrange("m (w u e) -> m w u e", u=2, e=2),
             )
 
         def round_last(g, copy=round_copy):
@@ -372,9 +372,10 @@ def tile_cubic_ocean_mode_step_h1_kernel(
         load_words(b_words, forc_words, 0)
         load_slow(0, 1)
         load_words(b_words, forc_words, 1)
-        nc.sync.dma_start(out=recip_rows[:], in_=parked[: 3 * BANK].partition_broadcast(P))
+        nc.sync.dma_start(out=recip_rows[:, :BANK], in_=parked[:BANK].partition_broadcast(P))
         load_slow(1, 1)
         load_amp(6)
+        nc.sync.dma_start(out=recip_rows[:, BANK:], in_=parked[BANK:POOL_END].partition_broadcast(P))
         load_amp(7)
         load_slow(2, 2)
 
@@ -416,65 +417,76 @@ def tile_cubic_ocean_mode_step_h1_kernel(
         cube(1, 0)
         quantize_h(0, 0, PAIR)
         cube(1, 1)
-        transpose_amp(2, range(GK))
-        for g in range(GK):
-            group_amp(2, g)
+        transpose_amp(2, (0, 1))
+        group_amp(2, 0)
+        group_amp(2, 1)
+        couple(2, 0)
+        square(2, 0)
+        transpose_amp(2, (2,))
+        group_amp(2, 2)
+        couple(2, 1)
+        square(2, 1)
         quantize_amp(2, 0, 1)
         group_h(1, vcopy, 0, PAIR)
         quantize_amp(2, 1, 1)
         quantize_h(0, PAIR, 2 * PAIR)
         quantize_amp(2, 2, 1)
-        for b in range(2):
-            couple(2, b)
-            square(2, b)
         cube(2, 0)
         cube(2, 1)
+        ends = (1536,)*6
 
         for c in range(PAIRS - 1):
             i, n = 2 * c, 2 * c + 2
             if c > 0:
-                damp_pool(i - 1, 1, 2, ("h_grouped1", "y_grouped02")[c - 1])
-                store_y(i - 1, 1, 2)
-                round_y(i - 2, 0, GN)
-                round_y(i - 1, 0, 1)
-                round_y(i - 1, 3, 1)
+                damp_pool(i - 1, BANK, ends[i - 1], ("h_grouped1", "y_grouped02")[c - 1])
+                store_y(i - 1, BANK, ends[i - 1])
+                round_y(i - 2, 0, N)
+                round_y(i - 1, 0, BANK)
+                round_y(i - 1, ends[i - 1], N)
                 cube(n, 0)
             for f in range(GF):
                 for j in range(3):
                     force(i, j, (f,))
-            for j in range(3):
+            for j in (0, 2, 1):
                 add_slow(i, j)
-            damp_pool(i, 0, 3)
+            if c == 0:
+                damp_pool(i, 0, BANK)
+            else:
+                damp_pool(i, 0, ends[i])
             if c > 0:
                 cube(n, 1)
             force(i, 3)
             add_slow(i, 3)
             if c > 0:
-                round_y(i - 1, 1, 2)
+                round_y(i - 1, BANK, ends[i - 1])
             group_h(n, scopy, 0, PAIR)
-            if c == 0:
-                sort_amp(6, scopy)
-                sort_amp(7, scopy)
             for j in (0, 3, 1, 2):
                 force(i + 1, j)
                 add_slow(i + 1, j)
                 if j == 0:
-                    damp_vector(i, 3)
-            store_y(i, 0, GN)
+                    damp_vector(i, ends[i], N)
             if c == 0:
+                damp_pool(i + 1, 0, BANK)
+                damp_pool(i, BANK, ends[i])
+                store_y(i + 1, 0, BANK)
+                store_y(i, 0, N)
                 load_slow(4, 4)
-            damp_pool(i + 1, 0, 1)
-            store_y(i + 1, 0, 1)
+            else:
+                store_y(i, 0, N)
+                damp_pool(i + 1, 0, BANK)
+                store_y(i + 1, 0, BANK)
             if c < PAIRS - 2:
-                damp_vector(i + 1, 3)
-                store_y(i + 1, 3, 1)
+                damp_vector(i + 1, ends[i + 1], N)
+                store_y(i + 1, ends[i + 1], N)
             for b in range(2):
                 couple(n + 1, b)
                 square(n + 1, b)
                 cube(n + 1, b)
+            if c == 0:
+                transpose_amp(3, range(GK), (0,))
             for g in range(GK if c == 0 else GN):
                 if c == 0:
-                    transpose_amp(3, (g,))
+                    transpose_amp(3, (g,), (1,))
                     group_amp(3, g)
                 else:
                     transpose_y(c - 1, g)
@@ -482,7 +494,7 @@ def tile_cubic_ocean_mode_step_h1_kernel(
                 if g == 2 and SHARE[c] < PAIR:
                     group_h(n + 1, scopy, SHARE[c], PAIR)
             if c == PAIRS - 2:
-                round_y(i, 0, GN)
+                round_y(i, 0, N)
             if c < PAIRS - 2:
                 for b in range(2):
                     couple(n + 2, b)
@@ -500,12 +512,12 @@ def tile_cubic_ocean_mode_step_h1_kernel(
                 store_codes(c - 1, slice(0, GN))
         store_scales([nc.sync], slice(0, 2 * PAIR))
 
-        damp_pool(5, 1, 2, "y_grouped12")
-        damp_vector(5, 3)
-        store_y(5, 3, 1)
-        store_y(5, 1, 2)
-        round_y(5, 0, 1)
-        round_y(5, 3, 1)
+        damp_pool(5, BANK, ends[5], "y_grouped12")
+        damp_vector(5, ends[5], N)
+        store_y(5, ends[5], N)
+        store_y(5, BANK, ends[5])
+        round_y(5, 0, BANK)
+        round_y(5, ends[5], N)
         recip_banks[2] = ring_bank(hold=True)
         spread_recip(2, recip_banks[2])
         first = ((6, 0), (7, 0), (6, 2))
@@ -522,18 +534,18 @@ def tile_cubic_ocean_mode_step_h1_kernel(
         for g in (0, 3):
             transpose_y(2, g)
             group_y(2, g)
-        damp_vector(6, 2)
+        damp_vector(6, 2 * BANK, 3 * BANK)
+        store_y(6, 2 * BANK, 3 * BANK)
         force(7, 1)
         add_slow(7, 1)
         damp_pool_last(1)
-        damp_vector(7, 2)
-        store_last(2)
+        damp_vector(7, 2 * BANK, 3 * BANK)
         store_last(0)
-        round_y(5, 1, 2)
+        store_y(7, 2 * BANK, 3 * BANK)
+        round_y(5, BANK, ends[5])
         for i in (6, 7):
             force(i, 3)
             add_slow(i, 3)
-        store_last(1)
         for g in (1, 2):
             transpose_y(2, g)
         round_last(2)
@@ -541,8 +553,10 @@ def tile_cubic_ocean_mode_step_h1_kernel(
         for g in (1, 2):
             group_y(2, g)
         for i in (6, 7):
-            damp_vector(i, 3)
-        store_last(3)
+            damp_vector(i, 3 * BANK, N)
+        store_y(6, 3 * BANK, N)
+        store_last(1)
+        store_y(7, 3 * BANK, N)
         for g in (2, 0):
             transpose_y(last, g)
             group_y(last, g)
@@ -555,8 +569,10 @@ def tile_cubic_ocean_mode_step_h1_kernel(
         for g in (1, 3):
             transpose_y(last, g)
             group_y(last, g)
-        quantize_y(last, (2, 0, 1))
-        store_codes(last, slice(0, 3))
+        quantize_y(last, (2, 0))
+        store_codes(last, slice(0, GN, 2))
+        quantize_y(last, (1,))
+        store_codes(last, slice(1, 2))
         quantize_y(last, (3,))
         store_scales([nc.scalar], slice(2 * PAIR, M))
         store_codes(last, slice(3, GN))

@@ -71,7 +71,8 @@ def tile_cubic_ocean_mode_step_h1_kernel(
         recip_blocks = named("recip_blocks", [P, P], F32)
         recip_rows = named("recip_rows", [P, POOL_END], F32)
         ident = named("ident", [P, P], F32)
-        y_scales = named("y_scales", [P, GN, M], U8)
+        y_scales = [named("y_scales%d" % c, [P, GN, PAIR], U8) for c in range(2)]
+        packed_scales = named("packed_scales", [P, 2 * PAIR], U8)
         warm_codes = named("warm_codes", [P, P], U32)
         warm_scales = named("warm_scales", [P, P], U8)
         recip_banks = {GN - 1: psum.tile([P, BANK], F32, name="recip_bank")}
@@ -298,30 +299,49 @@ def tile_cubic_ocean_mode_step_h1_kernel(
                 for u in range(2):
                     nc.tensor.transpose(y_banks[c, g][:, rows(2 * h + u)], words[:, u, rows(at)], ident[:])
 
-        def group_y(c, g, copy=nc.scalar.copy):
-            y_grouped[c, g] = named("y_grouped%d%d" % (c % 2, g), [P, 2 * BANK], BF16)
-            copy(
-                out=y_grouped[c, g][:].bitcast(F32).rearrange("p (h m u) -> p h m u", u=2, m=P),
+        def group_y(c, g):
+            if (c, g // 2) not in y_grouped:
+                y_grouped[c, g // 2] = named("y_grouped%d%d" % (c % 2, g // 2), [P, 2, 2 * BANK], BF16)
+            nc.scalar.copy(
+                out=y_grouped[c, g // 2][:, g % 2, :].bitcast(F32).rearrange("p (h m u) -> p h m u", u=2, m=P),
                 in_=y_banks[c, g][:].rearrange("p (h u m) -> p h m u", u=2, m=P),
             )
 
         out_words = out_1.rearrange("g p m t -> p g (m t)").bitcast(I32)
 
-        def store_scales(queues, members):
+        def store_scales(c):
             for q in range(4):
-                queues[q % len(queues)].dma_start(
-                    out=out_2[:, 4 * q : 4 * q + 4, members].rearrange("g r m -> r g m").bitcast(I32),
-                    in_=y_scales[32 * q : 32 * q + 4, :, members].bitcast(I32),
+                nc.sync.dma_start(
+                    out=out_2[:, 4 * q : 4 * q + 4, c * PAIR : (c + 1) * PAIR].rearrange("g r m -> r g m").bitcast(I32),
+                    in_=y_scales[c][32 * q : 32 * q + 4, :, :].bitcast(I32),
                 )
 
-        def quantize_y(c, groups):
+        def store_packed_scales():
+            for q in range(4):
+                nc.scalar.dma_start(
+                    out=out_2[:, 4 * q : 4 * q + 4, 2 * PAIR :].bitcast(I32),
+                    in_=packed_scales[32 * q : 32 * q + 16, :].bitcast(I32),
+                )
+
+        def codes_of(c):
             if c not in y_codes:
                 y_codes[c] = named(("y_codes0", "c_raw_words0", "c_raw_words1", "y_codes0")[c], [P, GN, PAIR], U32)
+            return y_codes[c]
+
+        def quantize_y_wide(c, half):
+            groups = slice(2 * half, 2 * half + 2)
+            nc.vector.quantize_mx(
+                out=codes_of(c)[:, groups, :].rearrange("p g m -> p (g m)").bitcast(FP8X4),
+                scales=y_scales[c][:, groups, :].rearrange("p g m -> p (g m)"),
+                in_=y_grouped[c, half][:].rearrange("p g x -> p (g x)"),
+            )
+
+        def quantize_y(c, groups):
             for g in groups:
                 nc.vector.quantize_mx(
-                    out=y_codes[c][:, g, :].bitcast(FP8X4),
-                    scales=y_scales[:, g, c * PAIR : (c + 1) * PAIR],
-                    in_=y_grouped[c, g][:],
+                    out=codes_of(c)[:, g, :].bitcast(FP8X4),
+                    scales=packed_scales[4 * g :, c % 2 * PAIR : (c % 2 + 1) * PAIR],
+                    in_=y_grouped[c, g // 2][:, g % 2, :],
                 )
 
         def store_codes(c, groups):
@@ -438,7 +458,7 @@ def tile_cubic_ocean_mode_step_h1_kernel(
         for c in range(PAIRS - 1):
             i, n = 2 * c, 2 * c + 2
             if c > 0:
-                damp_pool(i - 1, BANK, ends[i - 1], ("h_grouped1", "y_grouped02")[c - 1])
+                damp_pool(i - 1, BANK, ends[i - 1], "h_grouped%d" % (c % 2))
                 store_y(i - 1, BANK, ends[i - 1])
                 round_y(i - 2, 0, N)
                 round_y(i - 1, 0, BANK)
@@ -506,13 +526,13 @@ def tile_cubic_ocean_mode_step_h1_kernel(
                 quantize_h(c + 1, PAIR, 2 * PAIR)
                 quantize_amp(3, 2, 1)
             else:
-                quantize_y(c - 1, (0,))
+                quantize_y_wide(c - 1, 0)
                 quantize_h(c + 1, PAIR, 2 * PAIR)
-                quantize_y(c - 1, (1, 2, 3))
+                quantize_y_wide(c - 1, 1)
                 store_codes(c - 1, slice(0, GN))
-        store_scales([nc.sync], slice(0, 2 * PAIR))
+                store_scales(c - 1)
 
-        damp_pool(5, BANK, ends[5], "y_grouped12")
+        damp_pool(5, BANK, ends[5], "h_grouped1")
         damp_vector(5, ends[5], N)
         store_y(5, ends[5], N)
         store_y(5, BANK, ends[5])
@@ -550,29 +570,28 @@ def tile_cubic_ocean_mode_step_h1_kernel(
             transpose_y(2, g)
         round_last(2)
         round_last(0)
-        for g in (1, 2):
-            group_y(2, g)
         for i in (6, 7):
             damp_vector(i, 3 * BANK, N)
         store_y(6, 3 * BANK, N)
         store_last(1)
         store_y(7, 3 * BANK, N)
-        for g in (2, 0):
-            transpose_y(last, g)
-            group_y(last, g)
+        for early, late in ((2, 1), (0, 2)):
+            transpose_y(last, early)
+            group_y(last, early)
+            group_y(2, late)
         round_last(1, vcopy)
         round_last(3, vcopy)
-        quantize_y(2, (0, 3))
-        store_codes(2, slice(0, GN, 3))
-        quantize_y(2, (1, 2))
-        store_codes(2, slice(1, 3))
         for g in (1, 3):
             transpose_y(last, g)
             group_y(last, g)
-        quantize_y(last, (2, 0))
+        for g, h in ((0, 2), (3, 0)):
+            quantize_y(2, (g,))
+            quantize_y(last, (h,))
+        store_codes(2, slice(0, GN, 3))
         store_codes(last, slice(0, GN, 2))
-        quantize_y(last, (1,))
-        store_codes(last, slice(1, 2))
-        quantize_y(last, (3,))
-        store_scales([nc.scalar], slice(2 * PAIR, M))
-        store_codes(last, slice(3, GN))
+        quantize_y(2, (1, 2))
+        store_codes(2, slice(1, 3))
+        for g in (1, 3):
+            quantize_y(last, (g,))
+            store_codes(last, slice(g, g + 1))
+        store_packed_scales()

@@ -96,8 +96,14 @@ def tile_cubic_ocean_mode_step_h1_kernel(
             )
 
         def load_amp(i):
-            amp_sb[i] = named("amp%d" % (i % 5), [P, K], BF16)
+            amp_sb[i] = named("amp%d" % (i % 4), [P, K], BF16)
             nc.sync.dma_start(out=amp_sb[i][:], in_=amp[rows(i), :])
+
+        def load_amp_pair(c):
+            tiles = named("amp_pair%d" % c, [P, 2, K], BF16)
+            nc.sync.dma_start(out=tiles[:], in_=amp[c * PAIR : (c + 1) * PAIR, :].rearrange("(h m) k -> m h k", h=2))
+            for h in range(2):
+                amp_sb[2 * c + h] = tiles[:, h, :]
 
         def load_slow(first, count):
             tiles = named("slow%d" % first, [P, count, N], BF16)
@@ -377,17 +383,16 @@ def tile_cubic_ocean_mode_step_h1_kernel(
         load_scales(c_raw_scales[0], coup_scales[:, :, cols(0)])
         load_words(c_raw_words, coup_words, 0)
         load_amp(2)
-        load_amp(3)
         load_scales(c_raw_scales[1], coup_scales[:, :, cols(1)])
+        load_amp(3)
         nc.sync.dma_start(out=cubic_sb[:], in_=cubic.rearrange("(g p t) -> p g t", p=P, t=4))
         load_words(c_raw_words, coup_words, 1)
         nc.vector.tensor_scalar(out=denom_rows[:], in0=drag_rows[:], scalar1=1.0, scalar2=None, op0=ALU.add)
         nc.vector.quantize_mx(out=warm_codes[:].bitcast(FP8X4), scales=warm_scales[:], in_=amp_sb[0][:, :BANK])
         nc.vector.reciprocal(out=recip_blocks[:], in_=denom_rows[:])
         parked = out_0[M - 1, :]
+        load_amp_pair(2)
         nc.sync.dma_start(out=parked.rearrange("(j p) -> j p", p=P), in_=recip_blocks[: N // P, :])
-        for i in (4, 5):
-            load_amp(i)
         load_scales(b_scales, forc_scales)
         load_words(b_words, forc_words, 0)
         load_slow(0, 1)

from contextlib import ExitStack

import concourse.mybir as mybir
from concourse.masks import make_identity

M, K, F, N = 1024, 1536, 1024, 2048
FLOPS = 2 * M * K * F + 2 * M * F * N

F32 = mybir.dt.float32
BF16 = mybir.dt.bfloat16
U32 = mybir.dt.uint32
I32 = mybir.dt.int32
U16 = mybir.dt.uint16
U8 = mybir.dt.uint8
FP8X4 = mybir.dt.float8_e4m3fn_x4
FP4X4 = mybir.dt.float4_e2m1fn_x4
ALU = mybir.AluOpType
ACT = mybir.ActivationFunctionType

P = 128
BANK = 512
TILES = M // P
PAIR = 2 * P
PAIRS = TILES // 2
GK = K // BANK
GF = F // BANK
GN = N // BANK
RING = 7
POOL_END = 1536
SHARE = (192, 256, 256)


def tile_cubic_ocean_mode_step_h1_kernel(
    tc, amp, coup_words, coup_scales, cubic, forc_words, forc_scales, slow, drag, out_0, out_1, out_2
):
    nc = tc.nc
    with ExitStack() as ctx:
        keep = ctx.enter_context(tc.tile_pool(name="keep", bufs=1))
        work = ctx.enter_context(tc.tile_pool(name="work", bufs=2))
        deep = ctx.enter_context(tc.tile_pool(name="deep", bufs=3))
        psum = ctx.enter_context(tc.psum_pool(name="psum", bufs=1))
        ctx.enter_context(tc.manual_schedule())

        ring = list(range(RING))

        def ring_bank(hold=False):
            b = ring.pop(0)
            if not hold:
                ring.append(b)
            return psum.tile([P, BANK], F32, name="bank%d" % b)

        def rows(i):
            return slice(i * P, (i + 1) * P)

        def cols(g, count=1):
            return slice(g * BANK, (g + count) * BANK)

        def named(name, shape, dtype):
            return keep.tile(shape, dtype, align_bytes=64, name=name)

        c_raw_words = [named("c_raw_words%d" % f, [P, GK, 2 * BANK], U8) for f in range(GF)]
        c_raw_scales = [named("c_raw_scales%d" % f, [P, GK, BANK], U8) for f in range(GF)]
        c_words = {(f, b): named("c_words%d%d" % (f, b), [P, GK, BANK], U8) for f in range(GF) for b in range(2)}
        c_scales = [named("c_scales%d" % f, [P, GK, BANK], U8) for f in range(GF)]
        b_words = [named("b_words%d" % h, [P, GF, N], U8) for h in range(2)]
        b_scales = named("b_scales", [P, GF, N], U8)
        cubic_sb = named("cubic_sb", [P, GF, 4], BF16)
        drag_rows = named("drag_rows", [P, P], BF16)
        denom_rows = named("denom_rows", [P, P], F32)
        recip = named("recip", [P, GN, 4], F32)
        recip_blocks = named("recip_blocks", [P, P], F32)
        recip_rows = named("recip_rows", [P, POOL_END], F32)
        ident = named("ident", [P, P], F32)
        y_scales = [named("y_scales%d" % c, [P, GN, PAIR], U8) for c in range(2)]
        packed_scales = named("packed_scales", [P, 2 * PAIR], U8)
        warm_codes = named("warm_codes", [P, P], U32)
        warm_scales = named("warm_scales", [P, P], U8)
        recip_banks = {GN - 1: psum.tile([P, BANK], F32, name="recip_bank")}
        amp_sb, slow_sb, a_sorted = {}, {}, {}
        a_banks, a_grouped, a_codes, a_scales = {}, {}, {}, {}
        u_banks, squares, h_slots, h_grouped, h_codes, h_scales = {}, {}, {}, {}, {}, {}
        e_banks, sums, moved, y_pairs, y_banks, y_grouped, y_codes = {}, {}, {}, {}, {}, {}, {}

        def load_scales(plane, scales):
            for q in (0, 2, 1, 3):
                nc.sync.dma_start(
                    out=plane[32 * q : 32 * q + 4, :, :].bitcast(I32),
                    in_=scales[:, 4 * q : 4 * q + 4, :].rearrange("g r n -> r g n").bitcast(I32),
                )

        def load_words(words_sb, words, half):
            width = words.shape[2] // 2
            part = slice(half * width, (half + 1) * width)
            nc.sync.dma_start(
                out=words_sb[half][:].bitcast(I32), in_=words[:, :, part].rearrange("g p b -> p g b").bitcast(I32)
            )

        def load_amp(i):
            amp_sb[i] = named("amp%d" % (i % 4), [P, K], BF16)
            nc.sync.dma_start(out=amp_sb[i][:], in_=amp[rows(i), :])

        def load_amp_pair(c):
            tiles = named("amp_pair%d" % c, [P, 2, K], BF16)
            nc.sync.dma_start(out=tiles[:], in_=amp[c * PAIR : (c + 1) * PAIR, :].rearrange("(h m) k -> m h k", h=2))
            for h in range(2):
                amp_sb[2 * c + h] = tiles[:, h, :]

        def load_slow(first, count):
            tiles = named("slow%d" % first, [P, count, N], BF16)
            nc.sync.dma_start(
                out=tiles[:], in_=slow[first * P : (first + count) * P, :].rearrange("(i m) n -> m i n", m=P)
            )
            for i in range(count):
                slow_sb[first + i] = tiles[:, i, :]

        def deal_words(f, b, copy):
            copy(
                out=c_words[f, b][:].bitcast(U16).rearrange("p g (t c i) -> p c g t i", t=2, i=8),
                in_=c_raw_words[f][:].bitcast(U16).rearrange("p g (c i t) -> p c g t i", t=4, i=8)[
                    :, :, :, 2 * b : 2 * b + 2, :
                ],
            )

        def deal_scales(f):
            nc.vector.tensor_copy(
                out=c_scales[f][:].rearrange("p g (t c i) -> p c g t i", t=4, i=16),
                in_=c_raw_scales[f][:].rearrange("p g (c i t) -> p c g t i", t=4, i=16),
            )

        def spread_recip(g, bank):
            for t in range(4):
                nc.tensor.transpose(bank[:, rows(t)], recip[:, g, t : t + 1].to_broadcast([P, P]), ident[:])

        def sort_amp(i, copy):
            a_sorted[i] = named("a_sorted%d" % (i % 2), [P, GK, 2, P], F32)
            copy(
                out=a_sorted[i][:].rearrange("m g u p -> m g p u"),
                in_=amp_sb[i][:].bitcast(F32).rearrange("m (g p u) -> m g p u", p=P, u=2),
            )

        def transpose_amp(c, groups, tiles=range(2)):
            for g, h in [(g, h) for g in groups for h in tiles]:
                if (c, g) not in a_banks:
                    a_banks[c, g] = ring_bank()
                i = 2 * c + h
                words = amp_sb[i][:].bitcast(F32)
                for u in range(2):
                    source = a_sorted[i][:, g, u, :] if i in a_sorted else words[:, PAIR * g + u : PAIR * (g + 1) : 2]
                    nc.tensor.transpose(a_banks[c, g][:, rows(2 * h + u)], source, ident[:])

        def group_amp(c, g):
            if c not in a_grouped:
                a_grouped[c] = named("a_grouped%d" % (c % 2), [P, GK, 2 * BANK], BF16)
            nc.scalar.copy(
                out=a_grouped[c][:, g, :].bitcast(F32).rearrange("p (h m u) -> p h m u", u=2, m=P),
                in_=a_banks[c, g][:].rearrange("p (h u m) -> p h m u", u=2, m=P),
            )

        def quantize_amp(c, first, count):
            if c not in a_codes:
                a_codes[c] = work.tile([P, GK * PAIR], U32, align_bytes=64, name="a_codes")
                a_scales[c] = work.tile([P, GK * PAIR], U8, align_bytes=64, name="a_scales")
            part = slice(first * PAIR, (first + count) * PAIR)
            nc.vector.quantize_mx(
                out=a_codes[c][:, part].bitcast(FP8X4),
                scales=a_scales[c][:, part],
                in_=a_grouped[c][:, first : first + count, :].rearrange("p g x -> p (g x)"),
            )

        def couple(n, b):
            c, f = divmod(n, 2)
            u_banks[n, b] = ring_bank()
            for s in range(2):
                for g in range(GK):
                    members = slice(g * PAIR, (g + 1) * PAIR)
                    nc.tensor.matmul_mx(
                        out=u_banks[n, b][:, s * PAIR : (s + 1) * PAIR],
                        lhsT=c_words[f, b][:, g, s * PAIR : (s + 1) * PAIR].bitcast(FP4X4),
                        lhsT_scale=c_scales[f][:, g, rows(2 * b + s)],
                        rhs=a_codes[c][:, members].bitcast(FP8X4),
                        rhs_scale=a_scales[c][:, members],
                        start=(g == 0),
                        stop=(g == GK - 1),
                    )

        def square(n, b):
            squares[n, b] = deep.tile([P, BANK], F32, align_bytes=64, name="squares")
            nc.scalar.activation(out=squares[n, b][:], in_=u_banks[n, b][:], func=ACT.Square)

        def cube(n, b):
            if b == 0:
                h_slots[n] = work.tile([P, 4, PAIR], BF16, align_bytes=64, name="h_slots")
            for s in range(2):
                t = 2 * b + s
                part = slice(s * PAIR, (s + 1) * PAIR)
                nc.vector.scalar_tensor_tensor(
                    out=h_slots[n][:, t, :],
                    in0=u_banks[n, b][:, part],
                    scalar=cubic_sb[:, n % 2, t : t + 1],
                    in1=squares[n, b][:, part],
                    op0=ALU.mult,
                    op1=ALU.mult,
                )

        def group_h(n, copy, lo, hi):
            c, f = divmod(n, GF)
            if c not in h_grouped:
                h_grouped[c] = named("h_grouped%d" % (c % 2), [P, GF, PAIR, 4], BF16)
            copy(
                out=h_grouped[c][:, f, lo:hi, :].rearrange("p (c i) t -> p c t i", i=4),
                in_=h_slots[n][:, :, lo:hi].rearrange("p t (c i) -> p c t i", i=4),
            )

        def quantize_h(c, lo, hi):
            if c not in h_codes:
                h_codes[c] = work.tile([P, GF * PAIR], U32, align_bytes=64, name="h_codes")
                h_scales[c] = work.tile([P, GF * PAIR], U8, align_bytes=64, name="h_scales")
            nc.vector.quantize_mx(
                out=h_codes[c][:, lo:hi].bitcast(FP8X4),
                scales=h_scales[c][:, lo:hi],
                in_=h_grouped[c][:].rearrange("p f m t -> p (f m t)")[:, 4 * lo : 4 * hi],
            )

        def force(i, j, passes=range(GF)):
            if (i, j) not in e_banks:
                e_banks[i, j] = ring_bank()
            c, h = divmod(i, 2)
            for f in passes:
                nc.tensor.matmul_mx(
                    out=e_banks[i, j][:],
                    lhsT=h_codes[c][:, rows(2 * f + h)].bitcast(FP8X4),
                    lhsT_scale=h_scales[c][:, rows(2 * f + h)],
                    rhs=b_words[j // 2][:, f, 2 * BANK * (j % 2) : 2 * BANK * (j % 2 + 1)].bitcast(FP4X4),
                    rhs_scale=b_scales[:, f, cols(j)],
                    start=(f == 0),
                    stop=(f == GF - 1),
                )

        def sum_part(i, lo, hi):
            if i < 2 * last:
                if i not in sums:
                    sums[i] = named("sums%d" % (i % 4), [P, N], F32)
                return sums[i][:, lo:hi]
            g = lo // BANK
            if g not in last_sums:
                last_sums[g] = named("last_sums%d" % g, [P, 2, BANK], F32)
            return last_sums[g][:, i % 2, :]

        def add_slow(i, j):
            nc.vector.tensor_tensor(
                out=sum_part(i, j * BANK, (j + 1) * BANK), in0=e_banks[i, j][:], in1=slow_sb[i][:, cols(j)], op=ALU.add
            )

        def y_part(i, lo, hi):
            if (i, lo) in moved:
                return moved[i, lo][:]
            return sum_part(i, lo, hi)

        def damp_pool(i, lo, hi, into=None):
            if into is not None:
                moved[i, lo] = named(into, [P, hi - lo], F32)
            nc.gpsimd.tensor_tensor(out=y_part(i, lo, hi), in0=sum_part(i, lo, hi), in1=recip_rows[:, lo:hi], op=ALU.mult)

        def damp_pool_last(g):
            part = last_sums[g][:]
            factors = recip_rows[:, cols(g)].unsqueeze(1).to_broadcast([P, 2, BANK])
            nc.gpsimd.tensor_tensor(out=part, in0=part, in1=factors, op=ALU.mult)

        def damp_vector(i, lo, hi):
            part = y_part(i, lo, hi)
            g = lo // BANK
            nc.vector.tensor_tensor(out=part, in0=part, in1=recip_banks[g][:, lo - g * BANK :], op=ALU.mult)

        def store_y(i, lo, hi):
            nc.sync.dma_start(out=out_0[rows(i), lo:hi], in_=y_part(i, lo, hi))

        def round_copy(out, in_):
            nc.scalar.activation(out=out, in_=in_, func=ACT.Copy)

        def round_y(i, lo, hi):
            if i not in y_pairs:
                y_pairs[i] = named("y_pairs%d" % (i % 4), [P, 2, N // 4, 2], BF16)
            round_copy(
                out=y_pairs[i][:, :, lo // 4 : hi // 4, :].rearrange("m u w e -> m w u e"),
                in_=y_part(i, lo, hi).rearrange("m (w u e) -> m w u e", u=2, e=2),
            )

        def round_last(g, copy=round_copy):
            last_pairs[g] = named("last_pairs%d" % g, [P, 2, PAIR, 2], BF16)
            copy(
                out=last_pairs[g][:].rearrange("m u w e -> m w u e"),
                in_=last_sums[g][:].rearrange("m h (w u e) -> m (h w) u e", u=2, e=2),
            )

        def store_last(g):
            nc.sync.dma_start(
                out=out_0[last * PAIR :, cols(g)].rearrange("(h m) n -> m h n", h=2), in_=last_sums[g][:]
            )

        def transpose_y(c, g):
            y_banks[c, g] = ring_bank()
            for h in range(2):
                pairs, at = (last_pairs[g], h) if c == last else (y_pairs[2 * c + h], g)
                words = pairs[:].rearrange("m u w e -> m u (w e)").bitcast(F32)
                for u in range(2):
                    nc.tensor.transpose(y_banks[c, g][:, rows(2 * h + u)], words[:, u, rows(at)], ident[:])

        def group_y(c, g):
            if (c, g // 2) not in y_grouped:
                y_grouped[c, g // 2] = named("y_grouped%d%d" % (c % 2, g // 2), [P, 2, 2 * BANK], BF16)
            nc.scalar.copy(
                out=y_grouped[c, g // 2][:, g % 2, :].bitcast(F32).rearrange("p (h m u) -> p h m u", u=2, m=P),
                in_=y_banks[c, g][:].rearrange("p (h u m) -> p h m u", u=2, m=P),
            )

        out_words = out_1.rearrange("g p m t -> p g (m t)").bitcast(I32)

        def store_scales(c):
            for q in range(4):
                nc.sync.dma_start(
                    out=out_2[:, 4 * q : 4 * q + 4, c * PAIR : (c + 1) * PAIR].rearrange("g r m -> r g m").bitcast(I32),
                    in_=y_scales[c][32 * q : 32 * q + 4, :, :].bitcast(I32),
                )

        def store_packed_scales():
            for q in range(4):
                nc.scalar.dma_start(
                    out=out_2[:, 4 * q : 4 * q + 4, 2 * PAIR :].bitcast(I32),
                    in_=packed_scales[32 * q : 32 * q + 16, :].bitcast(I32),
                )

        def codes_of(c):
            if c not in y_codes:
                y_codes[c] = named(("y_codes0", "c_raw_words0", "c_raw_words1", "y_codes0")[c], [P, GN, PAIR], U32)
            return y_codes[c]

        def quantize_y_wide(c, half):
            groups = slice(2 * half, 2 * half + 2)
            nc.vector.quantize_mx(
                out=codes_of(c)[:, groups, :].rearrange("p g m -> p (g m)").bitcast(FP8X4),
                scales=y_scales[c][:, groups, :].rearrange("p g m -> p (g m)"),
                in_=y_grouped[c, half][:].rearrange("p g x -> p (g x)"),
            )

        def quantize_y(c, groups):
            for g in groups:
                nc.vector.quantize_mx(
                    out=codes_of(c)[:, g, :].bitcast(FP8X4),
                    scales=packed_scales[4 * g :, c % 2 * PAIR : (c % 2 + 1) * PAIR],
                    in_=y_grouped[c, g // 2][:, g % 2, :],
                )

        def store_codes(c, groups):
            nc.sync.dma_start(
                out=out_words[:, groups, c * PAIR : (c + 1) * PAIR], in_=y_codes[c][:, groups, :].bitcast(I32)
            )

        def warm_up(count):
            bank = ring_bank()
            for g in range(count):
                nc.tensor.matmul_mx(
                    out=bank[:],
                    lhsT=warm_codes[:].bitcast(FP8X4),
                    lhsT_scale=warm_scales[:],
                    rhs=c_raw_words[0][:, g, :].bitcast(FP4X4),
                    rhs_scale=c_raw_scales[0][:, g, :],
                    start=True,
                    stop=True,
                )

        last, last_sums, last_pairs = PAIRS - 1, {}, {}
        vcopy, scopy = nc.vector.tensor_copy, nc.scalar.copy

        nc.vector.memset(drag_rows[:].bitcast(I32), 0)
        for f in range(GF):
            nc.vector.memset(c_raw_scales[f][:].bitcast(I32), 0)
        nc.vector.memset(b_scales[:].bitcast(I32), 0)
        make_identity(nc, ident[:])

        load_amp(0)
        nc.sync.dma_start(out=drag_rows[: N // P, :], in_=drag.rearrange("(j p) -> j p", p=P))
        load_amp(1)
        load_scales(c_raw_scales[0], coup_scales[:, :, cols(0)])
        load_words(c_raw_words, coup_words, 0)
        load_amp(2)
        load_scales(c_raw_scales[1], coup_scales[:, :, cols(1)])
        load_amp(3)
        nc.sync.dma_start(out=cubic_sb[:], in_=cubic.rearrange("(g p t) -> p g t", p=P, t=4))
        load_words(c_raw_words, coup_words, 1)
        nc.vector.tensor_scalar(out=denom_rows[:], in0=drag_rows[:], scalar1=1.0, scalar2=None, op0=ALU.add)
        nc.vector.quantize_mx(out=warm_codes[:].bitcast(FP8X4), scales=warm_scales[:], in_=amp_sb[0][:, :BANK])
        nc.vector.reciprocal(out=recip_blocks[:], in_=denom_rows[:])
        parked = out_0[M - 1, :]
        load_amp_pair(2)
        nc.sync.dma_start(out=parked.rearrange("(j p) -> j p", p=P), in_=recip_blocks[: N // P, :])
        load_scales(b_scales, forc_scales)
        load_words(b_words, forc_words, 0)
        load_slow(0, 1)
        load_words(b_words, forc_words, 1)
        nc.sync.dma_start(out=recip_rows[:, :BANK], in_=parked[:BANK].partition_broadcast(P))
        load_slow(1, 1)
        load_amp(6)
        nc.sync.dma_start(out=recip_rows[:, BANK:], in_=parked[BANK:POOL_END].partition_broadcast(P))
        load_amp(7)
        load_slow(2, 2)

        transpose_amp(0, range(GK), (0,))
        transpose_amp(0, range(GK), (1,))
        recip_bank = ring_bank()
        nc.tensor.transpose(recip_bank[:, :P], recip_blocks[:], ident[:])
        group_amp(0, 0)
        group_amp(0, 1)
        nc.scalar.copy(out=recip[:].rearrange("p g t -> p (g t)"), in_=recip_bank[:, : N // P])
        group_amp(0, 2)
        warm_up(2)
        spread_recip(GN - 1, recip_banks[GN - 1])
        deal_scales(0)
        deal_words(0, 0, vcopy)
        for g in range(GK):
            quantize_amp(0, g, 1)
        deal_words(0, 1, vcopy)
        sort_amp(2, scopy)
        sort_amp(3, scopy)
        deal_scales(1)
        deal_words(1, 0, vcopy)
        for b in range(2):
            couple(0, b)
            square(0, b)
        transpose_amp(1, range(GK))
        for g in range(GK):
            group_amp(1, g)
        cube(0, 0)
        deal_words(1, 1, vcopy)
        cube(0, 1)
        quantize_amp(1, 0, 1)
        group_h(0, vcopy, 0, PAIR)
        couple(1, 0)
        square(1, 0)
        couple(1, 1)
        square(1, 1)
        quantize_amp(1, 1, 2)
        cube(1, 0)
        quantize_h(0, 0, PAIR)
        cube(1, 1)
        transpose_amp(2, (0, 1))
        group_amp(2, 0)
        group_amp(2, 1)
        couple(2, 0)
        square(2, 0)
        transpose_amp(2, (2,))
        group_amp(2, 2)
        couple(2, 1)
        square(2, 1)
        quantize_amp(2, 0, 1)
        group_h(1, vcopy, 0, PAIR)
        quantize_amp(2, 1, 1)
        quantize_h(0, PAIR, 2 * PAIR)
        quantize_amp(2, 2, 1)
        cube(2, 0)
        cube(2, 1)
        ends = (1536,)*6

        for c in range(PAIRS - 1):
            i, n = 2 * c, 2 * c + 2
            if c > 0:
                damp_pool(i - 1, BANK, ends[i - 1], "h_grouped%d" % (c % 2))
                store_y(i - 1, BANK, ends[i - 1])
                round_y(i - 2, 0, N)
                round_y(i - 1, 0, BANK)
                round_y(i - 1, ends[i - 1], N)
                cube(n, 0)
            for f in range(GF):
                for j in range(3):
                    force(i, j, (f,))
            for j in (0, 2, 1):
                add_slow(i, j)
            if c == 0:
                damp_pool(i, 0, BANK)
            else:
                damp_pool(i, 0, ends[i])
            if c > 0:
                cube(n, 1)
            force(i, 3)
            add_slow(i, 3)
            if c > 0:
                round_y(i - 1, BANK, ends[i - 1])
            group_h(n, scopy, 0, PAIR)
            for j in (0, 3, 1, 2):
                force(i + 1, j)
                add_slow(i + 1, j)
                if j == 0:
                    damp_vector(i, ends[i], N)
            if c == 0:
                damp_pool(i + 1, 0, BANK)
                damp_pool(i, BANK, ends[i])
                store_y(i + 1, 0, BANK)
                store_y(i, 0, N)
                load_slow(4, 4)
            else:
                store_y(i, 0, N)
                damp_pool(i + 1, 0, BANK)
                store_y(i + 1, 0, BANK)
            if c < PAIRS - 2:
                damp_vector(i + 1, ends[i + 1], N)
                store_y(i + 1, ends[i + 1], N)
            for b in range(2):
                couple(n + 1, b)
                square(n + 1, b)
                cube(n + 1, b)
            if c == 0:
                transpose_amp(3, range(GK), (0,))
            for g in range(GK if c == 0 else GN):
                if c == 0:
                    transpose_amp(3, (g,), (1,))
                    group_amp(3, g)
                else:
                    transpose_y(c - 1, g)
                    group_y(c - 1, g)
                if g == 2 and SHARE[c] < PAIR:
                    group_h(n + 1, scopy, SHARE[c], PAIR)
            if c == PAIRS - 2:
                round_y(i, 0, N)
            if c < PAIRS - 2:
                for b in range(2):
                    couple(n + 2, b)
                    square(n + 2, b)
            quantize_h(c + 1, 0, PAIR)
            group_h(n + 1, vcopy, 0, SHARE[c])
            if c == 0:
                quantize_amp(3, 0, 2)
                quantize_h(c + 1, PAIR, 2 * PAIR)
                quantize_amp(3, 2, 1)
            else:
                quantize_y_wide(c - 1, 0)
                quantize_h(c + 1, PAIR, 2 * PAIR)
                quantize_y_wide(c - 1, 1)
                store_codes(c - 1, slice(0, GN))
                store_scales(c - 1)

        damp_pool(5, BANK, ends[5], "h_grouped1")
        damp_vector(5, ends[5], N)
        store_y(5, ends[5], N)
        store_y(5, BANK, ends[5])
        round_y(5, 0, BANK)
        round_y(5, ends[5], N)
        recip_banks[2] = ring_bank(hold=True)
        spread_recip(2, recip_banks[2])
        first = ((6, 0), (7, 0), (6, 2))
        for f in range(GF):
            for i, j in first:
                force(i, j, (f,))
        force(7, 2)
        for j in (0, 2):
            for i in (6, 7):
                add_slow(i, j)
        damp_pool_last(0)
        force(6, 1)
        add_slow(6, 1)
        for g in (0, 3):
            transpose_y(2, g)
            group_y(2, g)
        damp_vector(6, 2 * BANK, 3 * BANK)
        store_y(6, 2 * BANK, 3 * BANK)
        force(7, 1)
        add_slow(7, 1)
        damp_pool_last(1)
        damp_vector(7, 2 * BANK, 3 * BANK)
        store_last(0)
        store_y(7, 2 * BANK, 3 * BANK)
        round_y(5, BANK, ends[5])
        for i in (6, 7):
            force(i, 3)
            add_slow(i, 3)
        for g in (1, 2):
            transpose_y(2, g)
        round_last(2)
        round_last(0)
        for i in (6, 7):
            damp_vector(i, 3 * BANK, N)
        store_y(6, 3 * BANK, N)
        store_last(1)
        store_y(7, 3 * BANK, N)
        for early, late in ((2, 1), (0, 2)):
            transpose_y(last, early)
            group_y(last, early)
            group_y(2, late)
        round_last(1, vcopy)
        round_last(3, vcopy)
        for g in (1, 3):
            transpose_y(last, g)
            group_y(last, g)
        for g, h in ((0, 2), (3, 0)):
            quantize_y(2, (g,))
            quantize_y(last, (h,))
        store_codes(2, slice(0, GN, 3))
        store_codes(last, slice(0, GN, 2))
        quantize_y(2, (1, 2))
        store_codes(2, slice(1, 3))
        for g in (1, 3):
            quantize_y(last, (g,))
            store_codes(last, slice(g, g + 1))
        store_packed_scales()
